import numpy as np
import ml_dtypes


def mxq(x, axis, fmt="e4m3"):
    dtype, down = {"e4m3": (ml_dtypes.float8_e4m3fn, 7), "e5m2": (ml_dtypes.float8_e5m2, 14)}[fmt]
    v = np.moveaxis(np.asarray(x, np.float32).astype(ml_dtypes.bfloat16).astype(np.float64), axis, -1)
    blocks = v.reshape(v.shape[:-1] + (-1, 32))
    amax = np.abs(blocks).max(-1, keepdims=True)
    byte = np.maximum(np.where(amax > 0, np.frexp(amax)[1] - 1 + 127, 0) - down, 1)
    scale = np.exp2(byte - 127.0)
    codes = (blocks / scale).astype(np.float32).astype(dtype).astype(np.float64)
    return np.moveaxis((codes * scale).reshape(v.shape), -1, axis)


WIDE = False


def mx_kscale(k):
    if not WIDE:
        return np.ones(k)
    levels = np.array([30, -30])
    if k % 512:
        return np.exp2(np.random.permutation(np.resize(levels, k // 32))).repeat(32)
    a = np.empty((k // 512, 16))
    for p in range(k // 512):
        a[p, :8] = np.random.permutation(np.resize(levels, 8))
        for g in range(8):
            far = levels[np.abs(levels - a[p, g]) >= 10]
            a[p, g + 8] = far[np.random.randint(len(far))]
    return np.exp2(a.ravel()).repeat(32)


def f64(x):
    return np.asarray(x).astype(np.float64)


def striped(idx):
    return np.tile(idx.reshape(-1, 16).T, (8, 1)).astype(np.uint16)


def unstriped(offs):
    return offs[:16].T.reshape(-1).astype(np.int64)


E2M1 = np.array([0.0, 0.5, 1.0, 1.5, 2.0, 3.0, 4.0, 6.0, -0.0, -0.5, -1.0, -1.5, -2.0, -3.0, -4.0, -6.0])


def pack_weight(w, fmt):
    k, n = w.shape
    w = f64(np.asarray(w, np.float32).astype(ml_dtypes.bfloat16)).reshape(k // 32, 32, n)
    amax = np.abs(w).max(1)
    if fmt == "e4m3":
        byte = np.frexp(amax)[1] - 1 + 127 - 7
    else:
        mant, ex = np.frexp(amax / 6.0)
        byte = np.where(mant > 0.5, ex, ex - 1) + 127
    byte = np.clip(np.where(amax > 0, byte, 1), 1, 254)
    scaled = (w * np.exp2(127.0 - byte)[:, None, :]).reshape(k, n).astype(np.float32)
    by_word = np.ascontiguousarray(scaled.reshape(k // 512, 128, 4, n).transpose(0, 1, 3, 2))
    if fmt == "e4m3":
        words = by_word.astype(ml_dtypes.float8_e4m3fn).view(np.uint8)
    else:
        c = by_word.astype(ml_dtypes.float4_e2m1fn).view(np.uint8) & 0xF
        words = (c[..., 0::2] | (c[..., 1::2] << 4)).reshape(k // 512, 128, 2 * n)
    return np.ascontiguousarray(words), np.ascontiguousarray(byte.astype(np.uint8).reshape(k // 512, 16, n))


def unpack_weight(words, scales, fmt):
    g, _, n = scales.shape
    words = np.ascontiguousarray(words).reshape(g, 128, n, -1)
    if fmt == "e4m3":
        vals = words.view(ml_dtypes.float8_e4m3fn).astype(np.float64)
    else:
        nib = np.empty((g, 128, n, 4), np.uint8)
        nib[..., 0::2] = words & 0xF
        nib[..., 1::2] = words >> 4
        vals = E2M1[nib]
    vals = vals * np.repeat(np.exp2(scales.astype(np.float64) - 127.0), 8, axis=1)[..., None]
    return vals.transpose(0, 1, 3, 2).reshape(g * 512, n)


K, T, E, C, N = 128, 1024, 6, 512, 1536
TOP = 3


def by_expert(wq, xq):
    return np.concatenate([wq[e].T @ xq[:, e * C:(e + 1) * C] for e in range(E)], axis=1)


def setup_inputs():
    n = np.random.standard_normal
    s = mx_kscale(N)[:, None]
    deal = np.repeat(np.arange(E), C).reshape(TOP, T)[:, np.random.permutation(T)]
    deal = np.take_along_axis(deal, np.argsort(np.random.rand(TOP, T), axis=0), axis=0)
    for _ in range(8):
        s_, t_ = np.random.permutation(T).reshape(2, -1); r = np.random.randint(TOP, size=T // 2); x, y = deal[r, s_].copy(), deal[r, t_].copy()
        ok = ~((deal[:, s_] == y).any(0) | (deal[:, t_] == x).any(0)); deal[r[ok], s_[ok]] = y[ok]; deal[r[ok], t_[ok]] = x[ok]
    order = np.lexsort((np.random.rand(TOP * T), deal.reshape(-1)))
    slot_token = order % T; pos = np.empty(TOP * T, np.int64); pos[order] = np.arange(TOP * T); pos = pos.reshape(TOP, T)
    g = np.random.uniform(0.5, 1.5, (TOP, T)); g = g / g.sum(0)
    w_slot = np.empty(E * C)
    for r in range(TOP): w_slot[pos[r]] = g[r]
    w = [pack_weight(m, "e2m1") for m in n((E + 1, N, K)) / np.sqrt(N) / s[None]]
    return {
        "dyT": (n((N, T)) * s).astype(np.float32),
        "w_words": np.stack([m[0] for m in w]),
        "w_scales": np.stack([m[1] for m in w]),
        "gate": np.tile(w_slot, (N, 1)).astype(np.float32),
        "offs": striped(slot_token),
        "pos1": striped(pos[0]),
        "pos2": striped(pos[1]),
        "pos3": striped(pos[2]),
    }


def reference(dyT, w_words, w_scales, gate, offs, pos1, pos2, pos3):
    idx = unstriped(offs)
    w = np.stack([unpack_weight(w_words[e], w_scales[e], "e2m1") for e in range(E + 1)])
    gq = mxq(f64(gate) * f64(dyT)[:, idx], 0, "e5m2")
    wq = w
    ds = wq[E].T @ mxq(f64(dyT), 0, "e5m2")
    dx = by_expert(wq, gq)
    return ds + dx[:, unstriped(pos1)] + dx[:, unstriped(pos2)] + dx[:, unstriped(pos3)]

@@ -1,0 +1,165 @@
+from contextlib import ExitStack
+
+import concourse.mybir as mybir
+
+K, T, E, C, N = 128, 1024, 6, 512, 1536
+S = E * C
+FLOPS = 2 * K * N * (S + T)
+BYTES = 4 * N * T + (E + 1) * (N * K // 2 + N * K // 32) + 4 * S + 2 * 128 * (S + 3 * T) // 16 + 4 * K * T
+
+F32 = mybir.dt.float32
+BF16 = mybir.dt.bfloat16
+I32 = mybir.dt.int32
+U32 = mybir.dt.uint32
+U16 = mybir.dt.uint16
+U8 = mybir.dt.uint8
+E5M2X4 = mybir.dt.float8_e5m2_x4
+E2M1X4 = mybir.dt.float4_e2m1fn_x4
+MULT = mybir.AluOpType.mult
+ADD = mybir.AluOpType.add
+
+P = 128
+PACK = 4
+PASSES = N // (P * PACK)
+BANK = 512
+PAD = 16
+FIRST = 256
+TOKEN_CUT = 640
+
+
+def tile_moe_bds_lin_none_kernel(tc, dyT, w_words, w_scales, gate, offs, pos1, pos2, pos3, out):
+    nc = tc.nc
+    with ExitStack() as ctx:
+        keep = ctx.enter_context(tc.tile_pool(name="keep", bufs=1))
+        ring = ctx.enter_context(tc.tile_pool(name="ring", bufs=2))
+        psum = ctx.enter_context(tc.psum_pool(name="psum", bufs=1))
+
+        offs_sb = keep.tile([P, S // 16], U16, name="offs_sb")
+        pos_sb = [keep.tile([P, T // 16], U16, name="pos_sb%d" % r) for r in range(3)]
+        gate_sb = keep.tile([P, S], F32, name="gate_sb")
+        window = {}
+        for a in range(PASSES):
+            for j in range(PACK):
+                window[a, j] = keep.tile([P, T + PAD], F32, name="window%d_%d" % (a, j))
+        words = keep.tile([P, (E + 1) * PASSES, 2 * K], U8, name="words", align_bytes=64)
+        wscale = keep.tile([P, (E + 1) * PASSES, K], U8, name="wscale", align_bytes=64)
+        dx = keep.tile([P, S], F32, name="dx")
+        ds = keep.tile([P, T], F32, name="ds")
+        banks = [psum.tile([P, BANK], F32, name="bank%d" % b) for b in range(E + T // BANK)]
+
+        rows = dyT.rearrange("(a p j) t -> a p j t", p=P, j=PACK)
+
+        def load_window(a, j):
+            nc.sync.dma_start(window[a, j][:, 0:T], rows[a, :, j, :])
+
+        def load_gate(c0, c1):
+            nc.sync.dma_start(gate_sb[:, c0:c1], gate[0:P, c0:c1])
+
+        nc.gpsimd.memset(wscale[:].rearrange("p m k -> p (m k)").bitcast(I32), 0)
+        nc.sync.dma_start(offs_sb[:], offs)
+        load_gate(0, FIRST)
+        load_window(0, 0)
+        load_gate(FIRST, 2 * FIRST)
+        load_gate(2 * FIRST, 2 * C)
+        for j in range(1, PACK):
+            load_window(0, j)
+        load_gate(2 * C, 4 * C)
+        nc.sync.dma_start(words[:].bitcast(I32), w_words.rearrange("e a p b -> p (e a) b").bitcast(I32))
+        scale_rows = w_scales.rearrange("e a f k -> f (e a) k")
+        for q in range(4):
+            nc.sync.dma_start(wscale[32 * q : 32 * q + 4, :, :].bitcast(I32), scale_rows[4 * q : 4 * q + 4, :, :].bitcast(I32))
+        load_gate(4 * C, S)
+        for a in range(1, PASSES):
+            for j in range(PACK):
+                load_window(a, j)
+        for tile, src in zip(pos_sb, (pos1, pos2, pos3)):
+            nc.sync.dma_start(tile[:], src)
+
+        def gather(a, s0, s1, cuts, tag):
+            g = ring.tile([P, PACK, s1 - s0], F32, name="g", tag=tag, bufs=1, align_bytes=64)
+            for j in range(PACK):
+                edges = [s0] + (cuts if j == 0 else []) + [s1]
+                for c0, c1 in zip(edges[:-1], edges[1:]):
+                    nc.vector.tensor_tensor(
+                        g[:, j, c0 - s0 : c1 - s0],
+                        window[a, j][:].indirect(offs_sb[:, c0 // 16 : c1 // 16]),
+                        gate_sb[:, c0:c1],
+                        MULT,
+                    )
+            return g
+
+        def interleave(dst, src):
+            nc.scalar.copy(dst, src.rearrange("p j c -> p c j"))
+
+        def quantize(codes, scales, src):
+            nc.vector.quantize_mx(out=codes.bitcast(E5M2X4), scales=scales, in_=src[:].rearrange("p c j -> p (c j)"))
+
+        def multiply(a, e, bank, codes, scales, c0):
+            m = e * PASSES + a
+            nc.tensor.matmul_mx(
+                out=banks[bank][:],
+                lhsT=words[:, m, :].bitcast(E2M1X4),
+                lhsT_scale=wscale[:, m, :],
+                rhs=codes[:, c0 : c0 + BANK].bitcast(E5M2X4),
+                rhs_scale=scales[:, c0 : c0 + BANK],
+                start=(a == 0),
+                stop=(a == PASSES - 1),
+            )
+
+        def finish_routed(a, s0, s1, gb):
+            codes = ring.tile([P, s1 - s0], U32, name="codes", tag="codes", bufs=2, align_bytes=64)
+            scales = ring.tile([P, s1 - s0], U8, name="scales", tag="scales", bufs=2, align_bytes=64)
+            quantize(codes[:], scales[:], gb)
+            for e in range(s0 // C, s1 // C):
+                multiply(a, e, e, codes, scales, e * C - s0)
+                if a == PASSES - 1:
+                    nc.scalar.copy(dx[:, e * C : (e + 1) * C], banks[e][:])
+
+        shared_b = [keep.tile([P, T, PACK], BF16, name="shared_b%d" % a, align_bytes=64) for a in range(PASSES)]
+
+        def round_shared(piece):
+            a, h = divmod(piece, T // BANK)
+            raw = ring.tile([P, PACK, BANK], F32, name="raw", tag="raw", bufs=2)
+            nc.sync.dma_start(raw[:], rows[a, :, :, h * BANK : (h + 1) * BANK])
+            interleave(shared_b[a][:, h * BANK : (h + 1) * BANK, :], raw[:])
+
+        def finish_shared(a, all_codes, all_scales):
+            codes = all_codes[:, a, :]
+            scales = all_scales[:, a, :]
+            quantize(codes, scales, shared_b[a])
+            for h in range(T // BANK):
+                multiply(a, E, E + h, codes, scales, h * BANK)
+                if a == PASSES - 1:
+                    nc.scalar.copy(ds[:, h * BANK : (h + 1) * BANK], banks[E + h][:])
+
+        units = [(a, s0, s0 + 2 * C) for a in range(PASSES) for s0 in range(0, S, 2 * C)]
+        last = units.pop()
+        units.extend([(last[0], last[1], last[1] + C), (last[0], last[1] + C, last[2])])
+
+        waiting = None
+        for u, (a, s0, s1) in enumerate(units):
+            g = gather(a, s0, s1, [FIRST, 2 * FIRST] if u == 0 else [], "g%d" % (u % 2))
+            gb = ring.tile([P, s1 - s0, PACK], BF16, name="gb", tag="gb", bufs=2, align_bytes=64)
+            interleave(gb[:], g[:])
+            if waiting is not None:
+                finish_routed(*waiting)
+            waiting = (a, s0, s1, gb)
+            if 2 <= u < 2 + PASSES * T // BANK:
+                round_shared(u - 2)
+        shared_codes = ring.tile([P, PASSES, T], U32, name="shared_codes", tag="g%d" % (len(units) % 2), bufs=1, align_bytes=64)
+        shared_scales = keep.tile([P, PASSES, T], U8, name="shared_scales", align_bytes=64)
+        finish_shared(0, shared_codes, shared_scales)
+        finish_shared(1, shared_codes, shared_scales)
+        finish_routed(*waiting)
+        finish_shared(2, shared_codes, shared_scales)
+
+        for t0, t1 in ((0, TOKEN_CUT), (TOKEN_CUT, T)):
+            back = ring.tile([P, 3, t1 - t0], F32, name="back", tag="back", bufs=2)
+            total = ring.tile([P, t1 - t0], F32, name="total", tag="total", bufs=2)
+            for r in range(3):
+                nc.vector.tensor_copy(back[:, r, :], dx[:].indirect(pos_sb[r][:, t0 // 16 : t1 // 16]))
+                if r == 1:
+                    nc.vector.tensor_tensor(total[:], back[:, 0, :], ds[:, t0:t1], ADD)
+            nc.vector.tensor_tensor(total[:], total[:], back[:, 1, :], ADD)
+            nc.vector.tensor_tensor(total[:], total[:], back[:, 2, :], ADD)
+            nc.sync.dma_start(out[:, t0:t1], total[:])

@@ -24,7 +24,7 @@ PASSES = N // (P * PACK)
 BANK = 512
 PAD = 16
 FIRST = 256
-TOKEN_CUT = 640
+TOKEN_CUT = 512
 
 
 def tile_moe_bds_lin_none_kernel(tc, dyT, w_words, w_scales, gate, offs, pos1, pos2, pos3, out):
@@ -64,14 +64,15 @@ def tile_moe_bds_lin_none_kernel(tc, dyT, w_words, w_scales, gate, offs, pos1, p
         for j in range(1, PACK):
             load_window(0, j)
         load_gate(2 * C, 4 * C)
+        load_gate(4 * C, S)
+        for j in range(PACK):
+            load_window(1, j)
         nc.sync.dma_start(words[:].bitcast(I32), w_words.rearrange("e a p b -> p (e a) b").bitcast(I32))
         scale_rows = w_scales.rearrange("e a f k -> f (e a) k")
         for q in range(4):
             nc.sync.dma_start(wscale[32 * q : 32 * q + 4, :, :].bitcast(I32), scale_rows[4 * q : 4 * q + 4, :, :].bitcast(I32))
-        load_gate(4 * C, S)
-        for a in range(1, PASSES):
-            for j in range(PACK):
-                load_window(a, j)
+        for j in range(PACK):
+            load_window(2, j)
         for tile, src in zip(pos_sb, (pos1, pos2, pos3)):
             nc.sync.dma_start(tile[:], src)
 
@@ -158,8 +159,6 @@ def tile_moe_bds_lin_none_kernel(tc, dyT, w_words, w_scales, gate, offs, pos1, p
             total = ring.tile([P, t1 - t0], F32, name="total", tag="total", bufs=2)
             for r in range(3):
                 nc.vector.tensor_copy(back[:, r, :], dx[:].indirect(pos_sb[r][:, t0 // 16 : t1 // 16]))
-                if r == 1:
-                    nc.vector.tensor_tensor(total[:], back[:, 0, :], ds[:, t0:t1], ADD)
-            nc.vector.tensor_tensor(total[:], total[:], back[:, 1, :], ADD)
-            nc.vector.tensor_tensor(total[:], total[:], back[:, 2, :], ADD)
+                adder = nc.vector if (r == 2 and t1 == T) else nc.gpsimd
+                adder.tensor_tensor(total[:], back[:, r, :], ds[:, t0:t1] if r == 0 else total[:], ADD)
             nc.sync.dma_start(out[:, t0:t1], total[:])

@@ -24,7 +24,6 @@ PASSES = N // (P * PACK)
 BANK = 512
 PAD = 16
 FIRST = 256
-TOKEN_CUT = 512
 
 
 def tile_moe_bds_lin_none_kernel(tc, dyT, w_words, w_scales, gate, offs, pos1, pos2, pos3, out):
@@ -124,9 +123,7 @@ def tile_moe_bds_lin_none_kernel(tc, dyT, w_words, w_scales, gate, offs, pos1, p
             nc.sync.dma_start(raw[:], rows[a, :, :, h * BANK : (h + 1) * BANK])
             interleave(shared_b[a][:, h * BANK : (h + 1) * BANK, :], raw[:])
 
-        def finish_shared(a, all_codes, all_scales):
-            codes = all_codes[:, a, :]
-            scales = all_scales[:, a, :]
+        def finish_shared(a, codes, scales):
             quantize(codes, scales, shared_b[a])
             for h in range(T // BANK):
                 multiply(a, E, E + h, codes, scales, h * BANK)
@@ -147,18 +144,24 @@ def tile_moe_bds_lin_none_kernel(tc, dyT, w_words, w_scales, gate, offs, pos1, p
             waiting = (a, s0, s1, gb)
             if 2 <= u < 2 + PASSES * T // BANK:
                 round_shared(u - 2)
-        shared_codes = ring.tile([P, PASSES, T], U32, name="shared_codes", tag="g%d" % (len(units) % 2), bufs=1, align_bytes=64)
+        early_codes = ring.tile([P, PASSES - 1, T], U32, name="early_codes", tag="g%d" % (len(units) % 2), bufs=1, align_bytes=64)
+        late_codes = ring.tile([P, T], U32, name="late_codes", tag="g%d" % ((len(units) - 1) % 2), bufs=1, align_bytes=64)
         shared_scales = keep.tile([P, PASSES, T], U8, name="shared_scales", align_bytes=64)
-        finish_shared(0, shared_codes, shared_scales)
-        finish_shared(1, shared_codes, shared_scales)
+        for a in range(PASSES - 1):
+            finish_shared(a, early_codes[:, a, :], shared_scales[:, a, :])
         finish_routed(*waiting)
-        finish_shared(2, shared_codes, shared_scales)
+        finish_shared(PASSES - 1, late_codes[:], shared_scales[:, PASSES - 1, :])
 
-        for t0, t1 in ((0, TOKEN_CUT), (TOKEN_CUT, T)):
-            back = ring.tile([P, 3, t1 - t0], F32, name="back", tag="back", bufs=2)
-            total = ring.tile([P, t1 - t0], F32, name="total", tag="total", bufs=2)
-            for r in range(3):
-                nc.vector.tensor_copy(back[:, r, :], dx[:].indirect(pos_sb[r][:, t0 // 16 : t1 // 16]))
-                adder = nc.vector if (r == 2 and t1 == T) else nc.gpsimd
-                adder.tensor_tensor(total[:], back[:, r, :], ds[:, t0:t1] if r == 0 else total[:], ADD)
-            nc.sync.dma_start(out[:, t0:t1], total[:])
+        back = keep.tile([P, 3, T], F32, name="back")
+        total = keep.tile([P, T], F32, name="total")
+        halves = ((0, T // 2), (T // 2, T))
+        for r in range(3):
+            for t0, t1 in halves:
+                nc.vector.tensor_copy(back[:, r, t0:t1], dx[:].indirect(pos_sb[r][:, t0 // 16 : t1 // 16]))
+        for r in range(3):
+            for t0, t1 in halves:
+                adder = nc.vector if r == 2 else nc.gpsimd
+                so_far = ds if r == 0 else total
+                adder.tensor_tensor(total[:, t0:t1], back[:, r, t0:t1], so_far[:, t0:t1], ADD)
+                if r == 2:
+                    nc.sync.dma_start(out[:, t0:t1], total[:, t0:t1])

@@ -23,6 +23,7 @@ PACK = 4
 PASSES = N // (P * PACK)
 BANK = 512
 PAD = 16
+RUN = 4
 FIRST = 256
 
 
@@ -70,10 +71,6 @@ def tile_moe_bds_lin_none_kernel(tc, dyT, w_words, w_scales, gate, offs, pos1, p
         scale_rows = w_scales.rearrange("e a f k -> f (e a) k")
         for q in range(4):
             nc.sync.dma_start(wscale[32 * q : 32 * q + 4, :, :].bitcast(I32), scale_rows[4 * q : 4 * q + 4, :, :].bitcast(I32))
-        for j in range(PACK):
-            load_window(2, j)
-        for tile, src in zip(pos_sb, (pos1, pos2, pos3)):
-            nc.sync.dma_start(tile[:], src)
 
         def gather(a, s0, s1, cuts, tag):
             g = ring.tile([P, PACK, s1 - s0], F32, name="g", tag=tag, bufs=1, align_bytes=64)
@@ -89,7 +86,7 @@ def tile_moe_bds_lin_none_kernel(tc, dyT, w_words, w_scales, gate, offs, pos1, p
             return g
 
         def interleave(dst, src):
-            nc.scalar.copy(dst, src.rearrange("p j c -> p c j"))
+            nc.scalar.copy(dst.rearrange("p (c i) j -> p c j i", i=RUN), src.rearrange("p j (c i) -> p c j i", i=RUN))
 
         def quantize(codes, scales, src):
             nc.vector.quantize_mx(out=codes.bitcast(E5M2X4), scales=scales, in_=src[:].rearrange("p c j -> p (c j)"))
@@ -142,8 +139,13 @@ def tile_moe_bds_lin_none_kernel(tc, dyT, w_words, w_scales, gate, offs, pos1, p
             if waiting is not None:
                 finish_routed(*waiting)
             waiting = (a, s0, s1, gb)
-            if 2 <= u < 2 + PASSES * T // BANK:
-                round_shared(u - 2)
+            if 1 <= u <= PASSES * T // BANK:
+                round_shared(u - 1)
+            if u == 2:
+                for j in range(PACK):
+                    load_window(2, j)
+                for tile, src in zip(pos_sb, (pos1, pos2, pos3)):
+                    nc.sync.dma_start(tile[:], src)
         early_codes = ring.tile([P, PASSES - 1, T], U32, name="early_codes", tag="g%d" % (len(units) % 2), bufs=1, align_bytes=64)
         late_codes = ring.tile([P, T], U32, name="late_codes", tag="g%d" % ((len(units) - 1) % 2), bufs=1, align_bytes=64)
         shared_scales = keep.tile([P, PASSES, T], U8, name="shared_scales", align_bytes=64)

@@ -72,8 +72,7 @@ def tile_moe_bds_lin_none_kernel(tc, dyT, w_words, w_scales, gate, offs, pos1, p
         for q in range(4):
             nc.sync.dma_start(wscale[32 * q : 32 * q + 4, :, :].bitcast(I32), scale_rows[4 * q : 4 * q + 4, :, :].bitcast(I32))
 
-        def gather(a, s0, s1, cuts, tag):
-            g = ring.tile([P, PACK, s1 - s0], F32, name="g", tag=tag, bufs=1, align_bytes=64)
+        def gather(g, a, s0, s1, cuts):
             for j in range(PACK):
                 edges = [s0] + (cuts if j == 0 else []) + [s1]
                 for c0, c1 in zip(edges[:-1], edges[1:]):
@@ -83,7 +82,6 @@ def tile_moe_bds_lin_none_kernel(tc, dyT, w_words, w_scales, gate, offs, pos1, p
                         gate_sb[:, c0:c1],
                         MULT,
                     )
-            return g
 
         def interleave(dst, src):
             nc.scalar.copy(dst.rearrange("p (c i) j -> p c j i", i=RUN), src.rearrange("p j (c i) -> p c j i", i=RUN))
@@ -130,12 +128,18 @@ def tile_moe_bds_lin_none_kernel(tc, dyT, w_words, w_scales, gate, offs, pos1, p
         units = [(a, s0, s0 + 2 * C) for a in range(PASSES) for s0 in range(0, S, 2 * C)]
         last = units.pop()
         units.extend([(last[0], last[1], last[1] + C), (last[0], last[1] + C, last[2])])
+        final = len(units) - 1
 
         waiting = None
         for u, (a, s0, s1) in enumerate(units):
-            g = gather(a, s0, s1, [FIRST, 2 * FIRST] if u == 0 else [], "g%d" % (u % 2))
+            parts = 2 if u == final else 1
+            width = (s1 - s0) // parts
+            g = ring.tile([P, parts, PACK, width], F32, name="g", tag="g%d" % (u % 2), bufs=1, align_bytes=64)
             gb = ring.tile([P, s1 - s0, PACK], BF16, name="gb", tag="gb", bufs=2, align_bytes=64)
-            interleave(gb[:], g[:])
+            for h in range(parts):
+                gather(g[:, h, :, :], a, s0 + h * width, s0 + (h + 1) * width, [FIRST, 2 * FIRST] if u == 0 else [])
+            for h in range(parts):
+                interleave(gb[:, h * width : (h + 1) * width, :], g[:, h, :, :])
             if waiting is not None:
                 finish_routed(*waiting)
             waiting = (a, s0, s1, gb)
@@ -146,13 +150,13 @@ def tile_moe_bds_lin_none_kernel(tc, dyT, w_words, w_scales, gate, offs, pos1, p
                     load_window(2, j)
                 for tile, src in zip(pos_sb, (pos1, pos2, pos3)):
                     nc.sync.dma_start(tile[:], src)
-        early_codes = ring.tile([P, PASSES - 1, T], U32, name="early_codes", tag="g%d" % (len(units) % 2), bufs=1, align_bytes=64)
-        late_codes = ring.tile([P, T], U32, name="late_codes", tag="g%d" % ((len(units) - 1) % 2), bufs=1, align_bytes=64)
+        early_codes = ring.tile([P, T], U32, name="early_codes", tag="g%d" % ((final - 1) % 2), bufs=1, align_bytes=64)
+        late_codes = ring.tile([P, PASSES - 1, T], U32, name="late_codes", tag="g%d" % (final % 2), bufs=1, align_bytes=64)
         shared_scales = keep.tile([P, PASSES, T], U8, name="shared_scales", align_bytes=64)
-        for a in range(PASSES - 1):
-            finish_shared(a, early_codes[:, a, :], shared_scales[:, a, :])
+        finish_shared(0, early_codes[:], shared_scales[:, 0, :])
         finish_routed(*waiting)
-        finish_shared(PASSES - 1, late_codes[:], shared_scales[:, PASSES - 1, :])
+        for a in range(1, PASSES):
+            finish_shared(a, late_codes[:, a - 1, :], shared_scales[:, a, :])
 
         back = keep.tile([P, 3, T], F32, name="back")
         total = keep.tile([P, T], F32, name="total")

@@ -25,6 +25,9 @@ BANK = 512
 PAD = 16
 RUN = 4
 FIRST = 256
+LAST = 128
+UNIT = 3 * C
+QUANT = 2 * C
 
 
 def tile_moe_bds_lin_none_kernel(tc, dyT, w_words, w_scales, gate, offs, pos1, pos2, pos3, out):
@@ -38,18 +41,16 @@ def tile_moe_bds_lin_none_kernel(tc, dyT, w_words, w_scales, gate, offs, pos1, p
         pos_sb = [keep.tile([P, T // 16], U16, name="pos_sb%d" % r) for r in range(3)]
         gate_sb = keep.tile([P, S], F32, name="gate_sb")
         window = {}
-        for a in range(PASSES):
-            for j in range(PACK):
-                window[a, j] = keep.tile([P, T + PAD], F32, name="window%d_%d" % (a, j))
         words = keep.tile([P, (E + 1) * PASSES, 2 * K], U8, name="words", align_bytes=64)
         wscale = keep.tile([P, (E + 1) * PASSES, K], U8, name="wscale", align_bytes=64)
         dx = keep.tile([P, S], F32, name="dx")
-        ds = keep.tile([P, T], F32, name="ds")
+        ds = [keep.tile([P, BANK], F32, name="ds%d" % h) for h in range(T // BANK)]
         banks = [psum.tile([P, BANK], F32, name="bank%d" % b) for b in range(E + T // BANK)]
 
         rows = dyT.rearrange("(a p j) t -> a p j t", p=P, j=PACK)
 
         def load_window(a, j):
+            window[a, j] = ring.tile([P, UNIT + PAD], F32, name="window", tag="window%d" % j, bufs=2)
             nc.sync.dma_start(window[a, j][:, 0:T], rows[a, :, j, :])
 
         def load_gate(c0, c1):
@@ -59,12 +60,11 @@ def tile_moe_bds_lin_none_kernel(tc, dyT, w_words, w_scales, gate, offs, pos1, p
         nc.sync.dma_start(offs_sb[:], offs)
         load_gate(0, FIRST)
         load_window(0, 0)
-        load_gate(FIRST, 2 * FIRST)
-        load_gate(2 * FIRST, 2 * C)
+        load_gate(FIRST, 3 * FIRST)
+        load_gate(3 * FIRST, UNIT)
         for j in range(1, PACK):
             load_window(0, j)
-        load_gate(2 * C, 4 * C)
-        load_gate(4 * C, S)
+        load_gate(UNIT, S)
         for j in range(PACK):
             load_window(1, j)
         nc.sync.dma_start(words[:].bitcast(I32), w_words.rearrange("e a p b -> p (e a) b").bitcast(I32))
@@ -87,7 +87,7 @@ def tile_moe_bds_lin_none_kernel(tc, dyT, w_words, w_scales, gate, offs, pos1, p
             nc.scalar.copy(dst.rearrange("p (c i) j -> p c j i", i=RUN), src.rearrange("p j (c i) -> p c j i", i=RUN))
 
         def quantize(codes, scales, src):
-            nc.vector.quantize_mx(out=codes.bitcast(E5M2X4), scales=scales, in_=src[:].rearrange("p c j -> p (c j)"))
+            nc.vector.quantize_mx(out=codes.bitcast(E5M2X4), scales=scales, in_=src.rearrange("p c j -> p (c j)"))
 
         def multiply(a, e, bank, codes, scales, c0):
             m = e * PASSES + a
@@ -101,73 +101,92 @@ def tile_moe_bds_lin_none_kernel(tc, dyT, w_words, w_scales, gate, offs, pos1, p
                 stop=(a == PASSES - 1),
             )
 
-        def finish_routed(a, s0, s1, gb):
+        gb = keep.tile([P, S, PACK], BF16, name="gb", align_bytes=64)
+
+        def finish_routed(a, s0, s1):
             codes = ring.tile([P, s1 - s0], U32, name="codes", tag="codes", bufs=2, align_bytes=64)
             scales = ring.tile([P, s1 - s0], U8, name="scales", tag="scales", bufs=2, align_bytes=64)
-            quantize(codes[:], scales[:], gb)
+            quantize(codes[:], scales[:], gb[:, s0:s1, :])
             for e in range(s0 // C, s1 // C):
                 multiply(a, e, e, codes, scales, e * C - s0)
-                if a == PASSES - 1:
+
+        def empty_banks(a, s0, s1):
+            if a == PASSES - 1:
+                for e in range(s0 // C, s1 // C):
                     nc.scalar.copy(dx[:, e * C : (e + 1) * C], banks[e][:])
 
-        shared_b = [keep.tile([P, T, PACK], BF16, name="shared_b%d" % a, align_bytes=64) for a in range(PASSES)]
+        shared_b = [keep.tile([P, PASSES, BANK, PACK], BF16, name="shared_b%d" % h, align_bytes=64) for h in range(T // BANK)]
 
         def round_shared(piece):
             a, h = divmod(piece, T // BANK)
             raw = ring.tile([P, PACK, BANK], F32, name="raw", tag="raw", bufs=2)
             nc.sync.dma_start(raw[:], rows[a, :, :, h * BANK : (h + 1) * BANK])
-            interleave(shared_b[a][:, h * BANK : (h + 1) * BANK, :], raw[:])
+            interleave(shared_b[h][:, a, :, :], raw[:])
 
-        def finish_shared(a, codes, scales):
-            quantize(codes, scales, shared_b[a])
-            for h in range(T // BANK):
-                multiply(a, E, E + h, codes, scales, h * BANK)
-                if a == PASSES - 1:
-                    nc.scalar.copy(ds[:, h * BANK : (h + 1) * BANK], banks[E + h][:])
+        def finish_shared(h, codes, scales):
+            flat = shared_b[h][:].rearrange("p a c j -> p (a c) j")
+            for c0, c1 in ((0, 2 * BANK), (2 * BANK, PASSES * BANK)):
+                quantize(codes[:, c0:c1], scales[:, c0:c1], flat[:, c0:c1, :])
+            for a in range(PASSES):
+                multiply(a, E, E + h, codes, scales, a * BANK)
+            nc.scalar.copy(ds[h][:], banks[E + h][:])
 
-        units = [(a, s0, s0 + 2 * C) for a in range(PASSES) for s0 in range(0, S, 2 * C)]
+        units = [(a, s0, s0 + UNIT) for a in range(PASSES) for s0 in range(0, S, UNIT)]
         last = units.pop()
-        units.extend([(last[0], last[1], last[1] + C), (last[0], last[1] + C, last[2])])
+        units.extend([(last[0], last[1], last[2] - C), (last[0], last[2] - C, last[2])])
         final = len(units) - 1
 
-        waiting = None
+        waiting = []
+        done = 0
         for u, (a, s0, s1) in enumerate(units):
-            parts = 2 if u == final else 1
-            width = (s1 - s0) // parts
-            g = ring.tile([P, parts, PACK, width], F32, name="g", tag="g%d" % (u % 2), bufs=1, align_bytes=64)
-            gb = ring.tile([P, s1 - s0, PACK], BF16, name="gb", tag="gb", bufs=2, align_bytes=64)
-            for h in range(parts):
-                gather(g[:, h, :, :], a, s0 + h * width, s0 + (h + 1) * width, [FIRST, 2 * FIRST] if u == 0 else [])
-            for h in range(parts):
-                interleave(gb[:, h * width : (h + 1) * width, :], g[:, h, :, :])
-            if waiting is not None:
-                finish_routed(*waiting)
-            waiting = (a, s0, s1, gb)
-            if 1 <= u <= PASSES * T // BANK:
-                round_shared(u - 1)
-            if u == 2:
+            g = ring.tile([P, PACK, s1 - s0], F32, name="g", tag="g%d" % (u % 2), bufs=1, align_bytes=64)
+            gather(g, a, s0, s1, [FIRST, 3 * FIRST] if u == 0 else [])
+            for piece in waiting:
+                finish_routed(*piece)
+            edges = [s0] + [c for c in range(s0 + 1, s1) if c % QUANT == 0] + [s1]
+            for e0, e1 in zip(edges[:-1], edges[1:]):
+                interleave(gb[:, e0:e1, :], g[:, :, e0 - s0 : e1 - s0])
+            for piece in waiting:
+                empty_banks(*piece)
+            waiting = []
+            done = done % S
+            while done + QUANT <= s1:
+                waiting.append((a, done, done + QUANT))
+                done = done + QUANT
+            if u >= final - 1 and done < s1:
+                waiting.append((a, done, s1))
+                done = s1
+            if 1 <= u <= PASSES:
+                round_shared(2 * u - 2)
+                round_shared(2 * u - 1)
+            if u == 1:
                 for j in range(PACK):
                     load_window(2, j)
                 for tile, src in zip(pos_sb, (pos1, pos2, pos3)):
                     nc.sync.dma_start(tile[:], src)
-        early_codes = ring.tile([P, T], U32, name="early_codes", tag="g%d" % ((final - 1) % 2), bufs=1, align_bytes=64)
-        late_codes = ring.tile([P, PASSES - 1, T], U32, name="late_codes", tag="g%d" % (final % 2), bufs=1, align_bytes=64)
-        shared_scales = keep.tile([P, PASSES, T], U8, name="shared_scales", align_bytes=64)
-        finish_shared(0, early_codes[:], shared_scales[:, 0, :])
-        finish_routed(*waiting)
-        for a in range(1, PASSES):
-            finish_shared(a, late_codes[:, a - 1, :], shared_scales[:, a, :])
+        early_codes = ring.tile([P, PASSES * BANK], U32, name="early_codes", tag="g%d" % ((final - 1) % 2), bufs=1, align_bytes=64)
+        late_codes = ring.tile([P, PASSES * BANK], U32, name="late_codes", tag="g%d" % (final % 2), bufs=1, align_bytes=64)
+        shared_scales = keep.tile([P, T // BANK, PASSES * BANK], U8, name="shared_scales", align_bytes=64)
+        finish_shared(0, early_codes, shared_scales[:, 0, :])
+        finish_routed(*waiting[0])
+        empty_banks(*waiting[0])
+        finish_shared(1, late_codes, shared_scales[:, 1, :])
 
-        back = keep.tile([P, 3, T], F32, name="back")
-        total = keep.tile([P, T], F32, name="total")
-        halves = ((0, T // 2), (T // 2, T))
-        for r in range(3):
-            for t0, t1 in halves:
-                nc.vector.tensor_copy(back[:, r, t0:t1], dx[:].indirect(pos_sb[r][:, t0 // 16 : t1 // 16]))
-        for r in range(3):
-            for t0, t1 in halves:
-                adder = nc.vector if r == 2 else nc.gpsimd
-                so_far = ds if r == 0 else total
-                adder.tensor_tensor(total[:, t0:t1], back[:, r, t0:t1], so_far[:, t0:t1], ADD)
-                if r == 2:
-                    nc.sync.dma_start(out[:, t0:t1], total[:, t0:t1])
+        sums = [keep.tile([P, T], F32, name="sums%d" % r) for r in range(3)]
+
+        def fetch(r, t0, t1):
+            so_far = ds[t0 // BANK][:, t0 % BANK : t0 % BANK + t1 - t0] if r == 0 else sums[r - 1][:, t0:t1]
+            nc.vector.tensor_tensor(sums[r][:, t0:t1], dx[:].indirect(pos_sb[r][:, t0 // 16 : t1 // 16]), so_far, ADD)
+            if r == 2:
+                nc.sync.dma_start(out[:, t0:t1], sums[r][:, t0:t1])
+
+        half = BANK // 2
+        cut = T - LAST
+        for r in range(2):
+            fetch(r, 0, half)
+            fetch(r, half, BANK)
+        fetch(0, BANK, T)
+        fetch(2, 0, BANK)
+        for r in range(1, 3):
+            fetch(r, BANK, cut)
+            fetch(r, cut, T)

@@ -50,7 +50,7 @@ def tile_moe_bds_lin_none_kernel(tc, dyT, w_words, w_scales, gate, offs, pos1, p
         rows = dyT.rearrange("(a p j) t -> a p j t", p=P, j=PACK)
 
         def load_window(a, j):
-            window[a, j] = ring.tile([P, UNIT + PAD], F32, name="window", tag="window%d" % j, bufs=2)
+            window[a, j] = ring.tile([P, UNIT + PAD], F32, name="window", tag="window%d" % j, bufs=PASSES)
             nc.sync.dma_start(window[a, j][:, 0:T], rows[a, :, j, :])
 
         def load_gate(c0, c1):
@@ -65,12 +65,15 @@ def tile_moe_bds_lin_none_kernel(tc, dyT, w_words, w_scales, gate, offs, pos1, p
         for j in range(1, PACK):
             load_window(0, j)
         load_gate(UNIT, S)
-        for j in range(PACK):
-            load_window(1, j)
+        for a in range(1, PASSES):
+            for j in range(PACK):
+                load_window(a, j)
         nc.sync.dma_start(words[:].bitcast(I32), w_words.rearrange("e a p b -> p (e a) b").bitcast(I32))
         scale_rows = w_scales.rearrange("e a f k -> f (e a) k")
         for q in range(4):
             nc.sync.dma_start(wscale[32 * q : 32 * q + 4, :, :].bitcast(I32), scale_rows[4 * q : 4 * q + 4, :, :].bitcast(I32))
+        for tile, src in zip(pos_sb, (pos1, pos2, pos3)):
+            nc.sync.dma_start(tile[:], src)
 
         def gather(g, a, s0, s1, cuts):
             for j in range(PACK):
@@ -103,16 +106,17 @@ def tile_moe_bds_lin_none_kernel(tc, dyT, w_words, w_scales, gate, offs, pos1, p
 
         gb = keep.tile([P, S, PACK], BF16, name="gb", align_bytes=64)
 
-        def finish_routed(a, s0, s1):
-            codes = ring.tile([P, s1 - s0], U32, name="codes", tag="codes", bufs=2, align_bytes=64)
-            scales = ring.tile([P, s1 - s0], U8, name="scales", tag="scales", bufs=2, align_bytes=64)
-            quantize(codes[:], scales[:], gb[:, s0:s1, :])
-            for e in range(s0 // C, s1 // C):
-                multiply(a, e, e, codes, scales, e * C - s0)
+        def finish_routed(blocks, r0):
+            width = len(blocks) * C
+            codes = ring.tile([P, width], U32, name="codes", tag="codes", bufs=2, align_bytes=64)
+            scales = ring.tile([P, width], U8, name="scales", tag="scales", bufs=2, align_bytes=64)
+            quantize(codes[:], scales[:], gb[:, r0 : r0 + width, :])
+            for i, (a, e) in enumerate(blocks):
+                multiply(a, e, e, codes, scales, i * C)
 
-        def empty_banks(a, s0, s1):
-            if a == PASSES - 1:
-                for e in range(s0 // C, s1 // C):
+        def empty_banks(blocks, r0):
+            for a, e in blocks:
+                if a == PASSES - 1:
                     nc.scalar.copy(dx[:, e * C : (e + 1) * C], banks[e][:])
 
         shared_b = [keep.tile([P, PASSES, BANK, PACK], BF16, name="shared_b%d" % h, align_bytes=64) for h in range(T // BANK)]
@@ -131,39 +135,37 @@ def tile_moe_bds_lin_none_kernel(tc, dyT, w_words, w_scales, gate, offs, pos1, p
                 multiply(a, E, E + h, codes, scales, a * BANK)
             nc.scalar.copy(ds[h][:], banks[E + h][:])
 
-        units = [(a, s0, s0 + UNIT) for a in range(PASSES) for s0 in range(0, S, UNIT)]
+        units = [(0, 0, UNIT), (0, UNIT, S)]
+        units.extend([(a, s0, s0 + UNIT) for s0 in range(0, S, UNIT) for a in range(1, PASSES)])
         last = units.pop()
         units.extend([(last[0], last[1], last[2] - C), (last[0], last[2] - C, last[2])])
         final = len(units) - 1
 
         waiting = []
-        done = 0
+        staged = []
+        r_in = 0
+        r_out = 0
         for u, (a, s0, s1) in enumerate(units):
             g = ring.tile([P, PACK, s1 - s0], F32, name="g", tag="g%d" % (u % 2), bufs=1, align_bytes=64)
             gather(g, a, s0, s1, [FIRST, 3 * FIRST] if u == 0 else [])
             for piece in waiting:
                 finish_routed(*piece)
-            edges = [s0] + [c for c in range(s0 + 1, s1) if c % QUANT == 0] + [s1]
+            r1 = r_in + s1 - s0
+            edges = [r_in] + [c for c in range(r_in + 1, r1) if c % QUANT == 0] + [r1]
             for e0, e1 in zip(edges[:-1], edges[1:]):
-                interleave(gb[:, e0:e1, :], g[:, :, e0 - s0 : e1 - s0])
+                interleave(gb[:, e0:e1, :], g[:, :, e0 - r_in : e1 - r_in])
+            r_in = r1 % S
             for piece in waiting:
                 empty_banks(*piece)
             waiting = []
-            done = done % S
-            while done + QUANT <= s1:
-                waiting.append((a, done, done + QUANT))
-                done = done + QUANT
-            if u >= final - 1 and done < s1:
-                waiting.append((a, done, s1))
-                done = s1
+            staged.extend([(a, e) for e in range(s0 // C, s1 // C)])
+            while len(staged) >= QUANT // C or (staged and u >= final - 1):
+                blocks, staged = staged[: QUANT // C], staged[QUANT // C :]
+                waiting.append((blocks, r_out))
+                r_out = (r_out + len(blocks) * C) % S
             if 1 <= u <= PASSES:
                 round_shared(2 * u - 2)
                 round_shared(2 * u - 1)
-            if u == 1:
-                for j in range(PACK):
-                    load_window(2, j)
-                for tile, src in zip(pos_sb, (pos1, pos2, pos3)):
-                    nc.sync.dma_start(tile[:], src)
         early_codes = ring.tile([P, PASSES * BANK], U32, name="early_codes", tag="g%d" % ((final - 1) % 2), bufs=1, align_bytes=64)
         late_codes = ring.tile([P, PASSES * BANK], U32, name="late_codes", tag="g%d" % (final % 2), bufs=1, align_bytes=64)
         shared_scales = keep.tile([P, T // BANK, PASSES * BANK], U8, name="shared_scales", align_bytes=64)
@@ -172,7 +174,7 @@ def tile_moe_bds_lin_none_kernel(tc, dyT, w_words, w_scales, gate, offs, pos1, p
         empty_banks(*waiting[0])
         finish_shared(1, late_codes, shared_scales[:, 1, :])
 
-        sums = [keep.tile([P, T], F32, name="sums%d" % r) for r in range(3)]
+        sums = [ring.tile([P, T], F32, name="sums", tag="window%d" % r, bufs=PASSES) for r in range(3)]
 
         def fetch(r, t0, t1):
             so_far = ds[t0 // BANK][:, t0 % BANK : t0 % BANK + t1 - t0] if r == 0 else sums[r - 1][:, t0:t1]

@@ -24,7 +24,7 @@ PASSES = N // (P * PACK)
 BANK = 512
 PAD = 16
 RUN = 4
-FIRST = 256
+FIRST = 128
 LAST = 128
 UNIT = 3 * C
 QUANT = 2 * C
@@ -57,11 +57,12 @@ def tile_moe_bds_lin_none_kernel(tc, dyT, w_words, w_scales, gate, offs, pos1, p
             nc.sync.dma_start(gate_sb[:, c0:c1], gate[0:P, c0:c1])
 
         nc.gpsimd.memset(wscale[:].rearrange("p m k -> p (m k)").bitcast(I32), 0)
+        load_window(0, 0)
         nc.sync.dma_start(offs_sb[:], offs)
         load_gate(0, FIRST)
-        load_window(0, 0)
         load_gate(FIRST, 3 * FIRST)
-        load_gate(3 * FIRST, UNIT)
+        load_gate(3 * FIRST, 7 * FIRST)
+        load_gate(7 * FIRST, UNIT)
         for j in range(1, PACK):
             load_window(0, j)
         load_gate(UNIT, S)
@@ -121,19 +122,22 @@ def tile_moe_bds_lin_none_kernel(tc, dyT, w_words, w_scales, gate, offs, pos1, p
 
         shared_b = [keep.tile([P, PASSES, BANK, PACK], BF16, name="shared_b%d" % h, align_bytes=64) for h in range(T // BANK)]
 
+        shared_scales = keep.tile([P, T // BANK, PASSES * BANK], U8, name="shared_scales", align_bytes=64)
+
         def round_shared(piece):
             a, h = divmod(piece, T // BANK)
             raw = ring.tile([P, PACK, BANK], F32, name="raw", tag="raw", bufs=2)
             nc.sync.dma_start(raw[:], rows[a, :, :, h * BANK : (h + 1) * BANK])
             interleave(shared_b[h][:, a, :, :], raw[:])
 
-        def finish_shared(h, codes, scales):
+        def finish_shared(h, a0, a1, codes):
             flat = shared_b[h][:].rearrange("p a c j -> p (a c) j")
-            for c0, c1 in ((0, 2 * BANK), (2 * BANK, PASSES * BANK)):
-                quantize(codes[:, c0:c1], scales[:, c0:c1], flat[:, c0:c1, :])
-            for a in range(PASSES):
-                multiply(a, E, E + h, codes, scales, a * BANK)
-            nc.scalar.copy(ds[h][:], banks[E + h][:])
+            scales = shared_scales[:, h, a0 * BANK : a1 * BANK]
+            quantize(codes, scales, flat[:, a0 * BANK : a1 * BANK, :])
+            for a in range(a0, a1):
+                multiply(a, E, E + h, codes, scales, (a - a0) * BANK)
+            if a1 == PASSES:
+                nc.scalar.copy(ds[h][:], banks[E + h][:])
 
         units = [(0, 0, UNIT), (0, UNIT, S)]
         units.extend([(a, s0, s0 + UNIT) for s0 in range(0, S, UNIT) for a in range(1, PASSES)])
@@ -147,7 +151,7 @@ def tile_moe_bds_lin_none_kernel(tc, dyT, w_words, w_scales, gate, offs, pos1, p
         r_out = 0
         for u, (a, s0, s1) in enumerate(units):
             g = ring.tile([P, PACK, s1 - s0], F32, name="g", tag="g%d" % (u % 2), bufs=1, align_bytes=64)
-            gather(g, a, s0, s1, [FIRST, 3 * FIRST] if u == 0 else [])
+            gather(g, a, s0, s1, [FIRST, 3 * FIRST, 7 * FIRST] if u == 0 else [])
             for piece in waiting:
                 finish_routed(*piece)
             r1 = r_in + s1 - s0
@@ -166,13 +170,14 @@ def tile_moe_bds_lin_none_kernel(tc, dyT, w_words, w_scales, gate, offs, pos1, p
             if 1 <= u <= PASSES:
                 round_shared(2 * u - 2)
                 round_shared(2 * u - 1)
-        early_codes = ring.tile([P, PASSES * BANK], U32, name="early_codes", tag="g%d" % ((final - 1) % 2), bufs=1, align_bytes=64)
-        late_codes = ring.tile([P, PASSES * BANK], U32, name="late_codes", tag="g%d" % (final % 2), bufs=1, align_bytes=64)
-        shared_scales = keep.tile([P, T // BANK, PASSES * BANK], U8, name="shared_scales", align_bytes=64)
-        finish_shared(0, early_codes, shared_scales[:, 0, :])
+        early_codes = ring.tile([P, 2 * BANK], U32, name="early_codes", tag="g%d" % ((final - 1) % 2), bufs=1, align_bytes=64)
+        late_codes = ring.tile([P, 4 * BANK], U32, name="late_codes", tag="g%d" % (final % 2), bufs=1, align_bytes=64)
+        finish_shared(0, 0, 2, early_codes[:])
         finish_routed(*waiting[0])
         empty_banks(*waiting[0])
-        finish_shared(1, late_codes, shared_scales[:, 1, :])
+        finish_shared(0, 2, PASSES, late_codes[:, 0:BANK])
+        finish_shared(1, 0, 2, late_codes[:, BANK : 3 * BANK])
+        finish_shared(1, 2, PASSES, late_codes[:, 3 * BANK : 4 * BANK])
 
         sums = [ring.tile([P, T], F32, name="sums", tag="window%d" % r, bufs=PASSES) for r in range(3)]
 

@@ -28,6 +28,8 @@ FIRST = 128
 LAST = 128
 UNIT = 3 * C
 QUANT = 2 * C
+RAW = 2
+HEAD = [FIRST, 3 * FIRST, 7 * FIRST, 15 * FIRST]
 
 
 def tile_moe_bds_lin_none_kernel(tc, dyT, w_words, w_scales, gate, offs, pos1, pos2, pos3, out):
@@ -43,15 +45,19 @@ def tile_moe_bds_lin_none_kernel(tc, dyT, w_words, w_scales, gate, offs, pos1, p
         window = {}
         words = keep.tile([P, (E + 1) * PASSES, 2 * K], U8, name="words", align_bytes=64)
         wscale = keep.tile([P, (E + 1) * PASSES, K], U8, name="wscale", align_bytes=64)
-        dx = keep.tile([P, S], F32, name="dx")
-        ds = [keep.tile([P, BANK], F32, name="ds%d" % h) for h in range(T // BANK)]
         banks = [psum.tile([P, BANK], F32, name="bank%d" % b) for b in range(E + T // BANK)]
 
         rows = dyT.rearrange("(a p j) t -> a p j t", p=P, j=PACK)
 
         def load_window(a, j):
-            window[a, j] = ring.tile([P, UNIT + PAD], F32, name="window", tag="window%d" % j, bufs=PASSES)
+            window[a, j] = ring.tile([P, S + PAD], F32, name="window", tag="window", bufs=PACK + 1)
             nc.sync.dma_start(window[a, j][:, 0:T], rows[a, :, j, :])
+            if j >= RAW:
+                h = j - RAW
+                nc.sync.dma_start(raw_piece(a, h), rows[a, :, :, h * BANK : (h + 1) * BANK])
+
+        def raw_piece(a, h):
+            return window[a, RAW + h][:, T : T + PACK * BANK].rearrange("p (j c) -> p j c", j=PACK)
 
         def load_gate(c0, c1):
             nc.sync.dma_start(gate_sb[:, c0:c1], gate[0:P, c0:c1])
@@ -59,25 +65,24 @@ def tile_moe_bds_lin_none_kernel(tc, dyT, w_words, w_scales, gate, offs, pos1, p
         nc.gpsimd.memset(wscale[:].rearrange("p m k -> p (m k)").bitcast(I32), 0)
         load_window(0, 0)
         nc.sync.dma_start(offs_sb[:], offs)
-        load_gate(0, FIRST)
-        load_gate(FIRST, 3 * FIRST)
-        load_gate(3 * FIRST, 7 * FIRST)
-        load_gate(7 * FIRST, UNIT)
+        for c0, c1 in zip([0] + HEAD, HEAD + [S]):
+            load_gate(c0, c1)
         for j in range(1, PACK):
             load_window(0, j)
-        load_gate(UNIT, S)
-        for a in range(1, PASSES):
-            for j in range(PACK):
-                load_window(a, j)
-        nc.sync.dma_start(words[:].bitcast(I32), w_words.rearrange("e a p b -> p (e a) b").bitcast(I32))
-        scale_rows = w_scales.rearrange("e a f k -> f (e a) k")
-        for q in range(4):
-            nc.sync.dma_start(wscale[32 * q : 32 * q + 4, :, :].bitcast(I32), scale_rows[4 * q : 4 * q + 4, :, :].bitcast(I32))
-        for tile, src in zip(pos_sb, (pos1, pos2, pos3)):
-            nc.sync.dma_start(tile[:], src)
+        load_window(1, 0)
 
-        def gather(g, a, s0, s1, cuts):
+        def load_weights():
+            nc.sync.dma_start(words[:].bitcast(I32), w_words.rearrange("e a p b -> p (e a) b").bitcast(I32))
+            scale_rows = w_scales.rearrange("e a f k -> f (e a) k")
+            for q in range(4):
+                nc.sync.dma_start(wscale[32 * q : 32 * q + 4, :, :].bitcast(I32), scale_rows[4 * q : 4 * q + 4, :, :].bitcast(I32))
+            for tile, src in zip(pos_sb, (pos1, pos2, pos3)):
+                nc.sync.dma_start(tile[:], src)
+
+        def gather(g, a, s0, s1, cuts, waiting):
             for j in range(PACK):
+                if 0 <= j - 1 - PACK + len(waiting):
+                    finish_routed(*waiting[j - 1 - PACK + len(waiting)])
                 edges = [s0] + (cuts if j == 0 else []) + [s1]
                 for c0, c1 in zip(edges[:-1], edges[1:]):
                     nc.vector.tensor_tensor(
@@ -122,13 +127,10 @@ def tile_moe_bds_lin_none_kernel(tc, dyT, w_words, w_scales, gate, offs, pos1, p
 
         shared_b = [keep.tile([P, PASSES, BANK, PACK], BF16, name="shared_b%d" % h, align_bytes=64) for h in range(T // BANK)]
 
-        shared_scales = keep.tile([P, T // BANK, PASSES * BANK], U8, name="shared_scales", align_bytes=64)
 
-        def round_shared(piece):
-            a, h = divmod(piece, T // BANK)
-            raw = ring.tile([P, PACK, BANK], F32, name="raw", tag="raw", bufs=2)
-            nc.sync.dma_start(raw[:], rows[a, :, :, h * BANK : (h + 1) * BANK])
-            interleave(shared_b[h][:, a, :, :], raw[:])
+        def round_shared(a):
+            for h in range(T // BANK):
+                interleave(shared_b[h][:, a, :, :], raw_piece(a, h))
 
         def finish_shared(h, a0, a1, codes):
             flat = shared_b[h][:].rearrange("p a c j -> p (a c) j")
@@ -137,12 +139,9 @@ def tile_moe_bds_lin_none_kernel(tc, dyT, w_words, w_scales, gate, offs, pos1, p
             for a in range(a0, a1):
                 multiply(a, E, E + h, codes, scales, (a - a0) * BANK)
             if a1 == PASSES:
-                nc.scalar.copy(ds[h][:], banks[E + h][:])
+                nc.scalar.copy(ds[h], banks[E + h][:])
 
-        units = [(0, 0, UNIT), (0, UNIT, S)]
-        units.extend([(a, s0, s0 + UNIT) for s0 in range(0, S, UNIT) for a in range(1, PASSES)])
-        last = units.pop()
-        units.extend([(last[0], last[1], last[2] - C), (last[0], last[2] - C, last[2])])
+        units = [(0, 0, S), (1, 0, S), (2, 0, UNIT), (2, UNIT, S - C), (2, S - C, S)]
         final = len(units) - 1
 
         waiting = []
@@ -151,8 +150,21 @@ def tile_moe_bds_lin_none_kernel(tc, dyT, w_words, w_scales, gate, offs, pos1, p
         r_out = 0
         for u, (a, s0, s1) in enumerate(units):
             g = ring.tile([P, PACK, s1 - s0], F32, name="g", tag="g%d" % (u % 2), bufs=1, align_bytes=64)
-            gather(g, a, s0, s1, [FIRST, 3 * FIRST, 7 * FIRST] if u == 0 else [])
-            for piece in waiting:
+            if u == 0:
+                round_shared(0)
+            gather(g, a, s0, s1, HEAD if u == 0 else [], waiting)
+            if u == 0:
+                for j in range(1, PACK):
+                    load_window(1, j)
+                load_weights()
+                round_shared(1)
+            if u == 1:
+                for j in range(PACK):
+                    load_window(2, j)
+                round_shared(2)
+            if u == 2:
+                dx = ring.tile([P, S], F32, name="dx", tag="window", bufs=PACK + 1)
+            for piece in waiting[-1:]:
                 finish_routed(*piece)
             r1 = r_in + s1 - s0
             edges = [r_in] + [c for c in range(r_in + 1, r1) if c % QUANT == 0] + [r1]
@@ -167,19 +179,19 @@ def tile_moe_bds_lin_none_kernel(tc, dyT, w_words, w_scales, gate, offs, pos1, p
                 blocks, staged = staged[: QUANT // C], staged[QUANT // C :]
                 waiting.append((blocks, r_out))
                 r_out = (r_out + len(blocks) * C) % S
-            if 1 <= u <= PASSES:
-                round_shared(2 * u - 2)
-                round_shared(2 * u - 1)
         early_codes = ring.tile([P, 2 * BANK], U32, name="early_codes", tag="g%d" % ((final - 1) % 2), bufs=1, align_bytes=64)
         late_codes = ring.tile([P, 4 * BANK], U32, name="late_codes", tag="g%d" % (final % 2), bufs=1, align_bytes=64)
+        shared_scales = ring.tile([P, T // BANK, PASSES * BANK], U8, name="shared_scales", tag="g_scales", bufs=1, align_bytes=64)
+        partial = ring.tile([P, 2, T], F32, name="partial", tag="window", bufs=PACK + 1)
+        further = ring.tile([P, 2, T], F32, name="further", tag="window", bufs=PACK + 1)
+        ds = [partial[:, 0, h * BANK : (h + 1) * BANK] for h in range(T // BANK)]
+        sums = [partial[:, 1, :], further[:, 0, :], further[:, 1, :]]
         finish_shared(0, 0, 2, early_codes[:])
         finish_routed(*waiting[0])
         empty_banks(*waiting[0])
         finish_shared(0, 2, PASSES, late_codes[:, 0:BANK])
         finish_shared(1, 0, 2, late_codes[:, BANK : 3 * BANK])
         finish_shared(1, 2, PASSES, late_codes[:, 3 * BANK : 4 * BANK])
-
-        sums = [ring.tile([P, T], F32, name="sums", tag="window%d" % r, bufs=PASSES) for r in range(3)]
 
         def fetch(r, t0, t1):
             so_far = ds[t0 // BANK][:, t0 % BANK : t0 % BANK + t1 - t0] if r == 0 else sums[r - 1][:, t0:t1]

@@ -28,7 +28,6 @@ FIRST = 128
 LAST = 128
 UNIT = 3 * C
 QUANT = 2 * C
-RAW = 2
 HEAD = [FIRST, 3 * FIRST, 7 * FIRST, 15 * FIRST]
 
 
@@ -52,12 +51,13 @@ def tile_moe_bds_lin_none_kernel(tc, dyT, w_words, w_scales, gate, offs, pos1, p
         def load_window(a, j):
             window[a, j] = ring.tile([P, S + PAD], F32, name="window", tag="window", bufs=PACK + 1)
             nc.sync.dma_start(window[a, j][:, 0:T], rows[a, :, j, :])
-            if j >= RAW:
-                h = j - RAW
-                nc.sync.dma_start(raw_piece(a, h), rows[a, :, :, h * BANK : (h + 1) * BANK])
+
+        raw_early = ring.tile([P, PASSES - 1, PACK, T], F32, name="raw_early", tag="g1", bufs=1, align_bytes=64)
+        raw_last = ring.tile([P, PACK, T], F32, name="raw_last", tag="gb", bufs=1, align_bytes=64)
+        raw = [raw_early[:, a, :, :] for a in range(PASSES - 1)] + [raw_last[:]]
 
         def raw_piece(a, h):
-            return window[a, RAW + h][:, T : T + PACK * BANK].rearrange("p (j c) -> p j c", j=PACK)
+            return raw[a][:, :, h * BANK : (h + 1) * BANK]
 
         def load_gate(c0, c1):
             nc.sync.dma_start(gate_sb[:, c0:c1], gate[0:P, c0:c1])
@@ -69,6 +69,7 @@ def tile_moe_bds_lin_none_kernel(tc, dyT, w_words, w_scales, gate, offs, pos1, p
             load_gate(c0, c1)
         for j in range(1, PACK):
             load_window(0, j)
+            nc.sync.dma_start(raw[j - 1], rows[j - 1])
         load_window(1, 0)
 
         def load_weights():
@@ -110,7 +111,6 @@ def tile_moe_bds_lin_none_kernel(tc, dyT, w_words, w_scales, gate, offs, pos1, p
                 stop=(a == PASSES - 1),
             )
 
-        gb = keep.tile([P, S, PACK], BF16, name="gb", align_bytes=64)
 
         def finish_routed(blocks, r0):
             width = len(blocks) * C
@@ -141,6 +141,10 @@ def tile_moe_bds_lin_none_kernel(tc, dyT, w_words, w_scales, gate, offs, pos1, p
             if a1 == PASSES:
                 nc.scalar.copy(ds[h], banks[E + h][:])
 
+        for a in range(PASSES):
+            round_shared(a)
+        gb = ring.tile([P, S, PACK], BF16, name="gb", tag="gb", bufs=1, align_bytes=64)
+
         units = [(0, 0, S), (1, 0, S), (2, 0, UNIT), (2, UNIT, S - C), (2, S - C, S)]
         final = len(units) - 1
 
@@ -150,18 +154,14 @@ def tile_moe_bds_lin_none_kernel(tc, dyT, w_words, w_scales, gate, offs, pos1, p
         r_out = 0
         for u, (a, s0, s1) in enumerate(units):
             g = ring.tile([P, PACK, s1 - s0], F32, name="g", tag="g%d" % (u % 2), bufs=1, align_bytes=64)
-            if u == 0:
-                round_shared(0)
             gather(g, a, s0, s1, HEAD if u == 0 else [], waiting)
             if u == 0:
                 for j in range(1, PACK):
                     load_window(1, j)
                 load_weights()
-                round_shared(1)
             if u == 1:
                 for j in range(PACK):
                     load_window(2, j)
-                round_shared(2)
             if u == 2:
                 dx = ring.tile([P, S], F32, name="dx", tag="window", bufs=PACK + 1)
             for piece in waiting[-1:]:

@@ -49,7 +49,7 @@ def tile_moe_bds_lin_none_kernel(tc, dyT, w_words, w_scales, gate, offs, pos1, p
         rows = dyT.rearrange("(a p j) t -> a p j t", p=P, j=PACK)
 
         def load_window(a, j):
-            window[a, j] = ring.tile([P, S + PAD], F32, name="window", tag="window", bufs=PACK + 1)
+            window[a, j] = ring.tile([P, S + PAD], F32, name="window", tag="window", bufs=PACK + 1, align_bytes=64)
             nc.sync.dma_start(window[a, j][:, 0:T], rows[a, :, j, :])
 
         raw_early = ring.tile([P, PASSES - 1, PACK, T], F32, name="raw_early", tag="g1", bufs=1, align_bytes=64)
@@ -125,21 +125,24 @@ def tile_moe_bds_lin_none_kernel(tc, dyT, w_words, w_scales, gate, offs, pos1, p
                 if a == PASSES - 1:
                     nc.scalar.copy(dx[:, e * C : (e + 1) * C], banks[e][:])
 
-        shared_b = [keep.tile([P, PASSES, BANK, PACK], BF16, name="shared_b%d" % h, align_bytes=64) for h in range(T // BANK)]
-
+        held = keep.tile([P, 1 + PASSES * T // BANK, BANK, PACK], BF16, name="held", align_bytes=64)
+        held_blocks = [(PASSES - 2, E - 1, E - 1)] + [(a, E, E + h) for h in range(T // BANK) for a in range(PASSES)]
 
         def round_shared(a):
             for h in range(T // BANK):
-                interleave(shared_b[h][:, a, :, :], raw_piece(a, h))
+                interleave(held[:, 1 + h * PASSES + a, :, :], raw_piece(a, h))
 
-        def finish_shared(h, a0, a1, codes):
-            flat = shared_b[h][:].rearrange("p a c j -> p (a c) j")
-            scales = shared_scales[:, h, a0 * BANK : a1 * BANK]
-            quantize(codes, scales, flat[:, a0 * BANK : a1 * BANK, :])
-            for a in range(a0, a1):
-                multiply(a, E, E + h, codes, scales, (a - a0) * BANK)
-            if a1 == PASSES:
-                nc.scalar.copy(ds[h], banks[E + h][:])
+        half = BANK // 2
+
+        def finish_held(b0, b1, codes):
+            scales = held_scales[:, b0 * BANK : b1 * BANK]
+            quantize(codes, scales, held[:].rearrange("p b c j -> p (b c) j")[:, b0 * BANK : b1 * BANK, :])
+            for b in range(b0, b1):
+                a, e, bank = held_blocks[b]
+                multiply(a, e, bank, codes, scales, (b - b0) * BANK)
+                if e == E and a == PASSES - 1:
+                    for c0 in range(0, BANK, half):
+                        nc.scalar.copy(ds[bank - E][:, c0 : c0 + half], banks[bank][:, c0 : c0 + half])
 
         for a in range(PASSES):
             round_shared(a)
@@ -151,7 +154,6 @@ def tile_moe_bds_lin_none_kernel(tc, dyT, w_words, w_scales, gate, offs, pos1, p
         waiting = []
         staged = []
         r_in = 0
-        r_out = 0
         for u, (a, s0, s1) in enumerate(units):
             g = ring.tile([P, PACK, s1 - s0], F32, name="g", tag="g%d" % (u % 2), bufs=1, align_bytes=64)
             gather(g, a, s0, s1, HEAD if u == 0 else [], waiting)
@@ -163,35 +165,37 @@ def tile_moe_bds_lin_none_kernel(tc, dyT, w_words, w_scales, gate, offs, pos1, p
                 for j in range(PACK):
                     load_window(2, j)
             if u == 2:
-                dx = ring.tile([P, S], F32, name="dx", tag="window", bufs=PACK + 1)
+                dx = ring.tile([P, S], F32, name="dx", tag="window", bufs=PACK + 1, align_bytes=64)
             for piece in waiting[-1:]:
                 finish_routed(*piece)
             r1 = r_in + s1 - s0
             edges = [r_in] + [c for c in range(r_in + 1, r1) if c % QUANT == 0] + [r1]
+            if u == 1:
+                edges[-1] = S - C
             for e0, e1 in zip(edges[:-1], edges[1:]):
                 interleave(gb[:, e0:e1, :], g[:, :, e0 - r_in : e1 - r_in])
+            if u == 1:
+                interleave(held[:, 0, :, :], g[:, :, S - C : S])
             r_in = r1 % S
             for piece in waiting:
                 empty_banks(*piece)
             waiting = []
-            staged.extend([(a, e) for e in range(s0 // C, s1 // C)])
-            while len(staged) >= QUANT // C or (staged and u >= final - 1):
+            staged.extend([(a, e) for e in range(s0 // C, s1 // C) if (a, e) != (PASSES - 2, E - 1)])
+            while len(staged) >= QUANT // C or (staged and (u == 1 or u >= final - 1)):
                 blocks, staged = staged[: QUANT // C], staged[QUANT // C :]
-                waiting.append((blocks, r_out))
-                r_out = (r_out + len(blocks) * C) % S
+                waiting.append((blocks, blocks[0][1] * C))
         early_codes = ring.tile([P, 2 * BANK], U32, name="early_codes", tag="g%d" % ((final - 1) % 2), bufs=1, align_bytes=64)
-        late_codes = ring.tile([P, 4 * BANK], U32, name="late_codes", tag="g%d" % (final % 2), bufs=1, align_bytes=64)
-        shared_scales = ring.tile([P, T // BANK, PASSES * BANK], U8, name="shared_scales", tag="g_scales", bufs=1, align_bytes=64)
-        partial = ring.tile([P, 2, T], F32, name="partial", tag="window", bufs=PACK + 1)
-        further = ring.tile([P, 2, T], F32, name="further", tag="window", bufs=PACK + 1)
+        late_codes = ring.tile([P, 5 * BANK], U32, name="late_codes", tag="g%d" % (final % 2), bufs=1, align_bytes=64)
+        held_scales = ring.tile([P, len(held_blocks) * BANK], U8, name="held_scales", tag="window", bufs=PACK + 1, align_bytes=64)
+        partial = ring.tile([P, 2, T], F32, name="partial", tag="window", bufs=PACK + 1, align_bytes=64)
+        further = ring.tile([P, 2, T], F32, name="further", tag="window", bufs=PACK + 1, align_bytes=64)
         ds = [partial[:, 0, h * BANK : (h + 1) * BANK] for h in range(T // BANK)]
         sums = [partial[:, 1, :], further[:, 0, :], further[:, 1, :]]
-        finish_shared(0, 0, 2, early_codes[:])
+        finish_held(0, 2, early_codes[:])
         finish_routed(*waiting[0])
         empty_banks(*waiting[0])
-        finish_shared(0, 2, PASSES, late_codes[:, 0:BANK])
-        finish_shared(1, 0, 2, late_codes[:, BANK : 3 * BANK])
-        finish_shared(1, 2, PASSES, late_codes[:, 3 * BANK : 4 * BANK])
+        for b0, b1 in ((2, 3), (3, 4), (4, 6), (6, 7)):
+            finish_held(b0, b1, late_codes[:, (b0 - 2) * BANK : (b1 - 2) * BANK])
 
         def fetch(r, t0, t1):
             so_far = ds[t0 // BANK][:, t0 % BANK : t0 % BANK + t1 - t0] if r == 0 else sums[r - 1][:, t0:t1]
@@ -199,7 +203,6 @@ def tile_moe_bds_lin_none_kernel(tc, dyT, w_words, w_scales, gate, offs, pos1, p
             if r == 2:
                 nc.sync.dma_start(out[:, t0:t1], sums[r][:, t0:t1])
 
-        half = BANK // 2
         cut = T - LAST
         for r in range(2):
             fetch(r, 0, half)

@@ -62,7 +62,7 @@ def tile_moe_bds_lin_none_kernel(tc, dyT, w_words, w_scales, gate, offs, pos1, p
         def load_gate(c0, c1):
             nc.sync.dma_start(gate_sb[:, c0:c1], gate[0:P, c0:c1])
 
-        nc.gpsimd.memset(wscale[:].rearrange("p m k -> p (m k)").bitcast(I32), 0)
+        nc.vector.memset(wscale[:].rearrange("p m k -> p (m k)").bitcast(I32), 0)
         load_window(0, 0)
         nc.sync.dma_start(offs_sb[:], offs)
         for c0, c1 in zip([0] + HEAD, HEAD + [S]):

@@ -26,8 +26,8 @@ PAD = 16
 RUN = 4
 FIRST = 128
 LAST = 128
-UNIT = 3 * C
 QUANT = 2 * C
+STAGE = 4 * PACK * S
 HEAD = [FIRST, 3 * FIRST, 7 * FIRST, 15 * FIRST]
 
 
@@ -36,6 +36,7 @@ def tile_moe_bds_lin_none_kernel(tc, dyT, w_words, w_scales, gate, offs, pos1, p
     with ExitStack() as ctx:
         keep = ctx.enter_context(tc.tile_pool(name="keep", bufs=1))
         ring = ctx.enter_context(tc.tile_pool(name="ring", bufs=2))
+        stage = ctx.enter_context(tc.tile_pool(name="stage", bufs=1))
         psum = ctx.enter_context(tc.psum_pool(name="psum", bufs=1))
 
         offs_sb = keep.tile([P, S // 16], U16, name="offs_sb")
@@ -52,7 +53,7 @@ def tile_moe_bds_lin_none_kernel(tc, dyT, w_words, w_scales, gate, offs, pos1, p
             window[a, j] = ring.tile([P, S + PAD], F32, name="window", tag="window", bufs=PACK + 1, align_bytes=64)
             nc.sync.dma_start(window[a, j][:, 0:T], rows[a, :, j, :])
 
-        raw_early = ring.tile([P, PASSES - 1, PACK, T], F32, name="raw_early", tag="g1", bufs=1, align_bytes=64)
+        raw_early = stage.tile([P, PASSES - 1, PACK, T], F32, name="raw_early", offset=STAGE, align_bytes=64)
         raw_last = ring.tile([P, PACK, T], F32, name="raw_last", tag="gb", bufs=1, align_bytes=64)
         raw = [raw_early[:, a, :, :] for a in range(PASSES - 1)] + [raw_last[:]]
 
@@ -80,18 +81,15 @@ def tile_moe_bds_lin_none_kernel(tc, dyT, w_words, w_scales, gate, offs, pos1, p
             for tile, src in zip(pos_sb, (pos1, pos2, pos3)):
                 nc.sync.dma_start(tile[:], src)
 
-        def gather(g, a, s0, s1, cuts, waiting):
-            for j in range(PACK):
-                if 0 <= j - 1 - PACK + len(waiting):
-                    finish_routed(*waiting[j - 1 - PACK + len(waiting)])
-                edges = [s0] + (cuts if j == 0 else []) + [s1]
-                for c0, c1 in zip(edges[:-1], edges[1:]):
-                    nc.vector.tensor_tensor(
-                        g[:, j, c0 - s0 : c1 - s0],
-                        window[a, j][:].indirect(offs_sb[:, c0 // 16 : c1 // 16]),
-                        gate_sb[:, c0:c1],
-                        MULT,
-                    )
+        def gather(g, a, j, s0, s1, cuts=()):
+            edges = [s0] + list(cuts) + [s1]
+            for c0, c1 in zip(edges[:-1], edges[1:]):
+                nc.vector.tensor_tensor(
+                    g[:, j, c0 - s0 : c1 - s0],
+                    window[a, j][:].indirect(offs_sb[:, c0 // 16 : c1 // 16]),
+                    gate_sb[:, c0:c1],
+                    MULT,
+                )
 
         def interleave(dst, src):
             nc.scalar.copy(dst.rearrange("p (c i) j -> p c j i", i=RUN), src.rearrange("p j (c i) -> p c j i", i=RUN))
@@ -112,90 +110,105 @@ def tile_moe_bds_lin_none_kernel(tc, dyT, w_words, w_scales, gate, offs, pos1, p
             )
 
 
-        def finish_routed(blocks, r0):
-            width = len(blocks) * C
-            codes = ring.tile([P, width], U32, name="codes", tag="codes", bufs=2, align_bytes=64)
-            scales = ring.tile([P, width], U8, name="scales", tag="scales", bufs=2, align_bytes=64)
-            quantize(codes[:], scales[:], gb[:, r0 : r0 + width, :])
-            for i, (a, e) in enumerate(blocks):
-                multiply(a, e, e, codes, scales, i * C)
+        def finish(blocks, src, codes=None, scales=None):
+            width = len(blocks) * BANK
+            if codes is None:
+                codes = ring.tile([P, width], U32, name="codes", tag="codes", bufs=2, align_bytes=64)[:]
+                scales = ring.tile([P, width], U8, name="scales", tag="scales", bufs=2, align_bytes=64)[:]
+            quantize(codes, scales, src)
+            for i, (a, e, bank) in enumerate(blocks):
+                multiply(a, e, bank, codes, scales, i * BANK)
 
-        def empty_banks(blocks, r0):
-            for a, e in blocks:
-                if a == PASSES - 1:
-                    nc.scalar.copy(dx[:, e * C : (e + 1) * C], banks[e][:])
+        def finish_routed(a, e0, e1, src, codes=None, scales=None):
+            finish([(a, e, e) for e in range(e0, e1)], src[:, e0 * C : e1 * C, :], codes, scales)
 
-        held = keep.tile([P, 1 + PASSES * T // BANK, BANK, PACK], BF16, name="held", align_bytes=64)
-        held_blocks = [(PASSES - 2, E - 1, E - 1)] + [(a, E, E + h) for h in range(T // BANK) for a in range(PASSES)]
+        def empty_banks(e0, e1):
+            for e in range(e0, e1):
+                nc.scalar.copy(dx[:, e * C : (e + 1) * C], banks[e][:])
 
-        def round_shared(a):
-            for h in range(T // BANK):
-                interleave(held[:, 1 + h * PASSES + a, :, :], raw_piece(a, h))
-
+        shared_b = keep.tile([P, PASSES * T // BANK, BANK, PACK], BF16, name="shared_b", align_bytes=64)
         half = BANK // 2
 
-        def finish_held(b0, b1, codes):
-            scales = held_scales[:, b0 * BANK : b1 * BANK]
-            quantize(codes, scales, held[:].rearrange("p b c j -> p (b c) j")[:, b0 * BANK : b1 * BANK, :])
-            for b in range(b0, b1):
-                a, e, bank = held_blocks[b]
-                multiply(a, e, bank, codes, scales, (b - b0) * BANK)
-                if e == E and a == PASSES - 1:
-                    for c0 in range(0, BANK, half):
-                        nc.scalar.copy(ds[bank - E][:, c0 : c0 + half], banks[bank][:, c0 : c0 + half])
+        def finish_shared(b0, b1, codes, scales):
+            src = shared_b[:].rearrange("p b c j -> p (b c) j")[:, b0 * BANK : b1 * BANK, :]
+            finish([(b % PASSES, E, E + b // PASSES) for b in range(b0, b1)], src, codes, scales)
+            if b1 % PASSES == 0:
+                h = b0 // PASSES
+                for c0 in range(0, BANK, half):
+                    nc.scalar.copy(ds[h][:, c0 : c0 + half], banks[E + h][:, c0 : c0 + half])
 
         for a in range(PASSES):
-            round_shared(a)
+            for h in range(T // BANK):
+                interleave(shared_b[:, h * PASSES + a, :, :], raw_piece(a, h))
         gb = ring.tile([P, S, PACK], BF16, name="gb", tag="gb", bufs=1, align_bytes=64)
 
-        units = [(0, 0, S), (1, 0, S), (2, 0, UNIT), (2, UNIT, S - C), (2, S - C, S)]
-        final = len(units) - 1
+        def interleave_pieces(dst, g, s0, s1, step):
+            for c0 in range(s0, s1, step):
+                interleave(dst[:, c0 : c0 + step, :], g[:, :, c0 - s0 : c0 - s0 + step])
 
-        waiting = []
-        staged = []
-        r_in = 0
-        for u, (a, s0, s1) in enumerate(units):
-            g = ring.tile([P, PACK, s1 - s0], F32, name="g", tag="g%d" % (u % 2), bufs=1, align_bytes=64)
-            gather(g, a, s0, s1, HEAD if u == 0 else [], waiting)
-            if u == 0:
-                for j in range(1, PACK):
-                    load_window(1, j)
-                load_weights()
-            if u == 1:
-                for j in range(PACK):
-                    load_window(2, j)
-            if u == 2:
-                dx = ring.tile([P, S], F32, name="dx", tag="window", bufs=PACK + 1, align_bytes=64)
-            for piece in waiting[-1:]:
-                finish_routed(*piece)
-            r1 = r_in + s1 - s0
-            edges = [r_in] + [c for c in range(r_in + 1, r1) if c % QUANT == 0] + [r1]
-            if u == 1:
-                edges[-1] = S - C
-            for e0, e1 in zip(edges[:-1], edges[1:]):
-                interleave(gb[:, e0:e1, :], g[:, :, e0 - r_in : e1 - r_in])
-            if u == 1:
-                interleave(held[:, 0, :, :], g[:, :, S - C : S])
-            r_in = r1 % S
-            for piece in waiting:
-                empty_banks(*piece)
-            waiting = []
-            staged.extend([(a, e) for e in range(s0 // C, s1 // C) if (a, e) != (PASSES - 2, E - 1)])
-            while len(staged) >= QUANT // C or (staged and (u == 1 or u >= final - 1)):
-                blocks, staged = staged[: QUANT // C], staged[QUANT // C :]
-                waiting.append((blocks, blocks[0][1] * C))
-        early_codes = ring.tile([P, 2 * BANK], U32, name="early_codes", tag="g%d" % ((final - 1) % 2), bufs=1, align_bytes=64)
-        late_codes = ring.tile([P, 5 * BANK], U32, name="late_codes", tag="g%d" % (final % 2), bufs=1, align_bytes=64)
-        held_scales = ring.tile([P, len(held_blocks) * BANK], U8, name="held_scales", tag="window", bufs=PACK + 1, align_bytes=64)
+        g = stage.tile([P, PACK, S], F32, name="g_first", offset=0, align_bytes=64)
+        for j in range(PACK):
+            gather(g, 0, j, 0, S, HEAD if j == 0 else ())
+        for j in range(1, PACK):
+            load_window(1, j)
+        load_weights()
+        interleave_pieces(gb, g, 0, S, QUANT)
+
+        g = stage.tile([P, PACK, S], F32, name="g_second", offset=STAGE, align_bytes=64)
+        for j in range(PACK):
+            gather(g, 1, j, 0, S)
+            if j > 0:
+                finish_routed(0, 2 * j - 2, 2 * j, gb)
+        for j in range(PACK):
+            load_window(2, j)
+        interleave_pieces(gb, g, 0, S, QUANT)
+
+        split = 2 * QUANT
+        g = stage.tile([P, PACK, split], F32, name="g_third", offset=0, align_bytes=64)
+        for j in range(PACK):
+            gather(g, 2, j, 0, split)
+            if j == 1:
+                finish_routed(1, 0, 2, gb)
+        dx = ring.tile([P, S], F32, name="dx", tag="window", bufs=PACK + 1, align_bytes=64)
+        g_last = stage.tile([P, PACK, S - split], F32, name="g_last", offset=STAGE, align_bytes=64)
+        gb_last = stage.tile([P, S, PACK], BF16, name="gb_last", offset=STAGE + 4 * PACK * (S - split), align_bytes=64)
+        interleave_pieces(gb_last, g, 0, split, QUANT)
+
+        for j in range(PACK):
+            gather(g_last, 2, j, split, S)
+        tail_scales = ring.tile([P, 16 * BANK], U8, name="tail_scales", tag="window", bufs=PACK + 1, align_bytes=64)
+        last_codes = stage.tile([P, S], U32, name="last_codes", offset=4 * PACK * split, align_bytes=64)
+
+        def finish_last(e):
+            finish_routed(2, e, e + 1, gb_last, last_codes[:, e * C : (e + 1) * C], tail_scales[:, e * C : (e + 1) * C])
+
+        finish_last(0)
+        finish_last(1)
+        interleave_pieces(gb_last, g_last, split, S, C)
+        empty_banks(0, 2)
+
         partial = ring.tile([P, 2, T], F32, name="partial", tag="window", bufs=PACK + 1, align_bytes=64)
         further = ring.tile([P, 2, T], F32, name="further", tag="window", bufs=PACK + 1, align_bytes=64)
+        held_codes = ring.tile([P, 4 * BANK], U32, name="held_codes", tag="window", bufs=PACK + 1, align_bytes=64)
+        early_codes = stage.tile([P, 2 * BANK], U32, name="early_codes", offset=0, align_bytes=64)
+        late_codes = stage.tile([P, 4 * BANK], U32, name="late_codes", offset=STAGE, align_bytes=64)
         ds = [partial[:, 0, h * BANK : (h + 1) * BANK] for h in range(T // BANK)]
         sums = [partial[:, 1, :], further[:, 0, :], further[:, 1, :]]
-        finish_held(0, 2, early_codes[:])
-        finish_routed(*waiting[0])
-        empty_banks(*waiting[0])
-        for b0, b1 in ((2, 3), (3, 4), (4, 6), (6, 7)):
-            finish_held(b0, b1, late_codes[:, (b0 - 2) * BANK : (b1 - 2) * BANK])
+        held_scales = tail_scales[:, S : S + 4 * C]
+        shared_scales = tail_scales[:, S + 4 * C :]
+        for e in range(2, E):
+            cols = slice((e - 2) * C, (e - 1) * C)
+            finish_routed(1, e, e + 1, gb, held_codes[:, cols], held_scales[:, cols])
+        for e in range(2, 4):
+            finish_last(e)
+        empty_banks(2, 4)
+        for b in range(2):
+            finish_shared(b, b + 1, early_codes[:, b * BANK : (b + 1) * BANK], shared_scales[:, b * BANK : (b + 1) * BANK])
+        for e in range(4, E):
+            finish_last(e)
+            empty_banks(e, e + 1)
+        for b in range(2, 6):
+            finish_shared(b, b + 1, late_codes[:, (b - 2) * BANK : (b - 1) * BANK], shared_scales[:, b * BANK : (b + 1) * BANK])
 
         def fetch(r, t0, t1):
             so_far = ds[t0 // BANK][:, t0 % BANK : t0 % BANK + t1 - t0] if r == 0 else sums[r - 1][:, t0:t1]

@@ -22,13 +22,18 @@ P = 128
 PACK = 4
 PASSES = N // (P * PACK)
 BANK = 512
+HALVES = T // BANK
+GROUP = 16
 PAD = 16
+SLOTS = PACK + 1
 RUN = 4
-FIRST = 128
-LAST = 128
-QUANT = 2 * C
+PAIR = 2 * C
 STAGE = 4 * PACK * S
+FIRST = 128
 HEAD = [FIRST, 3 * FIRST, 7 * FIRST, 15 * FIRST]
+SPLIT = 2 * PAIR
+EARLY = 2
+LAST = 128
 
 
 def tile_moe_bds_lin_none_kernel(tc, dyT, w_words, w_scales, gate, offs, pos1, pos2, pos3, out):
@@ -39,41 +44,42 @@ def tile_moe_bds_lin_none_kernel(tc, dyT, w_words, w_scales, gate, offs, pos1, p
         stage = ctx.enter_context(tc.tile_pool(name="stage", bufs=1))
         psum = ctx.enter_context(tc.psum_pool(name="psum", bufs=1))
 
-        offs_sb = keep.tile([P, S // 16], U16, name="offs_sb")
-        pos_sb = [keep.tile([P, T // 16], U16, name="pos_sb%d" % r) for r in range(3)]
+        def window_slot(shape, dtype, name):
+            return ring.tile(shape, dtype, name=name, tag="window", bufs=SLOTS, align_bytes=64)
+
+        def staged(shape, dtype, name, offset):
+            return stage.tile(shape, dtype, name=name, offset=offset, align_bytes=64)
+
+        offs_sb = keep.tile([P, S // GROUP], U16, name="offs_sb")
+        pos_sb = [keep.tile([P, T // GROUP], U16, name="pos_sb%d" % r) for r in range(3)]
         gate_sb = keep.tile([P, S], F32, name="gate_sb")
-        window = {}
         words = keep.tile([P, (E + 1) * PASSES, 2 * K], U8, name="words", align_bytes=64)
         wscale = keep.tile([P, (E + 1) * PASSES, K], U8, name="wscale", align_bytes=64)
-        banks = [psum.tile([P, BANK], F32, name="bank%d" % b) for b in range(E + T // BANK)]
+        banks = [psum.tile([P, BANK], F32, name="bank%d" % b) for b in range(E + HALVES)]
 
         rows = dyT.rearrange("(a p j) t -> a p j t", p=P, j=PACK)
+        window = {}
 
         def load_window(a, j):
-            window[a, j] = ring.tile([P, S + PAD], F32, name="window", tag="window", bufs=PACK + 1, align_bytes=64)
+            window[a, j] = window_slot([P, S + PAD], F32, "window")
             nc.sync.dma_start(window[a, j][:, 0:T], rows[a, :, j, :])
 
-        raw_early = stage.tile([P, PASSES - 1, PACK, T], F32, name="raw_early", offset=STAGE, align_bytes=64)
+        raw_early = staged([P, PASSES - 1, PACK, T], F32, "raw_early", STAGE)
         raw_last = ring.tile([P, PACK, T], F32, name="raw_last", tag="gb", bufs=1, align_bytes=64)
         raw = [raw_early[:, a, :, :] for a in range(PASSES - 1)] + [raw_last[:]]
 
-        def raw_piece(a, h):
-            return raw[a][:, :, h * BANK : (h + 1) * BANK]
-
-        def load_gate(c0, c1):
-            nc.sync.dma_start(gate_sb[:, c0:c1], gate[0:P, c0:c1])
-
         nc.vector.memset(wscale[:].rearrange("p m k -> p (m k)").bitcast(I32), 0)
+
         load_window(0, 0)
         nc.sync.dma_start(offs_sb[:], offs)
         for c0, c1 in zip([0] + HEAD, HEAD + [S]):
-            load_gate(c0, c1)
+            nc.sync.dma_start(gate_sb[:, c0:c1], gate[0:P, c0:c1])
         for j in range(1, PACK):
             load_window(0, j)
             nc.sync.dma_start(raw[j - 1], rows[j - 1])
         load_window(1, 0)
 
-        def load_weights():
+        def load_weights_and_lists():
             nc.sync.dma_start(words[:].bitcast(I32), w_words.rearrange("e a p b -> p (e a) b").bitcast(I32))
             scale_rows = w_scales.rearrange("e a f k -> f (e a) k")
             for q in range(4):
@@ -81,12 +87,12 @@ def tile_moe_bds_lin_none_kernel(tc, dyT, w_words, w_scales, gate, offs, pos1, p
             for tile, src in zip(pos_sb, (pos1, pos2, pos3)):
                 nc.sync.dma_start(tile[:], src)
 
-        def gather(g, a, j, s0, s1, cuts=()):
+        def gather(dst, a, j, s0, s1, cuts=()):
             edges = [s0] + list(cuts) + [s1]
             for c0, c1 in zip(edges[:-1], edges[1:]):
                 nc.vector.tensor_tensor(
-                    g[:, j, c0 - s0 : c1 - s0],
-                    window[a, j][:].indirect(offs_sb[:, c0 // 16 : c1 // 16]),
+                    dst[:, j, c0 - s0 : c1 - s0],
+                    window[a, j][:].indirect(offs_sb[:, c0 // GROUP : c1 // GROUP]),
                     gate_sb[:, c0:c1],
                     MULT,
                 )
@@ -94,134 +100,117 @@ def tile_moe_bds_lin_none_kernel(tc, dyT, w_words, w_scales, gate, offs, pos1, p
         def interleave(dst, src):
             nc.scalar.copy(dst.rearrange("p (c i) j -> p c j i", i=RUN), src.rearrange("p j (c i) -> p c j i", i=RUN))
 
-        def quantize(codes, scales, src):
+        def interleave_slots(dst, src, s0, s1, step):
+            for c0 in range(s0, s1, step):
+                interleave(dst[:, c0 : c0 + step, :], src[:, :, c0 - s0 : c0 - s0 + step])
+
+        def finish(pieces, src, codes, scales):
             nc.vector.quantize_mx(out=codes.bitcast(E5M2X4), scales=scales, in_=src.rearrange("p c j -> p (c j)"))
+            for i, (a, e, bank) in enumerate(pieces):
+                cols = slice(i * BANK, (i + 1) * BANK)
+                nc.tensor.matmul_mx(
+                    out=banks[bank][:],
+                    lhsT=words[:, e * PASSES + a, :].bitcast(E2M1X4),
+                    lhsT_scale=wscale[:, e * PASSES + a, :],
+                    rhs=codes[:, cols].bitcast(E5M2X4),
+                    rhs_scale=scales[:, cols],
+                    start=(a == 0),
+                    stop=(a == PASSES - 1),
+                )
 
-        def multiply(a, e, bank, codes, scales, c0):
-            m = e * PASSES + a
-            nc.tensor.matmul_mx(
-                out=banks[bank][:],
-                lhsT=words[:, m, :].bitcast(E2M1X4),
-                lhsT_scale=wscale[:, m, :],
-                rhs=codes[:, c0 : c0 + BANK].bitcast(E5M2X4),
-                rhs_scale=scales[:, c0 : c0 + BANK],
-                start=(a == 0),
-                stop=(a == PASSES - 1),
-            )
+        def finish_pair(e):
+            codes = ring.tile([P, PAIR], U32, name="codes", tag="codes", bufs=2, align_bytes=64)
+            scales = ring.tile([P, PAIR], U8, name="scales", tag="scales", bufs=2, align_bytes=64)
+            finish([(0, e, e), (0, e + 1, e + 1)], gb[:, e * C : e * C + PAIR, :], codes[:], scales[:])
 
-
-        def finish(blocks, src, codes=None, scales=None):
-            width = len(blocks) * BANK
-            if codes is None:
-                codes = ring.tile([P, width], U32, name="codes", tag="codes", bufs=2, align_bytes=64)[:]
-                scales = ring.tile([P, width], U8, name="scales", tag="scales", bufs=2, align_bytes=64)[:]
-            quantize(codes, scales, src)
-            for i, (a, e, bank) in enumerate(blocks):
-                multiply(a, e, bank, codes, scales, i * BANK)
-
-        def finish_routed(a, e0, e1, src, codes=None, scales=None):
-            finish([(a, e, e) for e in range(e0, e1)], src[:, e0 * C : e1 * C, :], codes, scales)
-
-        def empty_banks(e0, e1):
-            for e in range(e0, e1):
-                nc.scalar.copy(dx[:, e * C : (e + 1) * C], banks[e][:])
-
-        shared_b = keep.tile([P, PASSES * T // BANK, BANK, PACK], BF16, name="shared_b", align_bytes=64)
-        half = BANK // 2
-
-        def finish_shared(b0, b1, codes, scales):
-            src = shared_b[:].rearrange("p b c j -> p (b c) j")[:, b0 * BANK : b1 * BANK, :]
-            finish([(b % PASSES, E, E + b // PASSES) for b in range(b0, b1)], src, codes, scales)
-            if b1 % PASSES == 0:
-                h = b0 // PASSES
-                for c0 in range(0, BANK, half):
-                    nc.scalar.copy(ds[h][:, c0 : c0 + half], banks[E + h][:, c0 : c0 + half])
-
+        shared_b = keep.tile([P, HALVES * PASSES, BANK, PACK], BF16, name="shared_b", align_bytes=64)
         for a in range(PASSES):
-            for h in range(T // BANK):
-                interleave(shared_b[:, h * PASSES + a, :, :], raw_piece(a, h))
+            for h in range(HALVES):
+                interleave(shared_b[:, h * PASSES + a, :, :], raw[a][:, :, h * BANK : (h + 1) * BANK])
         gb = ring.tile([P, S, PACK], BF16, name="gb", tag="gb", bufs=1, align_bytes=64)
 
-        def interleave_pieces(dst, g, s0, s1, step):
-            for c0 in range(s0, s1, step):
-                interleave(dst[:, c0 : c0 + step, :], g[:, :, c0 - s0 : c0 - s0 + step])
-
-        g = stage.tile([P, PACK, S], F32, name="g_first", offset=0, align_bytes=64)
+        g_first = staged([P, PACK, S], F32, "g_first", 0)
         for j in range(PACK):
-            gather(g, 0, j, 0, S, HEAD if j == 0 else ())
+            gather(g_first, 0, j, 0, S, HEAD if j == 0 else ())
         for j in range(1, PACK):
             load_window(1, j)
-        load_weights()
-        interleave_pieces(gb, g, 0, S, QUANT)
+        load_weights_and_lists()
+        interleave_slots(gb, g_first, 0, S, PAIR)
 
-        g = stage.tile([P, PACK, S], F32, name="g_second", offset=STAGE, align_bytes=64)
+        g_second = staged([P, PACK, S], F32, "g_second", STAGE)
         for j in range(PACK):
-            gather(g, 1, j, 0, S)
+            gather(g_second, 1, j, 0, S)
             if j > 0:
-                finish_routed(0, 2 * j - 2, 2 * j, gb)
+                finish_pair(2 * (j - 1))
         for j in range(PACK):
             load_window(2, j)
-        interleave_pieces(gb, g, 0, S, QUANT)
+        interleave_slots(gb, g_second, 0, S, PAIR)
 
-        split = 2 * QUANT
-        g = stage.tile([P, PACK, split], F32, name="g_third", offset=0, align_bytes=64)
+        g_third = staged([P, PACK, SPLIT], F32, "g_third", 0)
         for j in range(PACK):
-            gather(g, 2, j, 0, split)
-            if j == 1:
-                finish_routed(1, 0, 2, gb)
-        dx = ring.tile([P, S], F32, name="dx", tag="window", bufs=PACK + 1, align_bytes=64)
-        g_last = stage.tile([P, PACK, S - split], F32, name="g_last", offset=STAGE, align_bytes=64)
-        gb_last = stage.tile([P, S, PACK], BF16, name="gb_last", offset=STAGE + 4 * PACK * (S - split), align_bytes=64)
-        interleave_pieces(gb_last, g, 0, split, QUANT)
+            gather(g_third, 2, j, 0, SPLIT)
+        dx = window_slot([P, S], F32, "dx")
+        g_last = staged([P, PACK, S - SPLIT], F32, "g_last", STAGE)
+        gb_last = staged([P, S, PACK], BF16, "gb_last", STAGE + 4 * PACK * (S - SPLIT))
+        interleave_slots(gb_last, g_third, 0, SPLIT, PAIR)
 
         for j in range(PACK):
-            gather(g_last, 2, j, split, S)
-        tail_scales = ring.tile([P, 16 * BANK], U8, name="tail_scales", tag="window", bufs=PACK + 1, align_bytes=64)
-        last_codes = stage.tile([P, S], U32, name="last_codes", offset=4 * PACK * split, align_bytes=64)
+            gather(g_last, 2, j, SPLIT, S)
+
+        interleave_slots(gb_last, g_last, SPLIT, S, C)
+
+        tail_scales = window_slot([P, 2 * S + HALVES * PASSES * BANK], U8, "tail_scales")
+        partial = window_slot([P, 2, T], F32, "partial")
+        further = window_slot([P, 2, T], F32, "further")
+        held_codes = window_slot([P, S], U32, "held_codes")
+        last_codes = staged([P, S], U32, "last_codes", 4 * PACK * SPLIT)
+        early_codes = staged([P, EARLY * BANK], U32, "early_codes", 0)
+        late_codes = staged([P, (HALVES * PASSES - EARLY) * BANK], U32, "late_codes", STAGE)
+        held_scales, last_scales, shared_scales = tail_scales[:, 0:S], tail_scales[:, S : 2 * S], tail_scales[:, 2 * S :]
+
+        def finish_held(e):
+            cols = slice(e * C, (e + 1) * C)
+            finish([(PASSES - 2, e, e)], gb[:, cols, :], held_codes[:, cols], held_scales[:, cols])
 
         def finish_last(e):
-            finish_routed(2, e, e + 1, gb_last, last_codes[:, e * C : (e + 1) * C], tail_scales[:, e * C : (e + 1) * C])
+            cols = slice(e * C, (e + 1) * C)
+            finish([(PASSES - 1, e, e)], gb_last[:, cols, :], last_codes[:, cols], last_scales[:, cols])
+            nc.scalar.copy(dx[:, cols], banks[e][:])
 
-        finish_last(0)
-        finish_last(1)
-        interleave_pieces(gb_last, g_last, split, S, C)
-        empty_banks(0, 2)
+        ds = partial[:, 0, :]
+        quarter = T // 4
 
-        partial = ring.tile([P, 2, T], F32, name="partial", tag="window", bufs=PACK + 1, align_bytes=64)
-        further = ring.tile([P, 2, T], F32, name="further", tag="window", bufs=PACK + 1, align_bytes=64)
-        held_codes = ring.tile([P, 4 * BANK], U32, name="held_codes", tag="window", bufs=PACK + 1, align_bytes=64)
-        early_codes = stage.tile([P, 2 * BANK], U32, name="early_codes", offset=0, align_bytes=64)
-        late_codes = stage.tile([P, 4 * BANK], U32, name="late_codes", offset=STAGE, align_bytes=64)
-        ds = [partial[:, 0, h * BANK : (h + 1) * BANK] for h in range(T // BANK)]
+        def finish_shared(b, codes):
+            h, a = divmod(b, PASSES)
+            finish([(a, E, E + h)], shared_b[:, b, :, :], codes, shared_scales[:, b * BANK : (b + 1) * BANK])
+            if a == PASSES - 1:
+                for c0 in range(0, BANK, quarter):
+                    nc.scalar.copy(ds[:, h * BANK + c0 : h * BANK + c0 + quarter], banks[E + h][:, c0 : c0 + quarter])
+
+        for e in range(E):
+            finish_held(e)
+            if e < SPLIT // C:
+                finish_last(e)
+        for b in range(EARLY):
+            finish_shared(b, early_codes[:, b * BANK : (b + 1) * BANK])
+        for e in range(SPLIT // C, E):
+            finish_last(e)
+        for b in range(EARLY, HALVES * PASSES):
+            finish_shared(b, late_codes[:, (b - EARLY) * BANK : (b - EARLY + 1) * BANK])
+
         sums = [partial[:, 1, :], further[:, 0, :], further[:, 1, :]]
-        held_scales = tail_scales[:, S : S + 4 * C]
-        shared_scales = tail_scales[:, S + 4 * C :]
-        for e in range(2, E):
-            cols = slice((e - 2) * C, (e - 1) * C)
-            finish_routed(1, e, e + 1, gb, held_codes[:, cols], held_scales[:, cols])
-        for e in range(2, 4):
-            finish_last(e)
-        empty_banks(2, 4)
-        for b in range(2):
-            finish_shared(b, b + 1, early_codes[:, b * BANK : (b + 1) * BANK], shared_scales[:, b * BANK : (b + 1) * BANK])
-        for e in range(4, E):
-            finish_last(e)
-            empty_banks(e, e + 1)
-        for b in range(2, 6):
-            finish_shared(b, b + 1, late_codes[:, (b - 2) * BANK : (b - 1) * BANK], shared_scales[:, b * BANK : (b + 1) * BANK])
 
         def fetch(r, t0, t1):
-            so_far = ds[t0 // BANK][:, t0 % BANK : t0 % BANK + t1 - t0] if r == 0 else sums[r - 1][:, t0:t1]
-            nc.vector.tensor_tensor(sums[r][:, t0:t1], dx[:].indirect(pos_sb[r][:, t0 // 16 : t1 // 16]), so_far, ADD)
+            so_far = ds if r == 0 else sums[r - 1]
+            nc.vector.tensor_tensor(sums[r][:, t0:t1], dx[:].indirect(pos_sb[r][:, t0 // GROUP : t1 // GROUP]), so_far[:, t0:t1], ADD)
             if r == 2:
                 nc.sync.dma_start(out[:, t0:t1], sums[r][:, t0:t1])
 
-        cut = T - LAST
         for r in range(2):
-            fetch(r, 0, half)
-            fetch(r, half, BANK)
+            fetch(r, 0, quarter)
+            fetch(r, quarter, BANK)
         fetch(0, BANK, T)
         fetch(2, 0, BANK)
         for r in range(1, 3):
-            fetch(r, BANK, cut)
-            fetch(r, cut, T)
+            fetch(r, BANK, T - LAST)
+            fetch(r, T - LAST, T)

@@ -24,16 +24,11 @@ PASSES = N // (P * PACK)
 BANK = 512
 HALVES = T // BANK
 GROUP = 16
-PAD = 16
-SLOTS = PACK + 1
+
+PAD_W = 16
+WIN = T + PAD_W
 RUN = 4
-PAIR = 2 * C
-STAGE = 4 * PACK * S
-FIRST = 128
-HEAD = [FIRST, 3 * FIRST, 7 * FIRST, 15 * FIRST]
-SPLIT = 2 * PAIR
-EARLY = 2
-LAST = 128
+COPY = mybir.ActivationFunctionType.Copy
 
 
 def tile_moe_bds_lin_none_kernel(tc, dyT, w_words, w_scales, gate, offs, pos1, pos2, pos3, out):
@@ -41,14 +36,7 @@ def tile_moe_bds_lin_none_kernel(tc, dyT, w_words, w_scales, gate, offs, pos1, p
     with ExitStack() as ctx:
         keep = ctx.enter_context(tc.tile_pool(name="keep", bufs=1))
         ring = ctx.enter_context(tc.tile_pool(name="ring", bufs=2))
-        stage = ctx.enter_context(tc.tile_pool(name="stage", bufs=1))
         psum = ctx.enter_context(tc.psum_pool(name="psum", bufs=1))
-
-        def window_slot(shape, dtype, name):
-            return ring.tile(shape, dtype, name=name, tag="window", bufs=SLOTS, align_bytes=64)
-
-        def staged(shape, dtype, name, offset):
-            return stage.tile(shape, dtype, name=name, offset=offset, align_bytes=64)
 
         offs_sb = keep.tile([P, S // GROUP], U16, name="offs_sb")
         pos_sb = [keep.tile([P, T // GROUP], U16, name="pos_sb%d" % r) for r in range(3)]
@@ -56,161 +44,180 @@ def tile_moe_bds_lin_none_kernel(tc, dyT, w_words, w_scales, gate, offs, pos1, p
         words = keep.tile([P, (E + 1) * PASSES, 2 * K], U8, name="words", align_bytes=64)
         wscale = keep.tile([P, (E + 1) * PASSES, K], U8, name="wscale", align_bytes=64)
         banks = [psum.tile([P, BANK], F32, name="bank%d" % b) for b in range(E + HALVES)]
+        window = {(a, j): keep.tile([P, WIN], F32, name="window%d_%d" % (a, j)) for a in range(PASSES) for j in range(PACK)}
+        dx = keep.tile([P, S], F32, name="dx")
+        ds = keep.tile([P, T], F32, name="ds")
 
         rows = dyT.rearrange("(a p j) t -> a p j t", p=P, j=PACK)
-        window = {}
 
         def load_window(a, j):
-            window[a, j] = window_slot([P, S + PAD], F32, "window")
             nc.sync.dma_start(window[a, j][:, 0:T], rows[a, :, j, :])
 
-        raw_early = staged([P, PASSES - 1, PACK, T], F32, "raw_early", STAGE)
-        raw_last = ring.tile([P, PACK, T], F32, name="raw_last", tag="gb", bufs=1, align_bytes=64)
-        raw = [raw_early[:, a, :, :] for a in range(PASSES - 1)] + [raw_last[:]]
+        def load_gate(e0, e1):
+            nc.sync.dma_start(gate_sb[:, e0 * C : e1 * C], gate[0:P, e0 * C : e1 * C])
+
+        raw = {}
+
+        def load_raw(b):
+            h, a = divmod(b, PASSES)
+            raw[b] = ring.tile([P, PACK, BANK], F32, name="raw", tag="raw", bufs=3)
+            nc.sync.dma_start(raw[b][:], rows[a, :, :, h * BANK : (h + 1) * BANK])
 
         nc.vector.memset(wscale[:].rearrange("p m k -> p (m k)").bitcast(I32), 0)
 
-        load_window(0, 0)
-        nc.sync.dma_start(offs_sb[:], offs)
-        for c0, c1 in zip([0] + HEAD, HEAD + [S]):
-            nc.sync.dma_start(gate_sb[:, c0:c1], gate[0:P, c0:c1])
-        for j in range(1, PACK):
-            load_window(0, j)
-            nc.sync.dma_start(raw[j - 1], rows[j - 1])
-        load_window(1, 0)
-
-        def load_weights_and_lists():
+        def load_weights():
             nc.sync.dma_start(words[:].bitcast(I32), w_words.rearrange("e a p b -> p (e a) b").bitcast(I32))
             scale_rows = w_scales.rearrange("e a f k -> f (e a) k")
             for q in range(4):
                 nc.sync.dma_start(wscale[32 * q : 32 * q + 4, :, :].bitcast(I32), scale_rows[4 * q : 4 * q + 4, :, :].bitcast(I32))
-            for tile, src in zip(pos_sb, (pos1, pos2, pos3)):
-                nc.sync.dma_start(tile[:], src)
 
-        def gather(dst, a, j, s0, s1, cuts=()):
-            edges = [s0] + list(cuts) + [s1]
-            for c0, c1 in zip(edges[:-1], edges[1:]):
-                nc.vector.tensor_tensor(
-                    dst[:, j, c0 - s0 : c1 - s0],
-                    window[a, j][:].indirect(offs_sb[:, c0 // GROUP : c1 // GROUP]),
-                    gate_sb[:, c0:c1],
-                    MULT,
-                )
-
-        def interleave(dst, src):
-            nc.scalar.copy(dst.rearrange("p (c i) j -> p c j i", i=RUN), src.rearrange("p j (c i) -> p c j i", i=RUN))
-
-        def interleave_slots(dst, src, s0, s1, step):
-            for c0 in range(s0, s1, step):
-                interleave(dst[:, c0 : c0 + step, :], src[:, :, c0 - s0 : c0 - s0 + step])
-
-        def finish(pieces, src, codes, scales):
-            nc.vector.quantize_mx(out=codes.bitcast(E5M2X4), scales=scales, in_=src.rearrange("p c j -> p (c j)"))
-            for i, (a, e, bank) in enumerate(pieces):
-                cols = slice(i * BANK, (i + 1) * BANK)
-                nc.tensor.matmul_mx(
-                    out=banks[bank][:],
-                    lhsT=words[:, e * PASSES + a, :].bitcast(E2M1X4),
-                    lhsT_scale=wscale[:, e * PASSES + a, :],
-                    rhs=codes[:, cols].bitcast(E5M2X4),
-                    rhs_scale=scales[:, cols],
-                    start=(a == 0),
-                    stop=(a == PASSES - 1),
-                )
-
-        def finish_pair(e):
-            codes = ring.tile([P, PAIR], U32, name="codes", tag="codes", bufs=2, align_bytes=64)
-            scales = ring.tile([P, PAIR], U8, name="scales", tag="scales", bufs=2, align_bytes=64)
-            finish([(0, e, e), (0, e + 1, e + 1)], gb[:, e * C : e * C + PAIR, :], codes[:], scales[:])
-
-        shared_b = keep.tile([P, HALVES * PASSES, BANK, PACK], BF16, name="shared_b", align_bytes=64)
-        for a in range(PASSES):
-            for h in range(HALVES):
-                interleave(shared_b[:, h * PASSES + a, :, :], raw[a][:, :, h * BANK : (h + 1) * BANK])
-        gb = ring.tile([P, S, PACK], BF16, name="gb", tag="gb", bufs=1, align_bytes=64)
-
-        g_first = staged([P, PACK, S], F32, "g_first", 0)
-        for j in range(PACK):
-            gather(g_first, 0, j, 0, S, HEAD if j == 0 else ())
+        load_window(0, 0)
+        nc.sync.dma_start(offs_sb[:], offs)
+        load_gate(0, 1)
         for j in range(1, PACK):
-            load_window(1, j)
-        load_weights_and_lists()
-        interleave_slots(gb, g_first, 0, S, PAIR)
-
-        g_second = staged([P, PACK, S], F32, "g_second", STAGE)
+            load_window(0, j)
+        load_raw(0)
+        load_gate(1, 3)
+        load_weights()
+        load_raw(1)
         for j in range(PACK):
-            gather(g_second, 1, j, 0, S)
-            if j > 0:
-                finish_pair(2 * (j - 1))
+            load_window(1, j)
+        load_gate(3, E)
+        load_raw(2)
         for j in range(PACK):
             load_window(2, j)
-        interleave_slots(gb, g_second, 0, S, PAIR)
+        for tile, src in zip(pos_sb, (pos1, pos2, pos3)):
+            nc.sync.dma_start(tile[:], src)
 
-        g_third = staged([P, PACK, SPLIT], F32, "g_third", 0)
-        for j in range(PACK):
-            gather(g_third, 2, j, 0, SPLIT)
-        dx = window_slot([P, S], F32, "dx")
-        g_last = staged([P, PACK, S - SPLIT], F32, "g_last", STAGE)
-        gb_last = staged([P, S, PACK], BF16, "gb_last", STAGE + 4 * PACK * (S - SPLIT))
-        interleave_slots(gb_last, g_third, 0, SPLIT, PAIR)
+        def offsets(s0, s1):
+            return offs_sb[:, s0 // GROUP : s1 // GROUP]
 
-        for j in range(PACK):
-            gather(g_last, 2, j, SPLIT, S)
+        def by_runs(ap):
+            return ap.rearrange("p j (c i) -> p c j i", i=RUN)
 
-        interleave_slots(gb_last, g_last, SPLIT, S, C)
+        def rounded_tile():
+            return ring.tile([P, BANK, PACK], BF16, name="rounded", tag="rounded", bufs=4, align_bytes=64)
 
-        tail_scales = window_slot([P, 2 * S + HALVES * PASSES * BANK], U8, "tail_scales")
-        partial = window_slot([P, 2, T], F32, "partial")
-        further = window_slot([P, 2, T], F32, "further")
-        held_codes = window_slot([P, S], U32, "held_codes")
-        last_codes = staged([P, S], U32, "last_codes", 4 * PACK * SPLIT)
-        early_codes = staged([P, EARLY * BANK], U32, "early_codes", 0)
-        late_codes = staged([P, (HALVES * PASSES - EARLY) * BANK], U32, "late_codes", STAGE)
-        held_scales, last_scales, shared_scales = tail_scales[:, 0:S], tail_scales[:, S : 2 * S], tail_scales[:, 2 * S :]
+        def words_view(tile):
+            return tile[:].rearrange("p (c i) j -> p c j i", i=RUN)
 
-        def finish_held(e):
-            cols = slice(e * C, (e + 1) * C)
-            finish([(PASSES - 2, e, e)], gb[:, cols, :], held_codes[:, cols], held_scales[:, cols])
+        staged = {}
 
-        def finish_last(e):
-            cols = slice(e * C, (e + 1) * C)
-            finish([(PASSES - 1, e, e)], gb_last[:, cols, :], last_codes[:, cols], last_scales[:, cols])
-            nc.scalar.copy(dx[:, cols], banks[e][:])
+        def scalar_gathers(a, e0, e1):
+            tile = ring.tile([P, PACK, (e1 - e0) * C], F32, name="staged", tag="staged", bufs=3)
+            for j in range(PACK):
+                nc.scalar.activation(tile[:, j, :], window[a, j][:].indirect(offsets(e0 * C, e1 * C)), COPY)
+            for e in range(e0, e1):
+                staged[a, e] = tile[:, :, (e - e0) * C : (e - e0 + 1) * C]
 
-        ds = partial[:, 0, :]
-        quarter = T // 4
+        rounded = {}
 
-        def finish_shared(b, codes):
+        def multiply(a, e):
+            rounded[a, e] = rounded_tile()
+            gate_runs = gate_sb[:, e * C : (e + 1) * C].rearrange("p (c i) -> p c i", i=RUN).unsqueeze(2).to_broadcast([P, C // RUN, PACK, RUN])
+            nc.vector.tensor_tensor(words_view(rounded[a, e]), by_runs(staged[a, e]), gate_runs, MULT)
+
+        own = {}
+
+        def own_gathers(a, planes):
+            if a not in own:
+                own[a] = ring.tile([P, PACK, C], F32, name="own", tag="own", bufs=1)
+            for j in planes:
+                nc.vector.tensor_tensor(own[a][:, j, :], window[a, j][:].indirect(offsets(0, C)), gate_sb[:, 0:C], MULT)
+
+        def round_own(a):
+            rounded[a, 0] = rounded_tile()
+            nc.vector.tensor_copy(words_view(rounded[a, 0]), by_runs(own[a][:]))
+
+        def round_shared(b):
             h, a = divmod(b, PASSES)
-            finish([(a, E, E + h)], shared_b[:, b, :, :], codes, shared_scales[:, b * BANK : (b + 1) * BANK])
+            rounded[a, E + h] = rounded_tile()
+            nc.vector.tensor_copy(words_view(rounded[a, E + h]), by_runs(raw[b][:]))
+            if b + 3 < HALVES * PASSES:
+                load_raw(b + 3)
+
+        def finish(a, bank):
+            e = min(bank, E)
+            codes = ring.tile([P, BANK], U32, name="codes", tag="codes", bufs=4, align_bytes=64)
+            scales = ring.tile([P, BANK], U8, name="scales", tag="scales", bufs=4, align_bytes=64)
+            nc.vector.quantize_mx(out=codes[:].bitcast(E5M2X4), scales=scales[:], in_=rounded[a, bank][:].rearrange("p c j -> p (c j)"))
+            nc.tensor.matmul_mx(
+                out=banks[bank][:],
+                lhsT=words[:, e * PASSES + a, :].bitcast(E2M1X4),
+                lhsT_scale=wscale[:, e * PASSES + a, :],
+                rhs=codes[:].bitcast(E5M2X4),
+                rhs_scale=scales[:],
+                start=(a == 0),
+                stop=(a == PASSES - 1),
+            )
             if a == PASSES - 1:
-                for c0 in range(0, BANK, quarter):
-                    nc.scalar.copy(ds[:, h * BANK + c0 : h * BANK + c0 + quarter], banks[E + h][:, c0 : c0 + quarter])
+                dst = dx[:, bank * C : (bank + 1) * C] if bank < E else ds[:, (bank - E) * BANK : (bank - E + 1) * BANK]
+                nc.scalar.copy(dst, banks[bank][:])
 
-        for e in range(E):
-            finish_held(e)
-            if e < SPLIT // C:
-                finish_last(e)
-        for b in range(EARLY):
-            finish_shared(b, early_codes[:, b * BANK : (b + 1) * BANK])
-        for e in range(SPLIT // C, E):
-            finish_last(e)
-        for b in range(EARLY, HALVES * PASSES):
-            finish_shared(b, late_codes[:, (b - EARLY) * BANK : (b - EARLY + 1) * BANK])
+        def finish_shared(b):
+            h, a = divmod(b, PASSES)
+            finish(a, E + h)
 
-        sums = [partial[:, 1, :], further[:, 0, :], further[:, 1, :]]
+        def pair(a, e):
+            multiply(a, e)
+            multiply(a, e + 1)
+            finish(a, e)
+            finish(a, e + 1)
 
-        def fetch(r, t0, t1):
-            so_far = ds if r == 0 else sums[r - 1]
-            nc.vector.tensor_tensor(sums[r][:, t0:t1], dx[:].indirect(pos_sb[r][:, t0 // GROUP : t1 // GROUP]), so_far[:, t0:t1], ADD)
-            if r == 2:
-                nc.sync.dma_start(out[:, t0:t1], sums[r][:, t0:t1])
+        groups = [(1, 3), (3, 5), (5, 6)]
+        steps = [(a, e0, e1) for a in range(PASSES) for e0, e1 in groups]
+        scalar_gathers(*steps[0])
+        scalar_gathers(*steps[1])
+        own_gathers(0, range(PACK))
+        round_shared(0)
+        round_own(0)
+        finish_shared(0)
+        finish(0, 0)
+        for a in range(PASSES):
+            last = a == PASSES - 1
+            scalar_gathers(*steps[3 * a + 2])
+            pair(a, 1)
+            if not last:
+                scalar_gathers(*steps[3 * a + 3])
+                round_shared(a + 1)
+                own_gathers(a + 1, (0, 1))
+                finish_shared(a + 1)
+            else:
+                round_shared(3)
+                round_shared(4)
+                finish_shared(3)
+                finish_shared(4)
+            pair(a, 3)
+            if not last:
+                scalar_gathers(*steps[3 * a + 4])
+            multiply(a, 5)
+            if not last:
+                own_gathers(a + 1, (2, 3))
+                finish(a, 5)
+                round_own(a + 1)
+                finish(a + 1, 0)
+            else:
+                round_shared(5)
+                finish(a, 5)
+                finish_shared(5)
 
-        for r in range(2):
-            fetch(r, 0, quarter)
-            fetch(r, quarter, BANK)
-        fetch(0, BANK, T)
-        fetch(2, 0, BANK)
-        for r in range(1, 3):
-            fetch(r, BANK, T - LAST)
-            fetch(r, T - LAST, T)
+        quarter = T // 4
+        first = keep.tile([P, T], F32, name="first")
+        fetched = [keep.tile([P, T], F32, name="fetched%d" % r) for r in range(2)]
+        second = keep.tile([P, T], F32, name="second")
+        total = keep.tile([P, T], F32, name="total")
+        for q in range(4):
+            cols = slice(q * quarter, (q + 1) * quarter)
+            lists = slice(q * quarter // GROUP, (q + 1) * quarter // GROUP)
+            for r in range(2):
+                nc.scalar.activation(fetched[r][:, cols], dx[:].indirect(pos_sb[r + 1][:, lists]), COPY)
+        for q in range(5):
+            if q < 4:
+                cols = slice(q * quarter, (q + 1) * quarter)
+                lists = slice(q * quarter // GROUP, (q + 1) * quarter // GROUP)
+                nc.vector.tensor_tensor(first[:, cols], dx[:].indirect(pos_sb[0][:, lists]), ds[:, cols], ADD)
+            if q > 0:
+                cols = slice((q - 1) * quarter, q * quarter)
+                nc.vector.tensor_tensor(second[:, cols], first[:, cols], fetched[0][:, cols], ADD)
+                nc.vector.tensor_tensor(total[:, cols], second[:, cols], fetched[1][:, cols], ADD)
+                nc.sync.dma_start(out[:, cols], total[:, cols])

@@ -1,6 +1,7 @@
 from contextlib import ExitStack
 
 import concourse.mybir as mybir
+from concourse.masks import make_identity
 
 K, T, E, C, N = 128, 1024, 6, 512, 1536
 S = E * C
@@ -25,10 +26,11 @@ BANK = 512
 HALVES = T // BANK
 GROUP = 16
 
-PAD_W = 16
-WIN = T + PAD_W
 RUN = 4
 COPY = mybir.ActivationFunctionType.Copy
+CYCLES = PASSES * HALVES
+ON_VECTOR = 4
+PIECE = 4 * PACK * C
 
 
 def tile_moe_bds_lin_none_kernel(tc, dyT, w_words, w_scales, gate, offs, pos1, pos2, pos3, out):
@@ -40,171 +42,166 @@ def tile_moe_bds_lin_none_kernel(tc, dyT, w_words, w_scales, gate, offs, pos1, p
 
         offs_sb = keep.tile([P, S // GROUP], U16, name="offs_sb")
         pos_sb = [keep.tile([P, T // GROUP], U16, name="pos_sb%d" % r) for r in range(3)]
-        gate_sb = keep.tile([P, S], F32, name="gate_sb")
+        gate_sb = keep.tile([P, (E - ON_VECTOR) * C], F32, name="gate_sb")
+        gate_col = keep.tile([P, ON_VECTOR, RUN], F32, name="gate_col")
+        ident = keep.tile([P, P], F32, name="ident")
         words = keep.tile([P, (E + 1) * PASSES, 2 * K], U8, name="words", align_bytes=64)
         wscale = keep.tile([P, (E + 1) * PASSES, K], U8, name="wscale", align_bytes=64)
-        banks = [psum.tile([P, BANK], F32, name="bank%d" % b) for b in range(E + HALVES)]
-        window = {(a, j): keep.tile([P, WIN], F32, name="window%d_%d" % (a, j)) for a in range(PASSES) for j in range(PACK)}
+        planes = [keep.tile([P, PACK, T], F32, name="planes%d" % a) for a in range(PASSES)]
         dx = keep.tile([P, S], F32, name="dx")
         ds = keep.tile([P, T], F32, name="ds")
 
+        def bank(b):
+            return psum.tile([P, BANK], F32, name="bank", tag="bank%d" % b, bufs=1)
+
         rows = dyT.rearrange("(a p j) t -> a p j t", p=P, j=PACK)
 
-        def load_window(a, j):
-            nc.sync.dma_start(window[a, j][:, 0:T], rows[a, :, j, :])
-
-        def load_gate(e0, e1):
-            nc.sync.dma_start(gate_sb[:, e0 * C : e1 * C], gate[0:P, e0 * C : e1 * C])
-
-        raw = {}
-
-        def load_raw(b):
-            h, a = divmod(b, PASSES)
-            raw[b] = ring.tile([P, PACK, BANK], F32, name="raw", tag="raw", bufs=3)
-            nc.sync.dma_start(raw[b][:], rows[a, :, :, h * BANK : (h + 1) * BANK])
+        def load_plane(a, j):
+            nc.sync.dma_start(planes[a][:, j, :], rows[a, :, j, :])
 
         nc.vector.memset(wscale[:].rearrange("p m k -> p (m k)").bitcast(I32), 0)
+        make_identity(nc, ident[:])
 
-        def load_weights():
-            nc.sync.dma_start(words[:].bitcast(I32), w_words.rearrange("e a p b -> p (e a) b").bitcast(I32))
-            scale_rows = w_scales.rearrange("e a f k -> f (e a) k")
-            for q in range(4):
-                nc.sync.dma_start(wscale[32 * q : 32 * q + 4, :, :].bitcast(I32), scale_rows[4 * q : 4 * q + 4, :, :].bitcast(I32))
-
-        load_window(0, 0)
+        load_plane(0, 0)
         nc.sync.dma_start(offs_sb[:], offs)
-        load_gate(0, 1)
-        for j in range(1, PACK):
-            load_window(0, j)
-        load_raw(0)
-        load_gate(1, 3)
-        load_weights()
-        load_raw(1)
-        for j in range(PACK):
-            load_window(1, j)
-        load_gate(3, E)
-        load_raw(2)
-        for j in range(PACK):
-            load_window(2, j)
+        load_plane(0, 1)
+        nc.sync.dma_start(gate_col[:], gate[0, 0 : ON_VECTOR * C].rearrange("(e p i) -> p e i", p=P, i=RUN))
+        load_plane(0, 2)
+        load_plane(0, 3)
+        nc.sync.dma_start(gate_sb[:], gate[0:P, ON_VECTOR * C : S])
+        nc.sync.dma_start(words[:].bitcast(I32), w_words.rearrange("e a p b -> p (e a) b").bitcast(I32))
+        scale_rows = w_scales.rearrange("e a f k -> f (e a) k")
+        for q in range(4):
+            nc.sync.dma_start(wscale[32 * q : 32 * q + 4, :, :].bitcast(I32), scale_rows[4 * q : 4 * q + 4, :, :].bitcast(I32))
+        for a in range(1, PASSES):
+            for j in range(PACK):
+                load_plane(a, j)
         for tile, src in zip(pos_sb, (pos1, pos2, pos3)):
             nc.sync.dma_start(tile[:], src)
 
-        def offsets(s0, s1):
-            return offs_sb[:, s0 // GROUP : s1 // GROUP]
+        gate_bank = [bank(e) for e in range(ON_VECTOR)]
+        for e in range(ON_VECTOR):
+            for i in range(RUN):
+                nc.tensor.transpose(gate_bank[e][:, i * P : (i + 1) * P], gate_col[:, e, i : i + 1].to_broadcast([P, P]), ident[:])
+
+        def looked_up(a, j, e):
+            return planes[a][:, j, :].indirect(offs_sb[:, e * C // GROUP : (e + 1) * C // GROUP])
 
         def by_runs(ap):
             return ap.rearrange("p j (c i) -> p c j i", i=RUN)
 
-        def rounded_tile():
-            return ring.tile([P, BANK, PACK], BF16, name="rounded", tag="rounded", bufs=4, align_bytes=64)
+        def as_words(ap):
+            return ap.rearrange("p (c i) j -> p c j i", i=RUN)
 
-        def words_view(tile):
-            return tile[:].rearrange("p (c i) j -> p c j i", i=RUN)
+        def over_planes(ap):
+            return ap.unsqueeze(2).to_broadcast([P, C // RUN, PACK, RUN])
 
         staged = {}
 
-        def scalar_gathers(a, e0, e1):
-            tile = ring.tile([P, PACK, (e1 - e0) * C], F32, name="staged", tag="staged", bufs=3)
+        def scalar_gathers(a, e):
+            staged[a, e] = ring.tile([P, PACK, C], F32, name="staged", tag="staged", bufs=4, align_bytes=64)
             for j in range(PACK):
-                nc.scalar.activation(tile[:, j, :], window[a, j][:].indirect(offsets(e0 * C, e1 * C)), COPY)
-            for e in range(e0, e1):
-                staged[a, e] = tile[:, :, (e - e0) * C : (e - e0 + 1) * C]
+                nc.scalar.activation(staged[a, e][:, j, :], looked_up(a, j, e), COPY)
 
-        rounded = {}
+        def vector_gathers(a, e):
+            staged[a, e] = ring.tile([P, PACK, C], F32, name="handed", tag="handed", bufs=2)
+            for j in range(PACK):
+                nc.vector.tensor_copy(staged[a, e][:, j, :], looked_up(a, j, e))
 
-        def multiply(a, e):
-            rounded[a, e] = rounded_tile()
-            gate_runs = gate_sb[:, e * C : (e + 1) * C].rearrange("p (c i) -> p c i", i=RUN).unsqueeze(2).to_broadcast([P, C // RUN, PACK, RUN])
-            nc.vector.tensor_tensor(words_view(rounded[a, e]), by_runs(staged[a, e]), gate_runs, MULT)
+        def vector_product(dst, a, e):
+            gates = gate_bank[e][:].rearrange("p (i c) -> p c i", i=RUN)
+            nc.vector.tensor_tensor(as_words(dst), by_runs(staged[a, e][:]), over_planes(gates), MULT)
 
-        own = {}
+        def gpsimd_product(dst, a, e):
+            gates = gate_sb[:, (e - ON_VECTOR) * C : (e - ON_VECTOR + 1) * C].unsqueeze(2).to_broadcast([P, C, PACK])
+            nc.gpsimd.tensor_tensor(dst, staged[a, e][:].rearrange("p j c -> p c j"), gates, MULT)
 
-        def own_gathers(a, planes):
-            if a not in own:
-                own[a] = ring.tile([P, PACK, C], F32, name="own", tag="own", bufs=1)
-            for j in planes:
-                nc.vector.tensor_tensor(own[a][:, j, :], window[a, j][:].indirect(offsets(0, C)), gate_sb[:, 0:C], MULT)
+        def tokens(a, h):
+            return by_runs(planes[a][:, :, h * BANK : (h + 1) * BANK])
 
-        def round_own(a):
-            rounded[a, 0] = rounded_tile()
-            nc.vector.tensor_copy(words_view(rounded[a, 0]), by_runs(own[a][:]))
+        quantised = {}
 
-        def round_shared(b):
-            h, a = divmod(b, PASSES)
-            rounded[a, E + h] = rounded_tile()
-            nc.vector.tensor_copy(words_view(rounded[a, E + h]), by_runs(raw[b][:]))
-            if b + 3 < HALVES * PASSES:
-                load_raw(b + 3)
+        def quantise(a, groups, src, codes, scales):
+            nc.vector.quantize_mx(out=codes.bitcast(E5M2X4), scales=scales, in_=src)
+            for n, g in enumerate(groups):
+                quantised[a, g] = (codes[:, n * BANK : (n + 1) * BANK], scales[:, n * BANK : (n + 1) * BANK])
 
-        def finish(a, bank):
-            e = min(bank, E)
-            codes = ring.tile([P, BANK], U32, name="codes", tag="codes", bufs=4, align_bytes=64)
-            scales = ring.tile([P, BANK], U8, name="scales", tag="scales", bufs=4, align_bytes=64)
-            nc.vector.quantize_mx(out=codes[:].bitcast(E5M2X4), scales=scales[:], in_=rounded[a, bank][:].rearrange("p c j -> p (c j)"))
+        bank_of = {E: 4, E + 1: 5, 0: 6, 4: 7, 1: 0, 2: 1, 5: 2, 3: 3}
+        sums = {}
+
+        def multiply(a, g):
+            if a == 0:
+                sums[g] = bank(bank_of[g])
+            e = min(g, E)
+            codes, scales = quantised[a, g]
             nc.tensor.matmul_mx(
-                out=banks[bank][:],
+                out=sums[g][:],
                 lhsT=words[:, e * PASSES + a, :].bitcast(E2M1X4),
                 lhsT_scale=wscale[:, e * PASSES + a, :],
-                rhs=codes[:].bitcast(E5M2X4),
-                rhs_scale=scales[:],
+                rhs=codes.bitcast(E5M2X4),
+                rhs_scale=scales,
                 start=(a == 0),
                 stop=(a == PASSES - 1),
             )
             if a == PASSES - 1:
-                dst = dx[:, bank * C : (bank + 1) * C] if bank < E else ds[:, (bank - E) * BANK : (bank - E + 1) * BANK]
-                nc.scalar.copy(dst, banks[bank][:])
+                dst = dx[:, g * C : (g + 1) * C] if g < E else ds[:, (g - E) * BANK : (g - E + 1) * BANK]
+                nc.scalar.copy(dst, sums[g][:])
 
-        def finish_shared(b):
-            h, a = divmod(b, PASSES)
-            finish(a, E + h)
+        def multiply_ready(a, groups):
+            for g in groups:
+                if bank_of[g] >= ON_VECTOR:
+                    multiply(a, g)
+                elif a == PASSES - 1:
+                    for earlier in range(PASSES):
+                        multiply(earlier, g)
 
-        def pair(a, e):
-            multiply(a, e)
-            multiply(a, e + 1)
-            finish(a, e)
-            finish(a, e + 1)
+        def cycle_of(k):
+            a, h = divmod(k, HALVES)
+            return a, h, 2 * h, 2 * h + 1, ON_VECTOR + h
 
-        groups = [(1, 3), (3, 5), (5, 6)]
-        steps = [(a, e0, e1) for a in range(PASSES) for e0, e1 in groups]
-        scalar_gathers(*steps[0])
-        scalar_gathers(*steps[1])
-        own_gathers(0, range(PACK))
-        round_shared(0)
-        round_own(0)
-        finish_shared(0)
-        finish(0, 0)
-        for a in range(PASSES):
-            last = a == PASSES - 1
-            scalar_gathers(*steps[3 * a + 2])
-            pair(a, 1)
+        def prepare(k):
+            a, h, first, second, handed = cycle_of(k)
+            scalar_gathers(a, first)
+            scalar_gathers(a, second)
+
+        prepare(0)
+        prepare(1)
+        vector_gathers(0, ON_VECTOR)
+        for k in range(CYCLES):
+            a, h, first, second, handed = cycle_of(k)
+            last = k == CYCLES - 1
+            rounded = ring.tile([P, 4, BANK, PACK], BF16, name="rounded", tag="rounded", bufs=1, align_bytes=64)
             if not last:
-                scalar_gathers(*steps[3 * a + 3])
-                round_shared(a + 1)
-                own_gathers(a + 1, (0, 1))
-                finish_shared(a + 1)
+                nc.gpsimd.tensor_scalar(rounded[:, 2], planes[a][:, :, h * BANK : (h + 1) * BANK].rearrange("p j c -> p c j"), 1.0, 0.0, MULT, ADD)
+            gpsimd_product(rounded[:, 0], a, handed)
+            vector_product(rounded[:, 1], a, first)
+            if not last:
+                vector_gathers(cycle_of(k + 1)[0], cycle_of(k + 1)[4])
+            vector_product(rounded[:, 3], a, second)
+            if k + 2 < CYCLES:
+                prepare(k + 2)
+            if k + 2 == CYCLES:
+                held = ring.tile([P, BANK, PACK], BF16, name="held", tag="staged", bufs=4, align_bytes=64)
+                nc.scalar.copy(as_words(held[:]), tokens(PASSES - 1, HALVES - 1))
+            codes = keep.tile([P, 4 * BANK], U32, name="codes%d" % k, align_bytes=64)
+            scales = keep.tile([P, 4 * BANK], U8, name="scales%d" % k, align_bytes=64)
+            flat = rounded[:].rearrange("p n c j -> p (n c j)")
+            width = BANK * PACK
+            quantise(a, [handed, first], flat[:, 0 : 2 * width], codes[:, 0 : 2 * BANK], scales[:, 0 : 2 * BANK])
+            if not last:
+                quantise(a, [E + h, second], flat[:, 2 * width :], codes[:, 2 * BANK :], scales[:, 2 * BANK :])
+                multiply_ready(a, [handed, first, E + h, second])
             else:
-                round_shared(3)
-                round_shared(4)
-                finish_shared(3)
-                finish_shared(4)
-            pair(a, 3)
-            if not last:
-                scalar_gathers(*steps[3 * a + 4])
-            multiply(a, 5)
-            if not last:
-                own_gathers(a + 1, (2, 3))
-                finish(a, 5)
-                round_own(a + 1)
-                finish(a + 1, 0)
-            else:
-                round_shared(5)
-                finish(a, 5)
-                finish_shared(5)
+                quantise(a, [second], flat[:, 3 * width :], codes[:, 3 * BANK :], scales[:, 3 * BANK :])
+                multiply_ready(a, [handed, first, second])
+                held_codes = ring.tile([P, BANK], U32, name="held_codes", tag="rounded", bufs=1, align_bytes=64)
+                quantise(a, [E + h], held[:].rearrange("p c j -> p (c j)"), held_codes[:], scales[:, 2 * BANK : 3 * BANK])
+                multiply_ready(a, [E + h])
 
         quarter = T // 4
-        first = keep.tile([P, T], F32, name="first")
+        first_sum = keep.tile([P, T], F32, name="first_sum")
         fetched = [keep.tile([P, T], F32, name="fetched%d" % r) for r in range(2)]
-        second = keep.tile([P, T], F32, name="second")
+        second_sum = keep.tile([P, T], F32, name="second_sum")
         total = keep.tile([P, T], F32, name="total")
         for q in range(4):
             cols = slice(q * quarter, (q + 1) * quarter)
@@ -215,9 +212,9 @@ def tile_moe_bds_lin_none_kernel(tc, dyT, w_words, w_scales, gate, offs, pos1, p
             if q < 4:
                 cols = slice(q * quarter, (q + 1) * quarter)
                 lists = slice(q * quarter // GROUP, (q + 1) * quarter // GROUP)
-                nc.vector.tensor_tensor(first[:, cols], dx[:].indirect(pos_sb[0][:, lists]), ds[:, cols], ADD)
+                nc.vector.tensor_tensor(first_sum[:, cols], dx[:].indirect(pos_sb[0][:, lists]), ds[:, cols], ADD)
             if q > 0:
                 cols = slice((q - 1) * quarter, q * quarter)
-                nc.vector.tensor_tensor(second[:, cols], first[:, cols], fetched[0][:, cols], ADD)
-                nc.vector.tensor_tensor(total[:, cols], second[:, cols], fetched[1][:, cols], ADD)
+                nc.vector.tensor_tensor(second_sum[:, cols], first_sum[:, cols], fetched[0][:, cols], ADD)
+                nc.vector.tensor_tensor(total[:, cols], second_sum[:, cols], fetched[1][:, cols], ADD)
                 nc.sync.dma_start(out[:, cols], total[:, cols])

@@ -38,6 +38,7 @@ def tile_moe_bds_lin_none_kernel(tc, dyT, w_words, w_scales, gate, offs, pos1, p
     with ExitStack() as ctx:
         keep = ctx.enter_context(tc.tile_pool(name="keep", bufs=1))
         ring = ctx.enter_context(tc.tile_pool(name="ring", bufs=2))
+        slide = ctx.enter_context(tc.tile_pool(name="slide", bufs=1))
         psum = ctx.enter_context(tc.psum_pool(name="psum", bufs=1))
 
         offs_sb = keep.tile([P, S // GROUP], U16, name="offs_sb")
@@ -49,7 +50,7 @@ def tile_moe_bds_lin_none_kernel(tc, dyT, w_words, w_scales, gate, offs, pos1, p
         wscale = keep.tile([P, (E + 1) * PASSES, K], U8, name="wscale", align_bytes=64)
         planes = [keep.tile([P, PACK, T], F32, name="planes%d" % a) for a in range(PASSES)]
         dx = keep.tile([P, S], F32, name="dx")
-        ds = keep.tile([P, T], F32, name="ds")
+        ds = keep.tile([P, BANK], F32, name="ds")
 
         def bank(b):
             return psum.tile([P, BANK], F32, name="bank", tag="bank%d" % b, bufs=1)
@@ -98,13 +99,19 @@ def tile_moe_bds_lin_none_kernel(tc, dyT, w_words, w_scales, gate, offs, pos1, p
 
         staged = {}
 
-        def scalar_gathers(a, e):
+        def scalar_gathers(a, e, count=PACK):
             staged[a, e] = ring.tile([P, PACK, C], F32, name="staged", tag="staged", bufs=4, align_bytes=64)
-            for j in range(PACK):
+            for j in range(count):
                 nc.scalar.activation(staged[a, e][:, j, :], looked_up(a, j, e), COPY)
+            for j in range(count, PACK):
+                nc.vector.tensor_copy(staged[a, e][:, j, :], looked_up(a, j, e))
 
-        def vector_gathers(a, e):
-            staged[a, e] = ring.tile([P, PACK, C], F32, name="handed", tag="handed", bufs=2)
+        def placed(shape, dtype, name, step):
+            return slide.tile(shape, dtype, name=name, offset=step * PIECE, align_bytes=64)
+
+        def vector_gathers(k):
+            a, e = cycle_of(k)[0], cycle_of(k)[4]
+            staged[a, e] = placed([P, PACK, C], F32, "handed%d" % k, k - 2 if k >= 2 else CYCLES - 1 + k)
             for j in range(PACK):
                 nc.vector.tensor_copy(staged[a, e][:, j, :], looked_up(a, j, e))
 
@@ -121,9 +128,13 @@ def tile_moe_bds_lin_none_kernel(tc, dyT, w_words, w_scales, gate, offs, pos1, p
 
         quantised = {}
 
-        def quantise(a, groups, src, codes, scales):
+        def gpsimd_round(dst, a, h):
+            src = planes[a][:, :, h * BANK : (h + 1) * BANK].rearrange("p j c -> p c j")
+            nc.gpsimd.tensor_scalar(dst, src, 1.0, 0.0, MULT, ADD)
+
+        def quantise(pieces, src, codes, scales):
             nc.vector.quantize_mx(out=codes.bitcast(E5M2X4), scales=scales, in_=src)
-            for n, g in enumerate(groups):
+            for n, (a, g) in enumerate(pieces):
                 quantised[a, g] = (codes[:, n * BANK : (n + 1) * BANK], scales[:, n * BANK : (n + 1) * BANK])
 
         bank_of = {E: 4, E + 1: 5, 0: 6, 4: 7, 1: 0, 2: 1, 5: 2, 3: 3}
@@ -143,8 +154,8 @@ def tile_moe_bds_lin_none_kernel(tc, dyT, w_words, w_scales, gate, offs, pos1, p
                 start=(a == 0),
                 stop=(a == PASSES - 1),
             )
-            if a == PASSES - 1:
-                dst = dx[:, g * C : (g + 1) * C] if g < E else ds[:, (g - E) * BANK : (g - E + 1) * BANK]
+            if a == PASSES - 1 and g <= E:
+                dst = dx[:, g * C : (g + 1) * C] if g < E else ds[:]
                 nc.scalar.copy(dst, sums[g][:])
 
         def multiply_ready(a, groups):
@@ -166,55 +177,83 @@ def tile_moe_bds_lin_none_kernel(tc, dyT, w_words, w_scales, gate, offs, pos1, p
 
         prepare(0)
         prepare(1)
-        vector_gathers(0, ON_VECTOR)
+        vector_gathers(0)
+        width = BANK * PACK
         for k in range(CYCLES):
             a, h, first, second, handed = cycle_of(k)
             last = k == CYCLES - 1
-            rounded = ring.tile([P, 4, BANK, PACK], BF16, name="rounded", tag="rounded", bufs=1, align_bytes=64)
-            if not last:
-                nc.gpsimd.tensor_scalar(rounded[:, 2], planes[a][:, :, h * BANK : (h + 1) * BANK].rearrange("p j c -> p c j"), 1.0, 0.0, MULT, ADD)
+            rounded = placed([P, 4, BANK, PACK], BF16, "rounded%d" % k, k)
+            shared = divmod(k + 1, HALVES) if k + 2 < CYCLES else None
+            if k == 0:
+                extra = keep.tile([P, BANK, PACK], BF16, name="extra", align_bytes=64)
+                gpsimd_round(extra[:], 0, 0)
+            if shared:
+                gpsimd_round(rounded[:, 2], *shared)
             gpsimd_product(rounded[:, 0], a, handed)
-            vector_product(rounded[:, 1], a, first)
-            if not last:
-                vector_gathers(cycle_of(k + 1)[0], cycle_of(k + 1)[4])
-            vector_product(rounded[:, 3], a, second)
+            if k > 0:
+                vector_product(rounded[:, 1], a, first)
             if k + 2 < CYCLES:
+                vector_gathers(k + 1)
+            if k == 0:
+                vector_product(rounded[:, 1], a, first)
+            vector_product(rounded[:, 3], a, second)
+            if k + 3 < CYCLES:
                 prepare(k + 2)
+            if k + 3 == CYCLES:
+                a5, h5, first5, second5, handed5 = cycle_of(k + 2)
+                scalar_gathers(a5, handed5)
+                scalar_gathers(a5, first5)
+                scalar_gathers(a5, second5, PACK - 1)
             if k + 2 == CYCLES:
                 held = ring.tile([P, BANK, PACK], BF16, name="held", tag="staged", bufs=4, align_bytes=64)
                 nc.scalar.copy(as_words(held[:]), tokens(PASSES - 1, HALVES - 1))
             codes = keep.tile([P, 4 * BANK], U32, name="codes%d" % k, align_bytes=64)
             scales = keep.tile([P, 4 * BANK], U8, name="scales%d" % k, align_bytes=64)
             flat = rounded[:].rearrange("p n c j -> p (n c j)")
-            width = BANK * PACK
-            quantise(a, [handed, first], flat[:, 0 : 2 * width], codes[:, 0 : 2 * BANK], scales[:, 0 : 2 * BANK])
-            if not last:
-                quantise(a, [E + h, second], flat[:, 2 * width :], codes[:, 2 * BANK :], scales[:, 2 * BANK :])
-                multiply_ready(a, [handed, first, E + h, second])
+            if last:
+                for n, g in enumerate((handed, first)):
+                    quantise([(a, g)], flat[:, n * width : (n + 1) * width], codes[:, n * BANK : (n + 1) * BANK], scales[:, n * BANK : (n + 1) * BANK])
             else:
-                quantise(a, [second], flat[:, 3 * width :], codes[:, 3 * BANK :], scales[:, 3 * BANK :])
-                multiply_ready(a, [handed, first, second])
-                held_codes = ring.tile([P, BANK], U32, name="held_codes", tag="rounded", bufs=1, align_bytes=64)
-                quantise(a, [E + h], held[:].rearrange("p c j -> p (c j)"), held_codes[:], scales[:, 2 * BANK : 3 * BANK])
-                multiply_ready(a, [E + h])
+                quantise([(a, handed), (a, first)], flat[:, 0 : 2 * width], codes[:, 0 : 2 * BANK], scales[:, 0 : 2 * BANK])
+            if k == 0:
+                extra_codes = placed([P, BANK], U32, "extra_codes", CYCLES - 1)
+                extra_scales = keep.tile([P, BANK], U8, name="extra_scales", align_bytes=64)
+                quantise([(0, E)], extra[:].rearrange("p c j -> p (c j)"), extra_codes[:], extra_scales[:])
+                multiply(0, E)
+            if shared:
+                quantise([(shared[0], E + shared[1]), (a, second)], flat[:, 2 * width :], codes[:, 2 * BANK :], scales[:, 2 * BANK :])
+                multiply(shared[0], E + shared[1])
+            else:
+                quantise([(a, second)], flat[:, 3 * width :], codes[:, 3 * BANK :], scales[:, 3 * BANK :])
+            multiply_ready(a, [handed, first, second])
+            if last:
+                held_codes = placed([P, BANK], U32, "held_codes", k)
+                quantise([(a, E + h)], held[:].rearrange("p c j -> p (c j)"), held_codes[:], scales[:, 2 * BANK : 3 * BANK])
+                multiply(a, E + h)
 
-        quarter = T // 4
-        first_sum = keep.tile([P, T], F32, name="first_sum")
-        fetched = [keep.tile([P, T], F32, name="fetched%d" % r) for r in range(2)]
-        second_sum = keep.tile([P, T], F32, name="second_sum")
-        total = keep.tile([P, T], F32, name="total")
-        for q in range(4):
-            cols = slice(q * quarter, (q + 1) * quarter)
-            lists = slice(q * quarter // GROUP, (q + 1) * quarter // GROUP)
-            for r in range(2):
-                nc.scalar.activation(fetched[r][:, cols], dx[:].indirect(pos_sb[r + 1][:, lists]), COPY)
-        for q in range(5):
-            if q < 4:
-                cols = slice(q * quarter, (q + 1) * quarter)
-                lists = slice(q * quarter // GROUP, (q + 1) * quarter // GROUP)
-                nc.vector.tensor_tensor(first_sum[:, cols], dx[:].indirect(pos_sb[0][:, lists]), ds[:, cols], ADD)
-            if q > 0:
-                cols = slice((q - 1) * quarter, q * quarter)
-                nc.vector.tensor_tensor(second_sum[:, cols], first_sum[:, cols], fetched[0][:, cols], ADD)
-                nc.vector.tensor_tensor(total[:, cols], second_sum[:, cols], fetched[1][:, cols], ADD)
-                nc.sync.dma_start(out[:, cols], total[:, cols])
+        pairs = [placed([P, 2, T], F32, "pair%d" % n, n) for n in range(3)]
+        first_sum, second_sum, total = pairs[0][:, 0], pairs[0][:, 1], pairs[1][:, 0]
+        fetched = [pairs[2][:, 0], pairs[2][:, 1]]
+
+        def slots_of(r, t0, t1):
+            return dx[:].indirect(pos_sb[r][:, t0 // GROUP : t1 // GROUP])
+
+        def add(dst, in0, in1):
+            nc.vector.tensor_tensor(dst, in0, in1, ADD)
+
+        cut = 3 * T // 4
+        low, high = slice(0, BANK), slice(BANK, T)
+        nc.scalar.activation(fetched[0][:, high], slots_of(1, BANK, T), COPY)
+        nc.scalar.activation(fetched[0][:, low], slots_of(1, 0, BANK), COPY)
+        nc.scalar.activation(fetched[1][:, low], slots_of(2, 0, BANK), COPY)
+        nc.scalar.activation(fetched[1][:, BANK:cut], slots_of(2, BANK, cut), COPY)
+        add(first_sum[:, low], slots_of(0, 0, BANK), ds[:])
+        add(first_sum[:, high], slots_of(0, BANK, T), fetched[0][:, high])
+        add(second_sum[:, low], first_sum[:, low], fetched[0][:, low])
+        add(second_sum[:, high], first_sum[:, high], sums[E + 1][:])
+        add(total[:, low], second_sum[:, low], fetched[1][:, low])
+        nc.sync.dma_start(out[:, low], total[:, low])
+        add(total[:, cut:T], slots_of(2, cut, T), second_sum[:, cut:T])
+        nc.sync.dma_start(out[:, cut:T], total[:, cut:T])
+        add(total[:, BANK:cut], second_sum[:, BANK:cut], fetched[1][:, BANK:cut])
+        nc.sync.dma_start(out[:, BANK:cut], total[:, BANK:cut])

@@ -27,6 +27,7 @@ HALVES = T // BANK
 GROUP = 16
 
 RUN = 4
+PAD = 16
 COPY = mybir.ActivationFunctionType.Copy
 CYCLES = PASSES * HALVES
 ON_VECTOR = 4
@@ -39,6 +40,7 @@ def tile_moe_bds_lin_none_kernel(tc, dyT, w_words, w_scales, gate, offs, pos1, p
         keep = ctx.enter_context(tc.tile_pool(name="keep", bufs=1))
         ring = ctx.enter_context(tc.tile_pool(name="ring", bufs=2))
         slide = ctx.enter_context(tc.tile_pool(name="slide", bufs=1))
+        stage = ctx.enter_context(tc.tile_pool(name="stage", bufs=1))
         psum = ctx.enter_context(tc.psum_pool(name="psum", bufs=1))
 
         offs_sb = keep.tile([P, S // GROUP], U16, name="offs_sb")
@@ -48,7 +50,6 @@ def tile_moe_bds_lin_none_kernel(tc, dyT, w_words, w_scales, gate, offs, pos1, p
         ident = keep.tile([P, P], F32, name="ident")
         words = keep.tile([P, (E + 1) * PASSES, 2 * K], U8, name="words", align_bytes=64)
         wscale = keep.tile([P, (E + 1) * PASSES, K], U8, name="wscale", align_bytes=64)
-        planes = [keep.tile([P, PACK, T], F32, name="planes%d" % a) for a in range(PASSES)]
         dx = keep.tile([P, S], F32, name="dx")
         ds = keep.tile([P, BANK], F32, name="ds")
 
@@ -57,8 +58,23 @@ def tile_moe_bds_lin_none_kernel(tc, dyT, w_words, w_scales, gate, offs, pos1, p
 
         rows = dyT.rearrange("(a p j) t -> a p j t", p=P, j=PACK)
 
+        window = {}
+
         def load_plane(a, j):
-            nc.sync.dma_start(planes[a][:, j, :], rows[a, :, j, :])
+            window[a, j] = ring.tile([P, T + PAD], F32, name="window", tag="window", bufs=2 * PACK)
+            nc.sync.dma_start(window[a, j][:, 0:T], rows[a, :, j, :])
+
+        raw = {}
+
+        def staged_tile(shape, dtype, name, slot):
+            return stage.tile(shape, dtype, name=name, offset=slot * 2 * PIECE, align_bytes=64)
+
+        def load_raw(a, h):
+            if a == 0:
+                raw[a, h] = stage.tile([P, PACK, BANK], F32, name="raw%d" % h, offset=(2 - h) * 2 * PIECE, align_bytes=64)
+            else:
+                raw[a, h] = ring.tile([P, PACK, BANK], F32, name="raw", tag="raw", bufs=2)
+            nc.sync.dma_start(raw[a, h][:], rows[a, :, :, h * BANK : (h + 1) * BANK])
 
         nc.vector.memset(wscale[:].rearrange("p m k -> p (m k)").bitcast(I32), 0)
         make_identity(nc, ident[:])
@@ -66,17 +82,21 @@ def tile_moe_bds_lin_none_kernel(tc, dyT, w_words, w_scales, gate, offs, pos1, p
         load_plane(0, 0)
         nc.sync.dma_start(offs_sb[:], offs)
         load_plane(0, 1)
-        nc.sync.dma_start(gate_col[:], gate[0, 0 : ON_VECTOR * C].rearrange("(e p i) -> p e i", p=P, i=RUN))
+        load_raw(0, 0)
         load_plane(0, 2)
+        load_raw(0, 1)
         load_plane(0, 3)
         nc.sync.dma_start(gate_sb[:], gate[0:P, ON_VECTOR * C : S])
+        nc.sync.dma_start(gate_col[:], gate[0, 0 : ON_VECTOR * C].rearrange("(e p i) -> p e i", p=P, i=RUN))
+        load_plane(1, 0)
+        load_plane(1, 1)
+        load_raw(1, 0)
+        load_plane(1, 2)
+        load_plane(1, 3)
         nc.sync.dma_start(words[:].bitcast(I32), w_words.rearrange("e a p b -> p (e a) b").bitcast(I32))
         scale_rows = w_scales.rearrange("e a f k -> f (e a) k")
         for q in range(4):
             nc.sync.dma_start(wscale[32 * q : 32 * q + 4, :, :].bitcast(I32), scale_rows[4 * q : 4 * q + 4, :, :].bitcast(I32))
-        for a in range(1, PASSES):
-            for j in range(PACK):
-                load_plane(a, j)
         for tile, src in zip(pos_sb, (pos1, pos2, pos3)):
             nc.sync.dma_start(tile[:], src)
 
@@ -85,8 +105,8 @@ def tile_moe_bds_lin_none_kernel(tc, dyT, w_words, w_scales, gate, offs, pos1, p
             for i in range(RUN):
                 nc.tensor.transpose(gate_bank[e][:, i * P : (i + 1) * P], gate_col[:, e, i : i + 1].to_broadcast([P, P]), ident[:])
 
-        def looked_up(a, j, e):
-            return planes[a][:, j, :].indirect(offs_sb[:, e * C // GROUP : (e + 1) * C // GROUP])
+        def looked_up(a, j, e, experts=1):
+            return window[a, j][:].indirect(offs_sb[:, e * C // GROUP : (e + experts) * C // GROUP])
 
         def by_runs(ap):
             return ap.rearrange("p j (c i) -> p c j i", i=RUN)
@@ -99,38 +119,39 @@ def tile_moe_bds_lin_none_kernel(tc, dyT, w_words, w_scales, gate, offs, pos1, p
 
         staged = {}
 
-        def scalar_gathers(a, e, count=PACK):
-            staged[a, e] = ring.tile([P, PACK, C], F32, name="staged", tag="staged", bufs=4, align_bytes=64)
-            for j in range(count):
-                nc.scalar.activation(staged[a, e][:, j, :], looked_up(a, j, e), COPY)
-            for j in range(count, PACK):
-                nc.vector.tensor_copy(staged[a, e][:, j, :], looked_up(a, j, e))
+        def scalar_gathers(a, e, experts, tile):
+            for j in range(PACK):
+                nc.scalar.activation(tile[:, j, :], looked_up(a, j, e, experts), COPY)
+            for n in range(experts):
+                staged[a, e + n] = tile[:, :, n * C : (n + 1) * C]
+
 
         def placed(shape, dtype, name, step):
             return slide.tile(shape, dtype, name=name, offset=step * PIECE, align_bytes=64)
 
-        def vector_gathers(k):
-            a, e = cycle_of(k)[0], cycle_of(k)[4]
-            staged[a, e] = placed([P, PACK, C], F32, "handed%d" % k, k - 2 if k >= 2 else CYCLES - 1 + k)
+        def vector_gathers(*cycles):
+            pieces = [(cycle_of(k)[0], cycle_of(k)[4]) for k in cycles]
+            for k, piece in zip(cycles, pieces):
+                staged[piece] = placed([P, PACK, C], F32, "handed%d" % k, k - 2 if k >= 2 else CYCLES - 1 + k)[:]
             for j in range(PACK):
-                nc.vector.tensor_copy(staged[a, e][:, j, :], looked_up(a, j, e))
+                for a, e in pieces:
+                    nc.vector.tensor_copy(staged[a, e][:, j, :], looked_up(a, j, e))
 
         def vector_product(dst, a, e):
             gates = gate_bank[e][:].rearrange("p (i c) -> p c i", i=RUN)
-            nc.vector.tensor_tensor(as_words(dst), by_runs(staged[a, e][:]), over_planes(gates), MULT)
+            nc.vector.tensor_tensor(as_words(dst), by_runs(staged[a, e]), over_planes(gates), MULT)
 
         def gpsimd_product(dst, a, e):
             gates = gate_sb[:, (e - ON_VECTOR) * C : (e - ON_VECTOR + 1) * C].unsqueeze(2).to_broadcast([P, C, PACK])
-            nc.gpsimd.tensor_tensor(dst, staged[a, e][:].rearrange("p j c -> p c j"), gates, MULT)
-
-        def tokens(a, h):
-            return by_runs(planes[a][:, :, h * BANK : (h + 1) * BANK])
+            nc.gpsimd.tensor_tensor(dst, staged[a, e].rearrange("p j c -> p c j"), gates, MULT)
 
         quantised = {}
 
         def gpsimd_round(dst, a, h):
-            src = planes[a][:, :, h * BANK : (h + 1) * BANK].rearrange("p j c -> p c j")
-            nc.gpsimd.tensor_scalar(dst, src, 1.0, 0.0, MULT, ADD)
+            nc.gpsimd.tensor_scalar(dst, raw[a, h][:].rearrange("p j c -> p c j"), 1.0, 0.0, MULT, ADD)
+            later = divmod(HALVES * a + h + 2, HALVES)
+            if later[0] < PASSES and later != (1, 0):
+                load_raw(*later)
 
         def quantise(pieces, src, codes, scales):
             nc.vector.quantize_mx(out=codes.bitcast(E5M2X4), scales=scales, in_=src)
@@ -172,12 +193,10 @@ def tile_moe_bds_lin_none_kernel(tc, dyT, w_words, w_scales, gate, offs, pos1, p
 
         def prepare(k):
             a, h, first, second, handed = cycle_of(k)
-            scalar_gathers(a, first)
-            scalar_gathers(a, second)
+            scalar_gathers(a, first, 2, staged_tile([P, PACK, 2 * C], F32, "staged%d" % k, k % 3))
 
         prepare(0)
-        prepare(1)
-        vector_gathers(0)
+        vector_gathers(0, 1)
         width = BANK * PACK
         for k in range(CYCLES):
             a, h, first, second, handed = cycle_of(k)
@@ -190,24 +209,30 @@ def tile_moe_bds_lin_none_kernel(tc, dyT, w_words, w_scales, gate, offs, pos1, p
             if shared:
                 gpsimd_round(rounded[:, 2], *shared)
             gpsimd_product(rounded[:, 0], a, handed)
-            if k > 0:
-                vector_product(rounded[:, 1], a, first)
-            if k + 2 < CYCLES:
-                vector_gathers(k + 1)
             if k == 0:
-                vector_product(rounded[:, 1], a, first)
+                prepare(1)
+            if 0 < k < CYCLES - 2:
+                vector_gathers(k + 1)
+            if k == 1:
+                for j in range(PACK):
+                    load_plane(2, j)
+            vector_product(rounded[:, 1], a, first)
             vector_product(rounded[:, 3], a, second)
             if k + 3 < CYCLES:
                 prepare(k + 2)
             if k + 3 == CYCLES:
                 a5, h5, first5, second5, handed5 = cycle_of(k + 2)
-                scalar_gathers(a5, handed5)
-                scalar_gathers(a5, first5)
-                scalar_gathers(a5, second5, PACK - 1)
+                both = staged_tile([P, 2, PACK, C], F32, "both", 2)
+                scalar_gathers(a5, handed5, 1, both[:, 0])
+                scalar_gathers(a5, first5, 1, both[:, 1])
+                scalar_gathers(a5, second5, 1, staged_tile([P, PACK, C], F32, "closing", 0)[:])
             if k + 2 == CYCLES:
-                held = ring.tile([P, BANK, PACK], BF16, name="held", tag="staged", bufs=4, align_bytes=64)
-                nc.scalar.copy(as_words(held[:]), tokens(PASSES - 1, HALVES - 1))
-            codes = keep.tile([P, 4 * BANK], U32, name="codes%d" % k, align_bytes=64)
+                held = staged_tile([P, BANK, PACK], BF16, "held", 1)
+                nc.scalar.copy(as_words(held[:]), by_runs(raw[PASSES - 1, HALVES - 1][:]))
+            if k < 4:
+                codes = keep.tile([P, 4 * BANK], U32, name="codes%d" % k, align_bytes=64)
+            else:
+                codes = placed([P, 4 * BANK], U32, "codes%d" % k, k - 4)
             scales = keep.tile([P, 4 * BANK], U8, name="scales%d" % k, align_bytes=64)
             flat = rounded[:].rearrange("p n c j -> p (n c j)")
             if last:

@@ -28,6 +28,9 @@ GROUP = 16
 
 RUN = 4
 PAD = 16
+REST = 80
+BLOCKS = 16
+WINDOW = 4 * (T + PAD)
 COPY = mybir.ActivationFunctionType.Copy
 CYCLES = PASSES * HALVES
 ON_VECTOR = 4
@@ -41,17 +44,18 @@ def tile_moe_bds_lin_none_kernel(tc, dyT, w_words, w_scales, gate, offs, pos1, p
         ring = ctx.enter_context(tc.tile_pool(name="ring", bufs=2))
         slide = ctx.enter_context(tc.tile_pool(name="slide", bufs=1))
         stage = ctx.enter_context(tc.tile_pool(name="stage", bufs=1))
+        panes = ctx.enter_context(tc.tile_pool(name="panes", bufs=1))
         psum = ctx.enter_context(tc.psum_pool(name="psum", bufs=1))
 
         offs_sb = keep.tile([P, S // GROUP], U16, name="offs_sb")
         pos_sb = [keep.tile([P, T // GROUP], U16, name="pos_sb%d" % r) for r in range(3)]
         gate_sb = keep.tile([P, (E - ON_VECTOR) * C], F32, name="gate_sb")
-        gate_col = keep.tile([P, ON_VECTOR, RUN], F32, name="gate_col")
+        gate_rows = keep.tile([P, P], F32, name="gate_rows")
+        gate_col = keep.tile([P, BLOCKS], F32, name="gate_col")
         ident = keep.tile([P, P], F32, name="ident")
         words = keep.tile([P, (E + 1) * PASSES, 2 * K], U8, name="words", align_bytes=64)
         wscale = keep.tile([P, (E + 1) * PASSES, K], U8, name="wscale", align_bytes=64)
         dx = keep.tile([P, S], F32, name="dx")
-        ds = keep.tile([P, BANK], F32, name="ds")
 
         def bank(b):
             return psum.tile([P, BANK], F32, name="bank", tag="bank%d" % b, bufs=1)
@@ -61,7 +65,7 @@ def tile_moe_bds_lin_none_kernel(tc, dyT, w_words, w_scales, gate, offs, pos1, p
         window = {}
 
         def load_plane(a, j):
-            window[a, j] = ring.tile([P, T + PAD], F32, name="window", tag="window", bufs=2 * PACK)
+            window[a, j] = panes.tile([P, T + PAD], F32, name="window%d_%d" % (a, j), offset=(a % 2 * PACK + j) * WINDOW)
             nc.sync.dma_start(window[a, j][:, 0:T], rows[a, :, j, :])
 
         raw = {}
@@ -76,18 +80,21 @@ def tile_moe_bds_lin_none_kernel(tc, dyT, w_words, w_scales, gate, offs, pos1, p
                 raw[a, h] = ring.tile([P, PACK, BANK], F32, name="raw", tag="raw", bufs=2)
             nc.sync.dma_start(raw[a, h][:], rows[a, :, :, h * BANK : (h + 1) * BANK])
 
+        nc.vector.memset(gate_rows[:], 0.0)
         nc.vector.memset(wscale[:].rearrange("p m k -> p (m k)").bitcast(I32), 0)
         make_identity(nc, ident[:])
 
         load_plane(0, 0)
         nc.sync.dma_start(offs_sb[:], offs)
         load_plane(0, 1)
+        by_block = gate[0, :].rearrange("(b s) -> b s", s=P)
+        for h in range(HALVES):
+            nc.sync.dma_start(gate_rows[8 * h : 8 * h + 8, :], by_block[16 * h : 16 * h + 8, :])
         load_raw(0, 0)
         load_plane(0, 2)
         load_raw(0, 1)
         load_plane(0, 3)
-        nc.sync.dma_start(gate_sb[:], gate[0:P, ON_VECTOR * C : S])
-        nc.sync.dma_start(gate_col[:], gate[0, 0 : ON_VECTOR * C].rearrange("(e p i) -> p e i", p=P, i=RUN))
+        nc.sync.dma_start(gate_sb[:], gate[0:P, 2 * C : 4 * C])
         load_plane(1, 0)
         load_plane(1, 1)
         load_raw(1, 0)
@@ -100,10 +107,14 @@ def tile_moe_bds_lin_none_kernel(tc, dyT, w_words, w_scales, gate, offs, pos1, p
         for tile, src in zip(pos_sb, (pos1, pos2, pos3)):
             nc.sync.dma_start(tile[:], src)
 
-        gate_bank = [bank(e) for e in range(ON_VECTOR)]
-        for e in range(ON_VECTOR):
-            for i in range(RUN):
-                nc.tensor.transpose(gate_bank[e][:, i * P : (i + 1) * P], gate_col[:, e, i : i + 1].to_broadcast([P, P]), ident[:])
+        turned = bank(7)
+        nc.tensor.transpose(turned[:, 0:P], gate_rows[:], ident[:])
+        nc.vector.tensor_copy(gate_col[:], turned[:, 0:BLOCKS])
+        gate_bank = {e: bank(n) for n, e in enumerate((0, 1, 4, 5))}
+        for n, e in enumerate(gate_bank):
+            for b in range(C // P):
+                column = gate_col[:, n * C // P + b : n * C // P + b + 1]
+                nc.tensor.transpose(gate_bank[e][:, b * P : (b + 1) * P], column.to_broadcast([P, P]), ident[:])
 
         def looked_up(a, j, e, experts=1):
             return window[a, j][:].indirect(offs_sb[:, e * C // GROUP : (e + experts) * C // GROUP])
@@ -127,23 +138,28 @@ def tile_moe_bds_lin_none_kernel(tc, dyT, w_words, w_scales, gate, offs, pos1, p
 
 
         def placed(shape, dtype, name, step):
-            return slide.tile(shape, dtype, name=name, offset=step * PIECE, align_bytes=64)
+            return slide.tile(shape, dtype, name=name, offset=step * 1024, align_bytes=64)
 
         def vector_gathers(*cycles):
             pieces = [(cycle_of(k)[0], cycle_of(k)[4]) for k in cycles]
             for k, piece in zip(cycles, pieces):
-                staged[piece] = placed([P, PACK, C], F32, "handed%d" % k, k - 2 if k >= 2 else CYCLES - 1 + k)[:]
+                staged[piece] = placed([P, PACK, C], F32, "handed%d" % k, [18, 26, 16, 26, 16][k])[:]
             for j in range(PACK):
                 for a, e in pieces:
                     nc.vector.tensor_copy(staged[a, e][:, j, :], looked_up(a, j, e))
 
         def vector_product(dst, a, e):
-            gates = gate_bank[e][:].rearrange("p (i c) -> p c i", i=RUN)
+            gates = gate_bank[e][:].rearrange("p (c i) -> p c i", i=RUN)
             nc.vector.tensor_tensor(as_words(dst), by_runs(staged[a, e]), over_planes(gates), MULT)
 
-        def gpsimd_product(dst, a, e):
-            gates = gate_sb[:, (e - ON_VECTOR) * C : (e - ON_VECTOR + 1) * C].unsqueeze(2).to_broadcast([P, C, PACK])
-            nc.gpsimd.tensor_tensor(dst, staged[a, e].rearrange("p j c -> p c j"), gates, MULT)
+        def gpsimd_product(dst, a, e, cols):
+            gates = gate_sb[:, (e - 2) * C : (e - 2) * C + cols].unsqueeze(2).to_broadcast([P, cols, PACK])
+            nc.gpsimd.tensor_tensor(dst[:, 0:cols, :], staged[a, e][:, :, 0:cols].rearrange("p j c -> p c j"), gates, MULT)
+
+        def vector_rest(dst, a, e):
+            gates = gate_sb[:, (e - 1) * C - REST : (e - 1) * C].rearrange("p (c i) -> p c i", i=RUN)
+            gates = gates.unsqueeze(2).to_broadcast([P, REST // RUN, PACK, RUN])
+            nc.vector.tensor_tensor(as_words(dst[:, C - REST : C, :]), by_runs(staged[a, e][:, :, C - REST : C]), gates, MULT)
 
         quantised = {}
 
@@ -158,7 +174,7 @@ def tile_moe_bds_lin_none_kernel(tc, dyT, w_words, w_scales, gate, offs, pos1, p
             for n, (a, g) in enumerate(pieces):
                 quantised[a, g] = (codes[:, n * BANK : (n + 1) * BANK], scales[:, n * BANK : (n + 1) * BANK])
 
-        bank_of = {E: 4, E + 1: 5, 0: 6, 4: 7, 1: 0, 2: 1, 5: 2, 3: 3}
+        bank_of = {E: 4, E + 1: 5, 0: 6, 2: 7, 1: 1, 4: 0, 3: 2, 5: 3}
         sums = {}
 
         def multiply(a, g):
@@ -175,9 +191,8 @@ def tile_moe_bds_lin_none_kernel(tc, dyT, w_words, w_scales, gate, offs, pos1, p
                 start=(a == 0),
                 stop=(a == PASSES - 1),
             )
-            if a == PASSES - 1 and g <= E:
-                dst = dx[:, g * C : (g + 1) * C] if g < E else ds[:]
-                nc.scalar.copy(dst, sums[g][:])
+            if a == PASSES - 1 and g < E:
+                nc.scalar.copy(dx[:, g * C : (g + 1) * C], sums[g][:])
 
         def multiply_ready(a, groups):
             for g in groups:
@@ -189,7 +204,7 @@ def tile_moe_bds_lin_none_kernel(tc, dyT, w_words, w_scales, gate, offs, pos1, p
 
         def cycle_of(k):
             a, h = divmod(k, HALVES)
-            return a, h, 2 * h, 2 * h + 1, ON_VECTOR + h
+            return a, h, 4 * h, 4 * h + 1, 2 + h
 
         def prepare(k):
             a, h, first, second, handed = cycle_of(k)
@@ -201,14 +216,14 @@ def tile_moe_bds_lin_none_kernel(tc, dyT, w_words, w_scales, gate, offs, pos1, p
         for k in range(CYCLES):
             a, h, first, second, handed = cycle_of(k)
             last = k == CYCLES - 1
-            rounded = placed([P, 4, BANK, PACK], BF16, "rounded%d" % k, k)
+            rounded = placed([P, 4, BANK, PACK], BF16, "rounded%d" % k, 0)
             shared = divmod(k + 1, HALVES) if k + 2 < CYCLES else None
             if k == 0:
                 extra = keep.tile([P, BANK, PACK], BF16, name="extra", align_bytes=64)
                 gpsimd_round(extra[:], 0, 0)
             if shared:
                 gpsimd_round(rounded[:, 2], *shared)
-            gpsimd_product(rounded[:, 0], a, handed)
+            gpsimd_product(rounded[:, 0], a, handed, C if shared else C - REST)
             if k == 0:
                 prepare(1)
             if 0 < k < CYCLES - 2:
@@ -216,23 +231,27 @@ def tile_moe_bds_lin_none_kernel(tc, dyT, w_words, w_scales, gate, offs, pos1, p
             if k == 1:
                 for j in range(PACK):
                     load_plane(2, j)
-            vector_product(rounded[:, 1], a, first)
+            if last:
+                vector_product(rounded[:, 1], a, first)
             vector_product(rounded[:, 3], a, second)
+            if not last:
+                vector_product(rounded[:, 1], a, first)
+            if not shared:
+                vector_rest(rounded[:, 0], a, handed)
             if k + 3 < CYCLES:
                 prepare(k + 2)
             if k + 3 == CYCLES:
-                a5, h5, first5, second5, handed5 = cycle_of(k + 2)
-                both = staged_tile([P, 2, PACK, C], F32, "both", 2)
-                scalar_gathers(a5, handed5, 1, both[:, 0])
-                scalar_gathers(a5, first5, 1, both[:, 1])
-                scalar_gathers(a5, second5, 1, staged_tile([P, PACK, C], F32, "closing", 0)[:])
+                scalar_gathers(PASSES - 1, 3, 2, staged_tile([P, PACK, 2 * C], F32, "both", 2))
+                scalar_gathers(PASSES - 1, E - 1, 1, staged_tile([P, PACK, C], F32, "closing", 0)[:])
             if k + 2 == CYCLES:
                 held = staged_tile([P, BANK, PACK], BF16, "held", 1)
                 nc.scalar.copy(as_words(held[:]), by_runs(raw[PASSES - 1, HALVES - 1][:]))
+                ds = panes.tile([P, BANK], F32, name="ds", offset=(PACK - 1) * WINDOW)
+                nc.scalar.copy(ds[:], sums[E][:])
             if k < 4:
                 codes = keep.tile([P, 4 * BANK], U32, name="codes%d" % k, align_bytes=64)
             else:
-                codes = placed([P, 4 * BANK], U32, "codes%d" % k, k - 4)
+                codes = placed([P, 4 * BANK], U32, "codes%d" % k, 34 + 8 * (k - 4))
             scales = keep.tile([P, 4 * BANK], U8, name="scales%d" % k, align_bytes=64)
             flat = rounded[:].rearrange("p n c j -> p (n c j)")
             if last:
@@ -241,7 +260,7 @@ def tile_moe_bds_lin_none_kernel(tc, dyT, w_words, w_scales, gate, offs, pos1, p
             else:
                 quantise([(a, handed), (a, first)], flat[:, 0 : 2 * width], codes[:, 0 : 2 * BANK], scales[:, 0 : 2 * BANK])
             if k == 0:
-                extra_codes = placed([P, BANK], U32, "extra_codes", CYCLES - 1)
+                extra_codes = placed([P, BANK], U32, "extra_codes", 24)
                 extra_scales = keep.tile([P, BANK], U8, name="extra_scales", align_bytes=64)
                 quantise([(0, E)], extra[:].rearrange("p c j -> p (c j)"), extra_codes[:], extra_scales[:])
                 multiply(0, E)
@@ -252,11 +271,11 @@ def tile_moe_bds_lin_none_kernel(tc, dyT, w_words, w_scales, gate, offs, pos1, p
                 quantise([(a, second)], flat[:, 3 * width :], codes[:, 3 * BANK :], scales[:, 3 * BANK :])
             multiply_ready(a, [handed, first, second])
             if last:
-                held_codes = placed([P, BANK], U32, "held_codes", k)
+                held_codes = placed([P, BANK], U32, "held_codes", 0)
                 quantise([(a, E + h)], held[:].rearrange("p c j -> p (c j)"), held_codes[:], scales[:, 2 * BANK : 3 * BANK])
                 multiply(a, E + h)
 
-        pairs = [placed([P, 2, T], F32, "pair%d" % n, n) for n in range(3)]
+        pairs = [placed([P, 2, T], F32, "pair%d" % n, 16 + 8 * n) for n in range(3)]
         first_sum, second_sum, total = pairs[0][:, 0], pairs[0][:, 1], pairs[1][:, 0]
         fetched = [pairs[2][:, 0], pairs[2][:, 1]]
 

@@ -244,8 +244,6 @@ def tile_moe_bds_lin_none_kernel(tc, dyT, w_words, w_scales, gate, offs, pos1, p
                 scalar_gathers(PASSES - 1, 3, 2, staged_tile([P, PACK, 2 * C], F32, "both", 2))
                 scalar_gathers(PASSES - 1, E - 1, 1, staged_tile([P, PACK, C], F32, "closing", 0)[:])
             if k + 2 == CYCLES:
-                held = staged_tile([P, BANK, PACK], BF16, "held", 1)
-                nc.scalar.copy(as_words(held[:]), by_runs(raw[PASSES - 1, HALVES - 1][:]))
                 ds = panes.tile([P, BANK], F32, name="ds", offset=(PACK - 1) * WINDOW)
                 nc.scalar.copy(ds[:], sums[E][:])
             if k < 4:
@@ -272,6 +270,8 @@ def tile_moe_bds_lin_none_kernel(tc, dyT, w_words, w_scales, gate, offs, pos1, p
             multiply_ready(a, [handed, first, second])
             if last:
                 held_codes = placed([P, BANK], U32, "held_codes", 0)
+                held = placed([P, BANK, PACK], BF16, "held", 4)
+                nc.vector.tensor_copy(as_words(held[:]), by_runs(raw[a, h][:]))
                 quantise([(a, E + h)], held[:].rearrange("p c j -> p (c j)"), held_codes[:], scales[:, 2 * BANK : 3 * BANK])
                 multiply(a, E + h)
 

@@ -29,6 +29,7 @@ GROUP = 16
 RUN = 4
 PAD = 16
 REST = 80
+TAIL = 128
 BLOCKS = 16
 WINDOW = 4 * (T + PAD)
 COPY = mybir.ActivationFunctionType.Copy
@@ -125,9 +126,6 @@ def tile_moe_bds_lin_none_kernel(tc, dyT, w_words, w_scales, gate, offs, pos1, p
         def as_words(ap):
             return ap.rearrange("p (c i) j -> p c j i", i=RUN)
 
-        def over_planes(ap):
-            return ap.unsqueeze(2).to_broadcast([P, C // RUN, PACK, RUN])
-
         staged = {}
 
         def scalar_gathers(a, e, experts, tile):
@@ -148,18 +146,13 @@ def tile_moe_bds_lin_none_kernel(tc, dyT, w_words, w_scales, gate, offs, pos1, p
                 for a, e in pieces:
                     nc.vector.tensor_copy(staged[a, e][:, j, :], looked_up(a, j, e))
 
-        def vector_product(dst, a, e):
-            gates = gate_bank[e][:].rearrange("p (c i) -> p c i", i=RUN)
-            nc.vector.tensor_tensor(as_words(dst), by_runs(staged[a, e]), over_planes(gates), MULT)
+        def vector_product(dst, src, gates):
+            runs = gates.rearrange("p (c i) -> p c i", i=RUN)
+            nc.vector.tensor_tensor(as_words(dst), by_runs(src), runs.unsqueeze(2).to_broadcast([P, runs.shape[1], PACK, RUN]), MULT)
 
         def gpsimd_product(dst, a, e, cols):
             gates = gate_sb[:, (e - 2) * C : (e - 2) * C + cols].unsqueeze(2).to_broadcast([P, cols, PACK])
             nc.gpsimd.tensor_tensor(dst[:, 0:cols, :], staged[a, e][:, :, 0:cols].rearrange("p j c -> p c j"), gates, MULT)
-
-        def vector_rest(dst, a, e):
-            gates = gate_sb[:, (e - 1) * C - REST : (e - 1) * C].rearrange("p (c i) -> p c i", i=RUN)
-            gates = gates.unsqueeze(2).to_broadcast([P, REST // RUN, PACK, RUN])
-            nc.vector.tensor_tensor(as_words(dst[:, C - REST : C, :]), by_runs(staged[a, e][:, :, C - REST : C]), gates, MULT)
 
         quantised = {}
 
@@ -232,17 +225,25 @@ def tile_moe_bds_lin_none_kernel(tc, dyT, w_words, w_scales, gate, offs, pos1, p
                 for j in range(PACK):
                     load_plane(2, j)
             if last:
-                vector_product(rounded[:, 1], a, first)
-            vector_product(rounded[:, 3], a, second)
-            if not last:
-                vector_product(rounded[:, 1], a, first)
+                vector_product(rounded[:, 1], staged[a, first], gate_bank[first][:])
+                for tile, c0, c1 in closing:
+                    vector_product(rounded[:, 3, c0:c1, :], tile[:], gate_bank[second][:, c0:c1])
+            else:
+                vector_product(rounded[:, 3], staged[a, second], gate_bank[second][:])
+                vector_product(rounded[:, 1], staged[a, first], gate_bank[first][:])
             if not shared:
-                vector_rest(rounded[:, 0], a, handed)
+                vector_product(rounded[:, 0, C - REST : C, :], staged[a, handed][:, :, C - REST : C], gate_sb[:, (handed - 1) * C - REST : (handed - 1) * C])
             if k + 3 < CYCLES:
                 prepare(k + 2)
             if k + 3 == CYCLES:
                 scalar_gathers(PASSES - 1, 3, 2, staged_tile([P, PACK, 2 * C], F32, "both", 2))
-                scalar_gathers(PASSES - 1, E - 1, 1, staged_tile([P, PACK, C], F32, "closing", 0)[:])
+                closing = []
+                for c0, c1 in ((0, C - TAIL), (C - TAIL, C)):
+                    tile = stage.tile([P, PACK, c1 - c0], F32, name="closing%d" % c0, offset=4 * PACK * c0, align_bytes=64)
+                    closing.append((tile, c0, c1))
+                    for j in range(PACK):
+                        slots = offs_sb[:, (S - C + c0) // GROUP : (S - C + c1) // GROUP]
+                        nc.scalar.activation(tile[:, j, :], window[PASSES - 1, j][:].indirect(slots), COPY)
             if k + 2 == CYCLES:
                 ds = panes.tile([P, BANK], F32, name="ds", offset=(PACK - 1) * WINDOW)
                 nc.scalar.copy(ds[:], sums[E][:])

@@ -18,107 +18,123 @@ E5M2X4 = mybir.dt.float8_e5m2_x4
 E2M1X4 = mybir.dt.float4_e2m1fn_x4
 MULT = mybir.AluOpType.mult
 ADD = mybir.AluOpType.add
+COPY = mybir.ActivationFunctionType.Copy
 
 P = 128
 PACK = 4
 PASSES = N // (P * PACK)
 BANK = 512
-HALVES = T // BANK
 GROUP = 16
-
+BLOCKS = S // P
 RUN = 4
 PAD = 16
-REST = 80
-TAIL = 128
-BLOCKS = 16
-WINDOW = 4 * (T + PAD)
-COPY = mybir.ActivationFunctionType.Copy
-CYCLES = PASSES * HALVES
-ON_VECTOR = 4
+CYCLES = 2 * PASSES
 PIECE = 4 * PACK * C
+HANDED = [(2, 0), (3, 0), (2, 1), (3, 1), (2, 2), (3, 2)]
+REST = [64, 0, 0, 0, 88, 160]
+SHARED = [(0, 0), (1, 0), (1, 1), (2, 0)]
+HALF = C // 2
+LAP = 64
+PLACE = [0, 6 * PIECE + LAP, 4 * PIECE + LAP, 6 * PIECE + LAP, LAP, 4 * PIECE + LAP, 6 * PIECE + LAP]
+HAND_PLACE = [3 * PIECE + LAP, 2 * PIECE, 3 * PIECE + LAP, 2 * PIECE + LAP, 3 * PIECE + LAP]
+CUT = T
 
 
 def tile_moe_bds_lin_none_kernel(tc, dyT, w_words, w_scales, gate, offs, pos1, pos2, pos3, out):
     nc = tc.nc
     with ExitStack() as ctx:
         keep = ctx.enter_context(tc.tile_pool(name="keep", bufs=1))
-        ring = ctx.enter_context(tc.tile_pool(name="ring", bufs=2))
-        slide = ctx.enter_context(tc.tile_pool(name="slide", bufs=1))
+        ring = ctx.enter_context(tc.tile_pool(name="ring", bufs=3))
+        work = ctx.enter_context(tc.tile_pool(name="work", bufs=1))
         stage = ctx.enter_context(tc.tile_pool(name="stage", bufs=1))
-        panes = ctx.enter_context(tc.tile_pool(name="panes", bufs=1))
         psum = ctx.enter_context(tc.psum_pool(name="psum", bufs=1))
 
         offs_sb = keep.tile([P, S // GROUP], U16, name="offs_sb")
         pos_sb = [keep.tile([P, T // GROUP], U16, name="pos_sb%d" % r) for r in range(3)]
-        gate_sb = keep.tile([P, (E - ON_VECTOR) * C], F32, name="gate_sb")
-        gate_rows = keep.tile([P, P], F32, name="gate_rows")
+        gate_sb = {e: keep.tile([P, C], F32, name="gate_sb%d" % e) for e in (2, 3)}
+        gate_rows = stage.tile([P, P], F32, name="gate_rows", offset=HAND_PLACE[1] + LAP, align_bytes=64)
         gate_col = keep.tile([P, BLOCKS], F32, name="gate_col")
         ident = keep.tile([P, P], F32, name="ident")
         words = keep.tile([P, (E + 1) * PASSES, 2 * K], U8, name="words", align_bytes=64)
         wscale = keep.tile([P, (E + 1) * PASSES, K], U8, name="wscale", align_bytes=64)
         dx = keep.tile([P, S], F32, name="dx")
+        opening = keep.tile([P, PACK, T], F32, name="opening")
+        window = {(a, j): keep.tile([P, T + PAD], F32, name="window%d_%d" % (a, j)) for a in (1, 2) for j in range(PACK)}
+        raw = {(a, h): keep.tile([P, PACK, BANK], F32, name="raw%d_%d" % (a, h))[:] for a in (1, 2) for h in range(2)}
+        for h in range(2):
+            raw[0, h] = opening[:, :, h * BANK : (h + 1) * BANK]
 
-        def bank(b):
-            return psum.tile([P, BANK], F32, name="bank", tag="bank%d" % b, bufs=1)
+        def bank(b, cols=BANK):
+            return psum.tile([P, cols], F32, name="bank", tag="bank%d" % b, bufs=1)
+
+        def staged_tile(shape, dtype, name, slot, at=0):
+            return stage.tile(shape, dtype, name=name, offset=PLACE[slot] + at, align_bytes=64)
+
+        def work_tile(shape, dtype, name, at):
+            return work.tile(shape, dtype, name=name, offset=at, align_bytes=64)
 
         rows = dyT.rearrange("(a p j) t -> a p j t", p=P, j=PACK)
 
-        window = {}
-
-        def load_plane(a, j):
-            window[a, j] = panes.tile([P, T + PAD], F32, name="window%d_%d" % (a, j), offset=(a % 2 * PACK + j) * WINDOW)
-            nc.sync.dma_start(window[a, j][:, 0:T], rows[a, :, j, :])
-
-        raw = {}
-
-        def staged_tile(shape, dtype, name, slot):
-            return stage.tile(shape, dtype, name=name, offset=slot * 2 * PIECE, align_bytes=64)
+        def load_windows(a):
+            for j in range(PACK):
+                nc.sync.dma_start(window[a, j][:, 0:T], rows[a, :, j, :])
 
         def load_raw(a, h):
-            if a == 0:
-                raw[a, h] = stage.tile([P, PACK, BANK], F32, name="raw%d" % h, offset=(2 - h) * 2 * PIECE, align_bytes=64)
-            else:
-                raw[a, h] = ring.tile([P, PACK, BANK], F32, name="raw", tag="raw", bufs=2)
-            nc.sync.dma_start(raw[a, h][:], rows[a, :, :, h * BANK : (h + 1) * BANK])
+            nc.sync.dma_start(raw[a, h], rows[a, :, :, h * BANK : (h + 1) * BANK])
 
-        nc.vector.memset(gate_rows[:], 0.0)
+        def load_gate(e):
+            nc.sync.dma_start(gate_sb[e][:], gate[0:P, e * C : (e + 1) * C])
+
+        nought = keep.tile([P, 1], F32, name="nought")
+        nc.vector.memset(nought[:], 0.0)
+        nc.scalar.activation(gate_rows[:], nought[:].to_broadcast([P, P]), COPY)
         nc.vector.memset(wscale[:].rearrange("p m k -> p (m k)").bitcast(I32), 0)
         make_identity(nc, ident[:])
 
-        load_plane(0, 0)
+        nc.sync.dma_start(opening[:, 0, :], rows[0, :, 0, :])
         nc.sync.dma_start(offs_sb[:], offs)
-        load_plane(0, 1)
-        by_block = gate[0, :].rearrange("(b s) -> b s", s=P)
-        for h in range(HALVES):
-            nc.sync.dma_start(gate_rows[8 * h : 8 * h + 8, :], by_block[16 * h : 16 * h + 8, :])
-        load_raw(0, 0)
-        load_plane(0, 2)
-        load_raw(0, 1)
-        load_plane(0, 3)
-        nc.sync.dma_start(gate_sb[:], gate[0:P, 2 * C : 4 * C])
-        load_plane(1, 0)
-        load_plane(1, 1)
+        nc.sync.dma_start(opening[:, 1, :], rows[0, :, 1, :])
+        nc.sync.dma_start(gate_rows[0:BLOCKS, :], gate[0, :].rearrange("(b s) -> b s", s=P))
+        for j in range(2, PACK):
+            nc.sync.dma_start(opening[:, j, :], rows[0, :, j, :])
+        load_gate(2)
+        load_windows(1)
+        load_windows(2)
         load_raw(1, 0)
-        load_plane(1, 2)
-        load_plane(1, 3)
+        load_gate(3)
+        load_raw(1, 1)
+        load_raw(2, 0)
         nc.sync.dma_start(words[:].bitcast(I32), w_words.rearrange("e a p b -> p (e a) b").bitcast(I32))
         scale_rows = w_scales.rearrange("e a f k -> f (e a) k")
         for q in range(4):
             nc.sync.dma_start(wscale[32 * q : 32 * q + 4, :, :].bitcast(I32), scale_rows[4 * q : 4 * q + 4, :, :].bitcast(I32))
+        load_raw(2, 1)
         for tile, src in zip(pos_sb, (pos1, pos2, pos3)):
             nc.sync.dma_start(tile[:], src)
 
-        turned = bank(7)
+        turned = bank(5)
         nc.tensor.transpose(turned[:, 0:P], gate_rows[:], ident[:])
         nc.vector.tensor_copy(gate_col[:], turned[:, 0:BLOCKS])
-        gate_bank = {e: bank(n) for n, e in enumerate((0, 1, 4, 5))}
-        for n, e in enumerate(gate_bank):
-            for b in range(C // P):
-                column = gate_col[:, n * C // P + b : n * C // P + b + 1]
-                nc.tensor.transpose(gate_bank[e][:, b * P : (b + 1) * P], column.to_broadcast([P, P]), ident[:])
 
-        def looked_up(a, j, e, experts=1):
-            return window[a, j][:].indirect(offs_sb[:, e * C // GROUP : (e + experts) * C // GROUP])
+        def spread_gates(tile, blocks):
+            for n, b in enumerate(blocks):
+                nc.tensor.transpose(tile[:, n * P : (n + 1) * P], gate_col[:, b : b + 1].to_broadcast([P, P]), ident[:])
+
+        gate_bank = {}
+
+        def make_gates(first):
+            for n in range(2):
+                gate_bank[first + n] = bank(n)
+                spread_gates(gate_bank[first + n], range((first + n) * C // P, (first + n + 1) * C // P))
+
+        make_gates(0)
+        rest_bank = bank(7)
+        spread_gates(rest_bank, (3 * C // P - 1, 4 * C // P - 2, 4 * C // P - 1))
+        rest_end = {2: P, 3: 3 * P}
+
+        def looked_up(a, j, s0, s1):
+            table = opening[:, j, :] if a == 0 else window[a, j][:]
+            return table.indirect(offs_sb[:, s0 // GROUP : s1 // GROUP])
 
         def by_runs(ap):
             return ap.rearrange("p j (c i) -> p c j i", i=RUN)
@@ -128,177 +144,184 @@ def tile_moe_bds_lin_none_kernel(tc, dyT, w_words, w_scales, gate, offs, pos1, p
 
         staged = {}
 
-        def scalar_gathers(a, e, experts, tile):
+        def scalar_gathers(a, e, tile):
             for j in range(PACK):
-                nc.scalar.activation(tile[:, j, :], looked_up(a, j, e, experts), COPY)
-            for n in range(experts):
-                staged[a, e + n] = tile[:, :, n * C : (n + 1) * C]
-
-
-        def placed(shape, dtype, name, step):
-            return slide.tile(shape, dtype, name=name, offset=step * 1024, align_bytes=64)
+                if a == 0:
+                    for n in range(2):
+                        nc.scalar.activation(tile[:, j, n * C : (n + 1) * C], looked_up(a, j, (e + n) * C, (e + n + 1) * C), COPY)
+                else:
+                    nc.scalar.activation(tile[:, j, :], looked_up(a, j, e * C, (e + 2) * C), COPY)
+            for n in range(2):
+                staged[e + n, a] = tile[:, :, n * C : (n + 1) * C]
 
         def vector_gathers(*cycles):
-            pieces = [(cycle_of(k)[0], cycle_of(k)[4]) for k in cycles]
-            for k, piece in zip(cycles, pieces):
-                staged[piece] = placed([P, PACK, C], F32, "handed%d" % k, [18, 26, 16, 26, 16][k])[:]
+            for k in cycles:
+                staged[HANDED[k]] = stage.tile([P, PACK, C], F32, name="handed%d" % k, offset=HAND_PLACE[k], align_bytes=64)[:]
             for j in range(PACK):
-                for a, e in pieces:
-                    nc.vector.tensor_copy(staged[a, e][:, j, :], looked_up(a, j, e))
+                for k in cycles:
+                    e, a = HANDED[k]
+                    nc.vector.tensor_copy(staged[e, a][:, j, :], looked_up(a, j, e * C, (e + 1) * C))
 
         def vector_product(dst, src, gates):
             runs = gates.rearrange("p (c i) -> p c i", i=RUN)
             nc.vector.tensor_tensor(as_words(dst), by_runs(src), runs.unsqueeze(2).to_broadcast([P, runs.shape[1], PACK, RUN]), MULT)
 
-        def gpsimd_product(dst, a, e, cols):
-            gates = gate_sb[:, (e - 2) * C : (e - 2) * C + cols].unsqueeze(2).to_broadcast([P, cols, PACK])
-            nc.gpsimd.tensor_tensor(dst[:, 0:cols, :], staged[a, e][:, :, 0:cols].rearrange("p j c -> p c j"), gates, MULT)
+        def gpsimd_product(dst, e, a, cols):
+            gates = gate_sb[e][:, 0:cols].unsqueeze(2).to_broadcast([P, cols, PACK])
+            nc.gpsimd.tensor_tensor(dst[:, 0:cols, :], staged[e, a][:, :, 0:cols].rearrange("p j c -> p c j"), gates, MULT)
+
+        def gpsimd_round(dst, a, h):
+            nc.gpsimd.tensor_scalar(dst, raw[a, h].rearrange("p j c -> p c j"), 1.0, 0.0, MULT, ADD)
 
         quantised = {}
 
-        def gpsimd_round(dst, a, h):
-            nc.gpsimd.tensor_scalar(dst, raw[a, h][:].rearrange("p j c -> p c j"), 1.0, 0.0, MULT, ADD)
-            later = divmod(HALVES * a + h + 2, HALVES)
-            if later[0] < PASSES and later != (1, 0):
-                load_raw(*later)
-
         def quantise(pieces, src, codes, scales):
-            nc.vector.quantize_mx(out=codes.bitcast(E5M2X4), scales=scales, in_=src)
-            for n, (a, g) in enumerate(pieces):
-                quantised[a, g] = (codes[:, n * BANK : (n + 1) * BANK], scales[:, n * BANK : (n + 1) * BANK])
+            nc.vector.quantize_mx(out=codes.bitcast(E5M2X4), scales=scales, in_=src.rearrange("p c j -> p (c j)"))
+            cols = src.shape[1] // len(pieces)
+            for n, piece in enumerate(pieces):
+                quantised[piece] = (codes[:, n * cols : (n + 1) * cols], scales[:, n * cols : (n + 1) * cols])
 
-        bank_of = {E: 4, E + 1: 5, 0: 6, 2: 7, 1: 1, 4: 0, 3: 2, 5: 3}
+        bank_of = {0: 2, 1: 3, 2: 4, 3: 5, 4: 2, 5: 3, E: 6, E + 1: 7}
         sums = {}
 
-        def multiply(a, g):
+        def multiply(g, a, c0=0, c1=BANK):
             if a == 0:
                 sums[g] = bank(bank_of[g])
             e = min(g, E)
-            codes, scales = quantised[a, g]
+            codes, scales = quantised[g, a]
+            closes = a == PASSES - 1 and c1 == BANK
             nc.tensor.matmul_mx(
-                out=sums[g][:],
+                out=sums[g][:, c0:c1],
                 lhsT=words[:, e * PASSES + a, :].bitcast(E2M1X4),
                 lhsT_scale=wscale[:, e * PASSES + a, :],
                 rhs=codes.bitcast(E5M2X4),
                 rhs_scale=scales,
                 start=(a == 0),
-                stop=(a == PASSES - 1),
+                stop=closes,
             )
-            if a == PASSES - 1 and g < E:
+            if closes and g < E:
                 nc.scalar.copy(dx[:, g * C : (g + 1) * C], sums[g][:])
 
-        def multiply_ready(a, groups):
-            for g in groups:
-                if bank_of[g] >= ON_VECTOR:
-                    multiply(a, g)
-                elif a == PASSES - 1:
-                    for earlier in range(PASSES):
-                        multiply(earlier, g)
-
-        def cycle_of(k):
-            a, h = divmod(k, HALVES)
-            return a, h, 4 * h, 4 * h + 1, 2 + h
+        def pair_of(k):
+            return 4 * (k // PASSES), k % PASSES
 
         def prepare(k):
-            a, h, first, second, handed = cycle_of(k)
-            scalar_gathers(a, first, 2, staged_tile([P, PACK, 2 * C], F32, "staged%d" % k, k % 3))
+            e, a = pair_of(k)
+            scalar_gathers(a, e, staged_tile([P, PACK, 2 * C], F32, "staged%d" % k, k))
+
+        def products(k, rounded, second_cols):
+            e, a = pair_of(k)
+            handed = HANDED[k]
+            rest = REST[k]
+            if k < CYCLES - 1:
+                vector_product(rounded[:, 3], staged[e + 1, a], gate_bank[e + 1][:])
+            vector_product(rounded[:, 1], staged[e, a], gate_bank[e][:])
+            if rest:
+                end = rest_end[handed[0]]
+                vector_product(rounded[:, 0, C - rest : C, :], staged[handed][:, :, C - rest : C], rest_bank[:, end - rest : end])
 
         prepare(0)
         vector_gathers(0, 1)
-        width = BANK * PACK
-        for k in range(CYCLES):
-            a, h, first, second, handed = cycle_of(k)
-            last = k == CYCLES - 1
-            rounded = placed([P, 4, BANK, PACK], BF16, "rounded%d" % k, 0)
-            shared = divmod(k + 1, HALVES) if k + 2 < CYCLES else None
+        prepare(1)
+        prepare(2)
+        for k in range(CYCLES - 1):
+            e, a = pair_of(k)
+            rounded = work_tile([P, 4, BANK, PACK], BF16, "rounded%d" % k, 0)
             if k == 0:
                 extra = keep.tile([P, BANK, PACK], BF16, name="extra", align_bytes=64)
-                gpsimd_round(extra[:], 0, 0)
-            if shared:
-                gpsimd_round(rounded[:, 2], *shared)
-            gpsimd_product(rounded[:, 0], a, handed, C if shared else C - REST)
-            if k == 0:
-                prepare(1)
+                gpsimd_round(extra[:], 0, 1)
+            if k < len(SHARED):
+                gpsimd_round(rounded[:, 2], *SHARED[k])
+            gpsimd_product(rounded[:, 0], *HANDED[k], C - REST[k])
             if 0 < k < CYCLES - 2:
                 vector_gathers(k + 1)
-            if k == 1:
-                for j in range(PACK):
-                    load_plane(2, j)
-            if last:
-                vector_product(rounded[:, 1], staged[a, first], gate_bank[first][:])
-                for tile, c0, c1 in closing:
-                    vector_product(rounded[:, 3, c0:c1, :], tile[:], gate_bank[second][:, c0:c1])
-            else:
-                vector_product(rounded[:, 3], staged[a, second], gate_bank[second][:])
-                vector_product(rounded[:, 1], staged[a, first], gate_bank[first][:])
-            if not shared:
-                vector_product(rounded[:, 0, C - REST : C, :], staged[a, handed][:, :, C - REST : C], gate_sb[:, (handed - 1) * C - REST : (handed - 1) * C])
-            if k + 3 < CYCLES:
-                prepare(k + 2)
+            products(k, rounded, C)
+            if k == PASSES - 1:
+                make_gates(4)
+            if k + 3 < CYCLES - 1:
+                prepare(k + 3)
             if k + 3 == CYCLES:
-                scalar_gathers(PASSES - 1, 3, 2, staged_tile([P, PACK, 2 * C], F32, "both", 2))
-                closing = []
-                for c0, c1 in ((0, C - TAIL), (C - TAIL, C)):
-                    tile = stage.tile([P, PACK, c1 - c0], F32, name="closing%d" % c0, offset=4 * PACK * c0, align_bytes=64)
-                    closing.append((tile, c0, c1))
+                closing = [staged_tile([P, PACK, HALF], F32, "closing%d" % n, 6, n * PIECE // 2) for n in range(2)]
+                for n in range(2):
                     for j in range(PACK):
-                        slots = offs_sb[:, (S - C + c0) // GROUP : (S - C + c1) // GROUP]
-                        nc.scalar.activation(tile[:, j, :], window[PASSES - 1, j][:].indirect(slots), COPY)
-            if k + 2 == CYCLES:
-                ds = panes.tile([P, BANK], F32, name="ds", offset=(PACK - 1) * WINDOW)
-                nc.scalar.copy(ds[:], sums[E][:])
-            if k < 4:
-                codes = keep.tile([P, 4 * BANK], U32, name="codes%d" % k, align_bytes=64)
-            else:
-                codes = placed([P, 4 * BANK], U32, "codes%d" % k, 34 + 8 * (k - 4))
-            scales = keep.tile([P, 4 * BANK], U8, name="scales%d" % k, align_bytes=64)
-            flat = rounded[:].rearrange("p n c j -> p (n c j)")
-            if last:
-                for n, g in enumerate((handed, first)):
-                    quantise([(a, g)], flat[:, n * width : (n + 1) * width], codes[:, n * BANK : (n + 1) * BANK], scales[:, n * BANK : (n + 1) * BANK])
-            else:
-                quantise([(a, handed), (a, first)], flat[:, 0 : 2 * width], codes[:, 0 : 2 * BANK], scales[:, 0 : 2 * BANK])
+                        nc.scalar.activation(closing[n][:, j, :], looked_up(PASSES - 1, j, S - C + n * HALF, S - C + (n + 1) * HALF), COPY)
+            codes = ring.tile([P, 4 * BANK], U32, name="codes", tag="codes", bufs=3, align_bytes=64)
+            scales = ring.tile([P, 4 * BANK], U8, name="scales", tag="scales", bufs=3, align_bytes=64)
+            flat = rounded[:].rearrange("p n c j -> p (n c) j")
             if k == 0:
-                extra_codes = placed([P, BANK], U32, "extra_codes", 24)
+                extra_codes = keep.tile([P, BANK], U32, name="extra_codes", align_bytes=64)
                 extra_scales = keep.tile([P, BANK], U8, name="extra_scales", align_bytes=64)
-                quantise([(0, E)], extra[:].rearrange("p c j -> p (c j)"), extra_codes[:], extra_scales[:])
-                multiply(0, E)
-            if shared:
-                quantise([(shared[0], E + shared[1]), (a, second)], flat[:, 2 * width :], codes[:, 2 * BANK :], scales[:, 2 * BANK :])
-                multiply(shared[0], E + shared[1])
+                quantise([(E + 1, 0)], extra[:], extra_codes[:], extra_scales[:])
+            if k < len(SHARED):
+                shared = (E + SHARED[k][1], SHARED[k][0])
+                quantise([shared, (e + 1, a)], flat[:, 2 * BANK :], codes[:, 2 * BANK :], scales[:, 2 * BANK :])
+                if shared[0] == E:
+                    multiply(*shared)
             else:
-                quantise([(a, second)], flat[:, 3 * width :], codes[:, 3 * BANK :], scales[:, 3 * BANK :])
-            multiply_ready(a, [handed, first, second])
-            if last:
-                held_codes = placed([P, BANK], U32, "held_codes", 0)
-                held = placed([P, BANK, PACK], BF16, "held", 4)
-                nc.vector.tensor_copy(as_words(held[:]), by_runs(raw[a, h][:]))
-                quantise([(a, E + h)], held[:].rearrange("p c j -> p (c j)"), held_codes[:], scales[:, 2 * BANK : 3 * BANK])
-                multiply(a, E + h)
+                quantise([(e + 1, a)], flat[:, 3 * BANK :], codes[:, 3 * BANK :], scales[:, 3 * BANK :])
+            multiply(e + 1, a)
+            quantise([HANDED[k], (e, a)], flat[:, 0 : 2 * BANK], codes[:, 0 : 2 * BANK], scales[:, 0 : 2 * BANK])
+            multiply(e, a)
+            multiply(*HANDED[k])
+            if k + 3 == CYCLES - 1:
+                scalar_gathers(PASSES - 1, 3, staged_tile([P, PACK, 2 * C], F32, "both", 5))
 
-        pairs = [placed([P, 2, T], F32, "pair%d" % n, 16 + 8 * n) for n in range(3)]
-        first_sum, second_sum, total = pairs[0][:, 0], pairs[0][:, 1], pairs[1][:, 0]
-        fetched = [pairs[2][:, 0], pairs[2][:, 1]]
+        k, a = CYCLES - 1, PASSES - 1
+        rounded = work_tile([P, 4, BANK, PACK], BF16, "rounded%d" % k, 0)
+        gpsimd_product(rounded[:, 0], *HANDED[k], C - REST[k])
+        products(k, rounded, HALF)
+        vector_product(rounded[:, 3, 0:HALF, :], closing[0][:], gate_bank[5][:, 0:HALF])
+        for earlier in range(a):
+            multiply(E + 1, earlier)
+        codes = staged_tile([P, 4 * BANK], U32, "last_codes", 5)
+        late = staged_tile([P, HALF, PACK], BF16, "late", 5, PIECE)
+        held = [staged_tile([P, HALF, PACK], BF16, "held%d" % n, 5, PIECE + (n + 1) * PIECE // 4) for n in range(2)]
+        scales = keep.tile([P, 4 * BANK], U8, name="last_scales", align_bytes=64)
 
-        def slots_of(r, t0, t1):
-            return dx[:].indirect(pos_sb[r][:, t0 // GROUP : t1 // GROUP])
+        def last_quantise(g, src, c0, c1):
+            quantise([(g, a)], src, codes[:, c0:c1], scales[:, c0:c1])
+
+        def round_held(n):
+            nc.vector.tensor_copy(as_words(held[n][:]), by_runs(raw[a, 1][:, :, n * HALF : (n + 1) * HALF]))
+
+        last_quantise(3, rounded[:, 0], 0, BANK)
+        multiply(3, a)
+        last_quantise(4, rounded[:, 1], BANK, 2 * BANK)
+        multiply(4, a)
+        ds = staged_tile([P, BANK], F32, "ds", 5, PIECE + 3 * PIECE // 4)
+        nc.scalar.copy(ds[:], sums[E][:])
+        vector_product(late[:], closing[1][:], gate_bank[5][:, HALF:C])
+        last_quantise(5, rounded[:, 3, 0:HALF, :], 2 * BANK, 2 * BANK + HALF)
+        multiply(5, a, 0, HALF)
+        last_quantise(5, late[:], 2 * BANK + HALF, 3 * BANK)
+        multiply(5, a, HALF, BANK)
+        for n in range(2):
+            round_held(n)
+        for n in range(2):
+            last_quantise(E + 1, held[n][:], 3 * BANK + n * HALF, 3 * BANK + (n + 1) * HALF)
+            multiply(E + 1, a, n * HALF, (n + 1) * HALF)
+
+        fetched = [staged_tile([P, T], F32, "fetched%d" % n, 4, n * 4 * T) for n in range(2)]
+        partial = [staged_tile([P, T], F32, "partial%d" % n, 4, (2 + n) * 4 * T) for n in range(2)]
+        total = stage.tile([P, T], F32, name="total", offset=HAND_PLACE[0], align_bytes=64)
+
+        def slots_of(r, cols):
+            return dx[:].indirect(pos_sb[r][:, cols.start // GROUP : cols.stop // GROUP])
 
         def add(dst, in0, in1):
             nc.vector.tensor_tensor(dst, in0, in1, ADD)
 
-        cut = 3 * T // 4
-        low, high = slice(0, BANK), slice(BANK, T)
-        nc.scalar.activation(fetched[0][:, high], slots_of(1, BANK, T), COPY)
-        nc.scalar.activation(fetched[0][:, low], slots_of(1, 0, BANK), COPY)
-        nc.scalar.activation(fetched[1][:, low], slots_of(2, 0, BANK), COPY)
-        nc.scalar.activation(fetched[1][:, BANK:cut], slots_of(2, BANK, cut), COPY)
-        add(first_sum[:, low], slots_of(0, 0, BANK), ds[:])
-        add(first_sum[:, high], slots_of(0, BANK, T), fetched[0][:, high])
-        add(second_sum[:, low], first_sum[:, low], fetched[0][:, low])
-        add(second_sum[:, high], first_sum[:, high], sums[E + 1][:])
-        add(total[:, low], second_sum[:, low], fetched[1][:, low])
-        nc.sync.dma_start(out[:, low], total[:, low])
-        add(total[:, cut:T], slots_of(2, cut, T), second_sum[:, cut:T])
-        nc.sync.dma_start(out[:, cut:T], total[:, cut:T])
-        add(total[:, BANK:cut], second_sum[:, BANK:cut], fetched[1][:, BANK:cut])
-        nc.sync.dma_start(out[:, BANK:cut], total[:, BANK:cut])
+        halves = [slice(0, BANK), slice(BANK, T)]
+        ends = [slice(0, BANK), slice(BANK, 3 * T // 4), slice(3 * T // 4, T)]
+        for cols in reversed(halves):
+            nc.scalar.activation(fetched[0][:, cols], slots_of(1, cols), COPY)
+        for cols in ends:
+            nc.scalar.activation(fetched[1][:, cols], slots_of(2, cols), COPY)
+        low, high = halves
+        add(partial[0][:, low], slots_of(0, low), ds[:])
+        add(partial[0][:, high], slots_of(0, high), fetched[0][:, high])
+        add(partial[1][:, low], partial[0][:, low], fetched[0][:, low])
+        add(partial[1][:, high], partial[0][:, high], sums[E + 1][:])
+        for cols in ends:
+            add(total[:, cols], partial[1][:, cols], fetched[1][:, cols])
+            nc.sync.dma_start(out[:, cols], total[:, cols])

@@ -26,7 +26,7 @@ PASSES = N // (P * PACK)
 BANK = 512
 GROUP = 16
 BLOCKS = S // P
-RUN = 4
+RUN = 2
 PAD = 16
 CYCLES = 2 * PASSES
 PIECE = 4 * PACK * C

@@ -167,8 +167,9 @@ def tile_moe_bds_lin_none_kernel(tc, dyT, w_words, w_scales, gate, offs, pos1, p
             nc.vector.tensor_tensor(as_words(dst), by_runs(src), runs.unsqueeze(2).to_broadcast([P, runs.shape[1], PACK, RUN]), MULT)
 
         def gpsimd_product(dst, e, a, cols):
-            gates = gate_sb[e][:, 0:cols].unsqueeze(2).to_broadcast([P, cols, PACK])
-            nc.gpsimd.tensor_tensor(dst[:, 0:cols, :], staged[e, a][:, :, 0:cols].rearrange("p j c -> p c j"), gates, MULT)
+            runs = gate_sb[e][:, 0:cols].rearrange("p (c i) -> p c i", i=RUN)
+            gates = runs.unsqueeze(2).to_broadcast([P, cols // RUN, PACK, RUN])
+            nc.gpsimd.tensor_tensor(as_words(dst[:, 0:cols, :]), by_runs(staged[e, a][:, :, 0:cols]), gates, MULT)
 
         def gpsimd_round(dst, a, h):
             nc.gpsimd.tensor_scalar(dst, raw[a, h].rearrange("p j c -> p c j"), 1.0, 0.0, MULT, ADD)

@@ -25,13 +25,12 @@ PACK = 4
 PASSES = N // (P * PACK)
 BANK = 512
 GROUP = 16
-BLOCKS = S // P
 RUN = 2
 PAD = 16
 CYCLES = 2 * PASSES
 PIECE = 4 * PACK * C
 HANDED = [(2, 0), (3, 0), (2, 1), (3, 1), (2, 2), (3, 2)]
-REST = [64, 0, 0, 0, 88, 160]
+REST = [0, 0, 0, 0, 88, 160]
 SHARED = [(0, 0), (1, 0), (1, 1), (2, 0)]
 HALF = C // 2
 LAP = 64
@@ -52,8 +51,7 @@ def tile_moe_bds_lin_none_kernel(tc, dyT, w_words, w_scales, gate, offs, pos1, p
         offs_sb = keep.tile([P, S // GROUP], U16, name="offs_sb")
         pos_sb = [keep.tile([P, T // GROUP], U16, name="pos_sb%d" % r) for r in range(3)]
         gate_sb = {e: keep.tile([P, C], F32, name="gate_sb%d" % e) for e in (2, 3)}
-        gate_rows = stage.tile([P, P], F32, name="gate_rows", offset=HAND_PLACE[1] + LAP, align_bytes=64)
-        gate_col = keep.tile([P, BLOCKS], F32, name="gate_col")
+        gate_col = keep.tile([P, E, PACK], F32, name="gate_col")
         ident = keep.tile([P, P], F32, name="ident")
         words = keep.tile([P, (E + 1) * PASSES, 2 * K], U8, name="words", align_bytes=64)
         wscale = keep.tile([P, (E + 1) * PASSES, K], U8, name="wscale", align_bytes=64)
@@ -87,16 +85,16 @@ def tile_moe_bds_lin_none_kernel(tc, dyT, w_words, w_scales, gate, offs, pos1, p
 
         nought = keep.tile([P, 1], F32, name="nought")
         nc.vector.memset(nought[:], 0.0)
-        nc.scalar.activation(gate_rows[:], nought[:].to_broadcast([P, P]), COPY)
+        nc.scalar.activation(ident[:], nought[:].to_broadcast([P, P]), COPY)
         nc.vector.memset(wscale[:].rearrange("p m k -> p (m k)").bitcast(I32), 0)
-        make_identity(nc, ident[:])
+        make_identity(nc, ident[:], nomemset=True)
 
         nc.sync.dma_start(opening[:, 0, :], rows[0, :, 0, :])
         nc.sync.dma_start(offs_sb[:], offs)
-        nc.sync.dma_start(opening[:, 1, :], rows[0, :, 1, :])
-        nc.sync.dma_start(gate_rows[0:BLOCKS, :], gate[0, :].rearrange("(b s) -> b s", s=P))
-        for j in range(2, PACK):
-            nc.sync.dma_start(opening[:, j, :], rows[0, :, j, :])
+        nc.sync.dma_start(opening[:, 1:PACK, 0:BANK], rows[0, :, 1:PACK, 0:BANK])
+        for j in range(1, PACK):
+            nc.sync.dma_start(opening[:, j, BANK:T], rows[0, :, j, BANK:T])
+        nc.sync.dma_start(gate_col[:], gate[0, :].rearrange("(e p i) -> p e i", p=P, i=PACK))
         load_gate(2)
         load_windows(1)
         load_windows(2)
@@ -112,25 +110,26 @@ def tile_moe_bds_lin_none_kernel(tc, dyT, w_words, w_scales, gate, offs, pos1, p
         for tile, src in zip(pos_sb, (pos1, pos2, pos3)):
             nc.sync.dma_start(tile[:], src)
 
-        turned = bank(5)
-        nc.tensor.transpose(turned[:, 0:P], gate_rows[:], ident[:])
-        nc.vector.tensor_copy(gate_col[:], turned[:, 0:BLOCKS])
-
-        def spread_gates(tile, blocks):
-            for n, b in enumerate(blocks):
-                nc.tensor.transpose(tile[:, n * P : (n + 1) * P], gate_col[:, b : b + 1].to_broadcast([P, P]), ident[:])
+        def spread_gates(tile, e):
+            by_place = tile[:].rearrange("p (c i) -> p i c", i=PACK)
+            for i in range(PACK):
+                nc.tensor.transpose(by_place[:, i, :], gate_col[:, e, i : i + 1].to_broadcast([P, P]), ident[:])
 
         gate_bank = {}
 
         def make_gates(first):
             for n in range(2):
                 gate_bank[first + n] = bank(n)
-                spread_gates(gate_bank[first + n], range((first + n) * C // P, (first + n + 1) * C // P))
+                spread_gates(gate_bank[first + n], first + n)
 
         make_gates(0)
-        rest_bank = bank(7)
-        spread_gates(rest_bank, (3 * C // P - 1, 4 * C // P - 2, 4 * C // P - 1))
-        rest_end = {2: P, 3: 3 * P}
+        rest_bank = {}
+
+        def make_rest_gates(e):
+            rest_bank[e] = bank(7)
+            spread_gates(rest_bank[e], e)
+
+        make_rest_gates(2)
 
         def looked_up(a, j, s0, s1):
             table = opening[:, j, :] if a == 0 else window[a, j][:]
@@ -218,8 +217,9 @@ def tile_moe_bds_lin_none_kernel(tc, dyT, w_words, w_scales, gate, offs, pos1, p
                 vector_product(rounded[:, 3], staged[e + 1, a], gate_bank[e + 1][:])
             vector_product(rounded[:, 1], staged[e, a], gate_bank[e][:])
             if rest:
-                end = rest_end[handed[0]]
-                vector_product(rounded[:, 0, C - rest : C, :], staged[handed][:, :, C - rest : C], rest_bank[:, end - rest : end])
+                vector_product(rounded[:, 0, C - rest : C, :], staged[handed][:, :, C - rest : C], rest_bank[handed[0]][:, C - rest : C])
+            if k == CYCLES - 2:
+                make_rest_gates(3)
 
         prepare(0)
         vector_gathers(0, 1)
@@ -230,9 +230,10 @@ def tile_moe_bds_lin_none_kernel(tc, dyT, w_words, w_scales, gate, offs, pos1, p
             rounded = work_tile([P, 4, BANK, PACK], BF16, "rounded%d" % k, 0)
             if k == 0:
                 extra = keep.tile([P, BANK, PACK], BF16, name="extra", align_bytes=64)
-                gpsimd_round(extra[:], 0, 1)
             if k < len(SHARED):
                 gpsimd_round(rounded[:, 2], *SHARED[k])
+            if k == 0:
+                gpsimd_round(extra[:], 0, 1)
             gpsimd_product(rounded[:, 0], *HANDED[k], C - REST[k])
             if 0 < k < CYCLES - 2:
                 vector_gathers(k + 1)

@@ -26,17 +26,16 @@ PASSES = N // (P * PACK)
 BANK = 512
 GROUP = 16
 RUN = 2
-PAD = 16
-CYCLES = 2 * PASSES
-PIECE = 4 * PACK * C
-HANDED = [(2, 0), (3, 0), (2, 1), (3, 1), (2, 2), (3, 2)]
-REST = [0, 0, 0, 0, 88, 160]
-SHARED = [(0, 0), (1, 0), (1, 1), (2, 0)]
+TRIO = 3
+WIDE = TRIO * C
+CYCLES = [(0, 0), (0, 1), (0, 2), (1, 1), (1, 2), (1, 0)]
+LAST = len(CYCLES) - 1
+GATHERED = [768, 384, 384, 384, 416, C]
+MULTIPLIED = [704, C, C, 544, 576, C]
+WINDOW = WIDE - min(GATHERED) + GROUP
 HALF = C // 2
-LAP = 64
-PLACE = [0, 6 * PIECE + LAP, 4 * PIECE + LAP, 6 * PIECE + LAP, LAP, 4 * PIECE + LAP, 6 * PIECE + LAP]
-HAND_PLACE = [3 * PIECE + LAP, 2 * PIECE, 3 * PIECE + LAP, 2 * PIECE + LAP, 3 * PIECE + LAP]
-CUT = T
+STAGED = 4 * PACK * WIDE
+PIECE = 2 * PACK * BANK
 
 
 def tile_moe_bds_lin_none_kernel(tc, dyT, w_words, w_scales, gate, offs, pos1, pos2, pos3, out):
@@ -50,26 +49,27 @@ def tile_moe_bds_lin_none_kernel(tc, dyT, w_words, w_scales, gate, offs, pos1, p
 
         offs_sb = keep.tile([P, S // GROUP], U16, name="offs_sb")
         pos_sb = [keep.tile([P, T // GROUP], U16, name="pos_sb%d" % r) for r in range(3)]
-        gate_sb = {e: keep.tile([P, C], F32, name="gate_sb%d" % e) for e in (2, 3)}
-        gate_col = keep.tile([P, E, PACK], F32, name="gate_col")
+        gate_cols = [max(MULTIPLIED[k] for k in range(len(CYCLES)) if CYCLES[k][0] == h) for h in range(2)]
+        gate_sb = [keep.tile([P, gate_cols[h]], F32, name="gate_sb%d" % h) for h in range(2)]
+        gate_col = [keep.tile([P, 2, PACK], F32, name="gate_col%d" % h) for h in range(2)]
         ident = keep.tile([P, P], F32, name="ident")
         words = keep.tile([P, (E + 1) * PASSES, 2 * K], U8, name="words", align_bytes=64)
         wscale = keep.tile([P, (E + 1) * PASSES, K], U8, name="wscale", align_bytes=64)
         dx = keep.tile([P, S], F32, name="dx")
         opening = keep.tile([P, PACK, T], F32, name="opening")
-        window = {(a, j): keep.tile([P, T + PAD], F32, name="window%d_%d" % (a, j)) for a in (1, 2) for j in range(PACK)}
+        window = {(a, j): keep.tile([P, WINDOW], F32, name="window%d_%d" % (a, j)) for a in (1, 2) for j in range(PACK)}
         raw = {(a, h): keep.tile([P, PACK, BANK], F32, name="raw%d_%d" % (a, h))[:] for a in (1, 2) for h in range(2)}
         for h in range(2):
             raw[0, h] = opening[:, :, h * BANK : (h + 1) * BANK]
 
-        def bank(b, cols=BANK):
-            return psum.tile([P, cols], F32, name="bank", tag="bank%d" % b, bufs=1)
+        def bank(b):
+            return psum.tile([P, BANK], F32, name="bank", tag="bank%d" % b, bufs=1)
 
-        def staged_tile(shape, dtype, name, slot, at=0):
-            return stage.tile(shape, dtype, name=name, offset=PLACE[slot] + at, align_bytes=64)
+        def stage_tile(shape, dtype, name, at):
+            return stage.tile(shape, dtype, name=name, offset=at, align_bytes=64)
 
-        def work_tile(shape, dtype, name, at):
-            return work.tile(shape, dtype, name=name, offset=at, align_bytes=64)
+        def work_tile(pieces, name, at):
+            return work.tile([P, pieces * BANK, PACK], BF16, name=name, offset=at * PIECE, align_bytes=64)
 
         rows = dyT.rearrange("(a p j) t -> a p j t", p=P, j=PACK)
 
@@ -80,8 +80,9 @@ def tile_moe_bds_lin_none_kernel(tc, dyT, w_words, w_scales, gate, offs, pos1, p
         def load_raw(a, h):
             nc.sync.dma_start(raw[a, h], rows[a, :, :, h * BANK : (h + 1) * BANK])
 
-        def load_gate(e):
-            nc.sync.dma_start(gate_sb[e][:], gate[0:P, e * C : (e + 1) * C])
+        def load_gates(h):
+            nc.sync.dma_start(gate_col[h][:], gate[0, h * WIDE + C : (h + 1) * WIDE].rearrange("(e p i) -> p e i", p=P, i=PACK))
+            nc.sync.dma_start(gate_sb[h][:], gate[0:P, h * WIDE : h * WIDE + gate_cols[h]])
 
         nought = keep.tile([P, 1], F32, name="nought")
         nc.vector.memset(nought[:], 0.0)
@@ -91,49 +92,37 @@ def tile_moe_bds_lin_none_kernel(tc, dyT, w_words, w_scales, gate, offs, pos1, p
 
         nc.sync.dma_start(opening[:, 0, :], rows[0, :, 0, :])
         nc.sync.dma_start(offs_sb[:], offs)
-        nc.sync.dma_start(opening[:, 1:PACK, 0:BANK], rows[0, :, 1:PACK, 0:BANK])
-        for j in range(1, PACK):
+        nc.sync.dma_start(opening[:, 1, :], rows[0, :, 1, :])
+        nc.sync.dma_start(opening[:, 2:PACK, 0:BANK], rows[0, :, 2:PACK, 0:BANK])
+        for j in range(2, PACK):
             nc.sync.dma_start(opening[:, j, BANK:T], rows[0, :, j, BANK:T])
-        nc.sync.dma_start(gate_col[:], gate[0, :].rearrange("(e p i) -> p e i", p=P, i=PACK))
-        load_gate(2)
+        load_gates(0)
         load_windows(1)
-        load_windows(2)
         load_raw(1, 0)
-        load_gate(3)
-        load_raw(1, 1)
+        load_windows(2)
         load_raw(2, 0)
         nc.sync.dma_start(words[:].bitcast(I32), w_words.rearrange("e a p b -> p (e a) b").bitcast(I32))
         scale_rows = w_scales.rearrange("e a f k -> f (e a) k")
         for q in range(4):
             nc.sync.dma_start(wscale[32 * q : 32 * q + 4, :, :].bitcast(I32), scale_rows[4 * q : 4 * q + 4, :, :].bitcast(I32))
+        load_gates(1)
+        load_raw(1, 1)
         load_raw(2, 1)
         for tile, src in zip(pos_sb, (pos1, pos2, pos3)):
             nc.sync.dma_start(tile[:], src)
 
-        def spread_gates(tile, e):
-            by_place = tile[:].rearrange("p (c i) -> p i c", i=PACK)
-            for i in range(PACK):
-                nc.tensor.transpose(by_place[:, i, :], gate_col[:, e, i : i + 1].to_broadcast([P, P]), ident[:])
-
         gate_bank = {}
-
-        def make_gates(first):
+        for h in range(2):
             for n in range(2):
-                gate_bank[first + n] = bank(n)
-                spread_gates(gate_bank[first + n], first + n)
+                gate_bank[h, n + 1] = bank(2 * h + n)
+                by_place = gate_bank[h, n + 1][:].rearrange("p (c i) -> p i c", i=PACK)
+                for i in range(PACK):
+                    nc.tensor.transpose(by_place[:, i, :], gate_col[h][:, n, i : i + 1].to_broadcast([P, P]), ident[:])
 
-        make_gates(0)
-        rest_bank = {}
-
-        def make_rest_gates(e):
-            rest_bank[e] = bank(7)
-            spread_gates(rest_bank[e], e)
-
-        make_rest_gates(2)
-
-        def looked_up(a, j, s0, s1):
+        def looked_up(k, j, c0, c1):
+            h, a = CYCLES[k]
             table = opening[:, j, :] if a == 0 else window[a, j][:]
-            return table.indirect(offs_sb[:, s0 // GROUP : s1 // GROUP])
+            return table.indirect(offs_sb[:, (h * WIDE + c0) // GROUP : (h * WIDE + c1) // GROUP])
 
         def by_runs(ap):
             return ap.rearrange("p j (c i) -> p c j i", i=RUN)
@@ -141,171 +130,138 @@ def tile_moe_bds_lin_none_kernel(tc, dyT, w_words, w_scales, gate, offs, pos1, p
         def as_words(ap):
             return ap.rearrange("p (c i) j -> p c j i", i=RUN)
 
-        staged = {}
+        def spread(gates):
+            runs = gates.rearrange("p (c i) -> p c i", i=RUN)
+            return runs.unsqueeze(2).to_broadcast([P, runs.shape[1], PACK, RUN])
 
-        def scalar_gathers(a, e, tile):
+        def vector_gathers(k, tile):
             for j in range(PACK):
-                if a == 0:
-                    for n in range(2):
-                        nc.scalar.activation(tile[:, j, n * C : (n + 1) * C], looked_up(a, j, (e + n) * C, (e + n + 1) * C), COPY)
-                else:
-                    nc.scalar.activation(tile[:, j, :], looked_up(a, j, e * C, (e + 2) * C), COPY)
-            for n in range(2):
-                staged[e + n, a] = tile[:, :, n * C : (n + 1) * C]
+                nc.vector.tensor_copy(tile[:, j, 0 : GATHERED[k]], looked_up(k, j, 0, GATHERED[k]))
 
-        def vector_gathers(*cycles):
-            for k in cycles:
-                staged[HANDED[k]] = stage.tile([P, PACK, C], F32, name="handed%d" % k, offset=HAND_PLACE[k], align_bytes=64)[:]
+        def scalar_gathers(k, tile, cuts, first=0):
             for j in range(PACK):
-                for k in cycles:
-                    e, a = HANDED[k]
-                    nc.vector.tensor_copy(staged[e, a][:, j, :], looked_up(a, j, e * C, (e + 1) * C))
+                for c0, c1 in zip(cuts, cuts[1:]):
+                    nc.scalar.activation(tile[:, j, c0 - first : c1 - first], looked_up(k, j, c0, c1), COPY)
 
         def vector_product(dst, src, gates):
-            runs = gates.rearrange("p (c i) -> p c i", i=RUN)
-            nc.vector.tensor_tensor(as_words(dst), by_runs(src), runs.unsqueeze(2).to_broadcast([P, runs.shape[1], PACK, RUN]), MULT)
+            nc.vector.tensor_tensor(as_words(dst), by_runs(src), spread(gates), MULT)
 
-        def gpsimd_product(dst, e, a, cols):
-            runs = gate_sb[e][:, 0:cols].rearrange("p (c i) -> p c i", i=RUN)
-            gates = runs.unsqueeze(2).to_broadcast([P, cols // RUN, PACK, RUN])
-            nc.gpsimd.tensor_tensor(as_words(dst[:, 0:cols, :]), by_runs(staged[e, a][:, :, 0:cols]), gates, MULT)
+        def gpsimd_product(dst, src, gates):
+            nc.gpsimd.tensor_tensor(as_words(dst), by_runs(src), spread(gates), MULT)
 
         def gpsimd_round(dst, a, h):
             nc.gpsimd.tensor_scalar(dst, raw[a, h].rearrange("p j c -> p c j"), 1.0, 0.0, MULT, ADD)
 
-        quantised = {}
+        bank_of = {0: 4, 1: 5, 2: 6, 3: 4, 4: 5, 5: 6, E: 7, E + 1: 0}
+        sums = {}
+        added = {g: 0 for g in bank_of}
+
+        def multiply(g, a, codes, scales):
+            if added[g] == 0:
+                sums[g] = bank(bank_of[g])
+            added[g] = added[g] + 1
+            m = min(g, E) * PASSES + a
+            nc.tensor.matmul_mx(
+                out=sums[g][:],
+                lhsT=words[:, m, :].bitcast(E2M1X4),
+                lhsT_scale=wscale[:, m, :],
+                rhs=codes.bitcast(E5M2X4),
+                rhs_scale=scales,
+                start=added[g] == 1,
+                stop=added[g] == PASSES,
+            )
 
         def quantise(pieces, src, codes, scales):
             nc.vector.quantize_mx(out=codes.bitcast(E5M2X4), scales=scales, in_=src.rearrange("p c j -> p (c j)"))
-            cols = src.shape[1] // len(pieces)
-            for n, piece in enumerate(pieces):
-                quantised[piece] = (codes[:, n * cols : (n + 1) * cols], scales[:, n * cols : (n + 1) * cols])
+            for n, (g, a) in enumerate(pieces):
+                multiply(g, a, codes[:, n * BANK : (n + 1) * BANK], scales[:, n * BANK : (n + 1) * BANK])
 
-        bank_of = {0: 2, 1: 3, 2: 4, 3: 5, 4: 2, 5: 3, E: 6, E + 1: 7}
-        sums = {}
+        def bring_out(g):
+            nc.scalar.copy(dx[:, g * C : (g + 1) * C], sums[g][:])
 
-        def multiply(g, a, c0=0, c1=BANK):
-            if a == 0:
-                sums[g] = bank(bank_of[g])
-            e = min(g, E)
-            codes, scales = quantised[g, a]
-            closes = a == PASSES - 1 and c1 == BANK
-            nc.tensor.matmul_mx(
-                out=sums[g][:, c0:c1],
-                lhsT=words[:, e * PASSES + a, :].bitcast(E2M1X4),
-                lhsT_scale=wscale[:, e * PASSES + a, :],
-                rhs=codes.bitcast(E5M2X4),
-                rhs_scale=scales,
-                start=(a == 0),
-                stop=closes,
-            )
-            if closes and g < E:
-                nc.scalar.copy(dx[:, g * C : (g + 1) * C], sums[g][:])
-
-        def pair_of(k):
-            return 4 * (k // PASSES), k % PASSES
-
-        def prepare(k):
-            e, a = pair_of(k)
-            scalar_gathers(a, e, staged_tile([P, PACK, 2 * C], F32, "staged%d" % k, k))
-
-        def products(k, rounded, second_cols):
-            e, a = pair_of(k)
-            handed = HANDED[k]
-            rest = REST[k]
-            if k < CYCLES - 1:
-                vector_product(rounded[:, 3], staged[e + 1, a], gate_bank[e + 1][:])
-            vector_product(rounded[:, 1], staged[e, a], gate_bank[e][:])
-            if rest:
-                vector_product(rounded[:, 0, C - rest : C, :], staged[handed][:, :, C - rest : C], rest_bank[handed[0]][:, C - rest : C])
-            if k == CYCLES - 2:
-                make_rest_gates(3)
-
-        prepare(0)
-        vector_gathers(0, 1)
-        prepare(1)
-        prepare(2)
-        for k in range(CYCLES - 1):
-            e, a = pair_of(k)
-            rounded = work_tile([P, 4, BANK, PACK], BF16, "rounded%d" % k, 0)
-            if k == 0:
-                extra = keep.tile([P, BANK, PACK], BF16, name="extra", align_bytes=64)
-            if k < len(SHARED):
-                gpsimd_round(rounded[:, 2], *SHARED[k])
-            if k == 0:
-                gpsimd_round(extra[:], 0, 1)
-            gpsimd_product(rounded[:, 0], *HANDED[k], C - REST[k])
-            if 0 < k < CYCLES - 2:
-                vector_gathers(k + 1)
-            products(k, rounded, C)
-            if k == PASSES - 1:
-                make_gates(4)
-            if k + 3 < CYCLES - 1:
-                prepare(k + 3)
-            if k + 3 == CYCLES:
-                closing = [staged_tile([P, PACK, HALF], F32, "closing%d" % n, 6, n * PIECE // 2) for n in range(2)]
-                for n in range(2):
-                    for j in range(PACK):
-                        nc.scalar.activation(closing[n][:, j, :], looked_up(PASSES - 1, j, S - C + n * HALF, S - C + (n + 1) * HALF), COPY)
+        def code_tiles():
             codes = ring.tile([P, 4 * BANK], U32, name="codes", tag="codes", bufs=3, align_bytes=64)
             scales = ring.tile([P, 4 * BANK], U8, name="scales", tag="scales", bufs=3, align_bytes=64)
-            flat = rounded[:].rearrange("p n c j -> p (n c) j")
-            if k == 0:
-                extra_codes = keep.tile([P, BANK], U32, name="extra_codes", align_bytes=64)
-                extra_scales = keep.tile([P, BANK], U8, name="extra_scales", align_bytes=64)
-                quantise([(E + 1, 0)], extra[:], extra_codes[:], extra_scales[:])
-            if k < len(SHARED):
-                shared = (E + SHARED[k][1], SHARED[k][0])
-                quantise([shared, (e + 1, a)], flat[:, 2 * BANK :], codes[:, 2 * BANK :], scales[:, 2 * BANK :])
-                if shared[0] == E:
-                    multiply(*shared)
+            return codes, scales
+
+        staged = {}
+
+        def stage_cycle(k):
+            staged[k] = stage_tile([P, PACK, WIDE], F32, "staged%d" % k, (k % 2) * STAGED)
+
+        stage_cycle(0)
+        vector_gathers(0, staged[0])
+        scalar_gathers(0, staged[0], [GATHERED[0], 2 * C, WIDE])
+        stage_cycle(1)
+        scalar_gathers(1, staged[1], [GATHERED[1], WIDE])
+        held = []
+        for k in range(LAST):
+            h, a = CYCLES[k]
+            g = MULTIPLIED[k]
+            if k < PASSES:
+                tile = work_tile(4, "rounded%d" % k, 1)
+                routed, shared = (tile[:, BANK:], tile[:, 0:BANK]) if k == 0 else (tile[:, 0:WIDE], tile[:, WIDE:])
+                gpsimd_round(shared, a, 0)
             else:
-                quantise([(e + 1, a)], flat[:, 3 * BANK :], codes[:, 3 * BANK :], scales[:, 3 * BANK :])
-            multiply(e + 1, a)
-            quantise([HANDED[k], (e, a)], flat[:, 0 : 2 * BANK], codes[:, 0 : 2 * BANK], scales[:, 0 : 2 * BANK])
-            multiply(e, a)
-            multiply(*HANDED[k])
-            if k + 3 == CYCLES - 1:
-                scalar_gathers(PASSES - 1, 3, staged_tile([P, PACK, 2 * C], F32, "both", 5))
+                tile = work_tile(TRIO, "rounded%d" % k, 4 - k)
+                routed = tile[:]
+            if k == 0 or k >= PASSES:
+                held.append((a, work_tile(1, "held%d" % k, {0: 5, 3: 4, 4: 3}[k])))
+                gpsimd_round(held[-1][1][:], a, 1)
+            gpsimd_product(routed[:, 0:g], staged[k][:, :, 0:g], gate_sb[h][:, 0:g])
+            if k + 1 < LAST:
+                vector_gathers(k + 1, staged[k + 1])
+            else:
+                vector_gathers(LAST, parts[0])
+            vector_product(routed[:, 2 * C :], staged[k][:, :, 2 * C :], gate_bank[h, 2][:])
+            vector_product(routed[:, g : 2 * C], staged[k][:, :, g : 2 * C], gate_bank[h, 1][:, g - C :])
+            if k + 2 < LAST:
+                stage_cycle(k + 2)
+                scalar_gathers(k + 2, staged[k + 2], [GATHERED[k + 2], WIDE])
+            codes, scales = code_tiles()
+            experts = [(TRIO * h + n, a) for n in range(TRIO)]
+            if k == 0:
+                quantise([(E, a), experts[0]], tile[:, 0 : 2 * BANK], codes[:, 0 : 2 * BANK], scales[:, 0 : 2 * BANK])
+                quantise(experts[1:], tile[:, 2 * BANK :], codes[:, 2 * BANK :], scales[:, 2 * BANK :])
+            else:
+                behind = experts[2:] + ([(E, a)] if k < PASSES else [])
+                end = (2 + len(behind)) * BANK
+                quantise(behind, tile[:, 2 * BANK :], codes[:, 2 * BANK : end], scales[:, 2 * BANK : end])
+                quantise(experts[0:2], tile[:, 0 : 2 * BANK], codes[:, 0 : 2 * BANK], scales[:, 0 : 2 * BANK])
+            if k == PASSES - 1:
+                for n in range(TRIO):
+                    bring_out(n)
+            if k + 2 == LAST:
+                cuts = [0, C, 2 * C, 2 * C + HALF, WIDE]
+                parts = []
+                for c0, c1 in zip(cuts, cuts[1:]):
+                    parts.append(stage_tile([P, PACK, c1 - c0], F32, "part%d" % c0, STAGED + 4 * PACK * c0))
+                    if c0 > 0:
+                        scalar_gathers(LAST, parts[-1], [c0, c1], c0)
 
-        k, a = CYCLES - 1, PASSES - 1
-        rounded = work_tile([P, 4, BANK, PACK], BF16, "rounded%d" % k, 0)
-        gpsimd_product(rounded[:, 0], *HANDED[k], C - REST[k])
-        products(k, rounded, HALF)
-        vector_product(rounded[:, 3, 0:HALF, :], closing[0][:], gate_bank[5][:, 0:HALF])
-        for earlier in range(a):
-            multiply(E + 1, earlier)
-        codes = staged_tile([P, 4 * BANK], U32, "last_codes", 5)
-        late = staged_tile([P, HALF, PACK], BF16, "late", 5, PIECE)
-        held = [staged_tile([P, HALF, PACK], BF16, "held%d" % n, 5, PIECE + (n + 1) * PIECE // 4) for n in range(2)]
-        scales = keep.tile([P, 4 * BANK], U8, name="last_scales", align_bytes=64)
-
-        def last_quantise(g, src, c0, c1):
-            quantise([(g, a)], src, codes[:, c0:c1], scales[:, c0:c1])
-
-        def round_held(n):
-            nc.vector.tensor_copy(as_words(held[n][:]), by_runs(raw[a, 1][:, :, n * HALF : (n + 1) * HALF]))
-
-        last_quantise(3, rounded[:, 0], 0, BANK)
-        multiply(3, a)
-        last_quantise(4, rounded[:, 1], BANK, 2 * BANK)
-        multiply(4, a)
-        ds = staged_tile([P, BANK], F32, "ds", 5, PIECE + 3 * PIECE // 4)
+        h, a = CYCLES[LAST]
+        tile = work_tile(TRIO, "rounded_last", 0)
+        gpsimd_product(tile[:, 0:C], parts[0][:], gate_sb[h][:, 0:C])
+        vector_product(tile[:, C : 2 * C], parts[1][:], gate_bank[h, 1][:])
+        for n in range(2):
+            cols = slice(n * HALF, (n + 1) * HALF)
+            vector_product(tile[:, 2 * C + cols.start : 2 * C + cols.stop], parts[2 + n][:], gate_bank[h, 2][:, cols])
+        ds = stage_tile([P, BANK], F32, "ds", STAGED + PASSES * 4 * BANK)
         nc.scalar.copy(ds[:], sums[E][:])
-        vector_product(late[:], closing[1][:], gate_bank[5][:, HALF:C])
-        last_quantise(5, rounded[:, 3, 0:HALF, :], 2 * BANK, 2 * BANK + HALF)
-        multiply(5, a, 0, HALF)
-        last_quantise(5, late[:], 2 * BANK + HALF, 3 * BANK)
-        multiply(5, a, HALF, BANK)
-        for n in range(2):
-            round_held(n)
-        for n in range(2):
-            last_quantise(E + 1, held[n][:], 3 * BANK + n * HALF, 3 * BANK + (n + 1) * HALF)
-            multiply(E + 1, a, n * HALF, (n + 1) * HALF)
+        codes, scales = code_tiles()
+        for n in (1, 2, 0):
+            cols = slice(n * C, (n + 1) * C)
+            quantise([(TRIO + n, a)], tile[:, cols], codes[:, cols], scales[:, cols])
+            bring_out(TRIO + n)
+        codes = stage_tile([P, PASSES * BANK], U32, "held_codes", STAGED)
+        scales = keep.tile([P, PASSES * BANK], U8, name="held_scales", align_bytes=64)
+        for n, (a, tile) in enumerate(held):
+            cols = slice(n * BANK, (n + 1) * BANK)
+            quantise([(E + 1, a)], tile[:], codes[:, cols], scales[:, cols])
 
-        fetched = [staged_tile([P, T], F32, "fetched%d" % n, 4, n * 4 * T) for n in range(2)]
-        partial = [staged_tile([P, T], F32, "partial%d" % n, 4, (2 + n) * 4 * T) for n in range(2)]
-        total = stage.tile([P, T], F32, name="total", offset=HAND_PLACE[0], align_bytes=64)
+        fetched = [stage_tile([P, T], F32, "fetched%d" % n, n * 4 * T) for n in range(2)]
+        partial = [stage_tile([P, T], F32, "partial%d" % n, (2 + n) * 4 * T) for n in range(2)]
+        total = stage_tile([P, T], F32, "total", 4 * 4 * T)
 
         def slots_of(r, cols):
             return dx[:].indirect(pos_sb[r][:, cols.start // GROUP : cols.stop // GROUP])

@@ -30,12 +30,17 @@ TRIO = 3
 WIDE = TRIO * C
 CYCLES = [(0, 0), (0, 1), (0, 2), (1, 1), (1, 2), (1, 0)]
 LAST = len(CYCLES) - 1
-GATHERED = [768, 384, 384, 384, 416, C]
-MULTIPLIED = [704, C, C, 544, 576, C]
+GATHERED = [768, 384, 384, 384, 384, 384]
+MULTIPLIED = [640, C, C, C, C, 384]
 WINDOW = WIDE - min(GATHERED) + GROUP
 HALF = C // 2
 STAGED = 4 * PACK * WIDE
 PIECE = 2 * PACK * BANK
+LAP = 64
+FRONT = {1: PIECE + 2 * LAP, 2: PIECE + LAP, 3: PIECE + 2 * LAP, 4: PIECE, 5: PIECE}
+THIRD = {1: 2 * LAP, 2: 3 * PIECE + LAP, 3: 2 * LAP, 4: 3 * PIECE}
+SHARED = {1: 3 * PIECE + 2 * LAP, 2: LAP}
+HELD = {0: 5 * PIECE, 3: 4 * PIECE, 4: 0}
 
 
 def tile_moe_bds_lin_none_kernel(tc, dyT, w_words, w_scales, gate, offs, pos1, pos2, pos3, out):
@@ -52,6 +57,7 @@ def tile_moe_bds_lin_none_kernel(tc, dyT, w_words, w_scales, gate, offs, pos1, p
         gate_cols = [max(MULTIPLIED[k] for k in range(len(CYCLES)) if CYCLES[k][0] == h) for h in range(2)]
         gate_sb = [keep.tile([P, gate_cols[h]], F32, name="gate_sb%d" % h) for h in range(2)]
         gate_col = [keep.tile([P, 2, PACK], F32, name="gate_col%d" % h) for h in range(2)]
+        rest_col = keep.tile([P, 1], F32, name="rest_col")
         ident = keep.tile([P, P], F32, name="ident")
         words = keep.tile([P, (E + 1) * PASSES, 2 * K], U8, name="words", align_bytes=64)
         wscale = keep.tile([P, (E + 1) * PASSES, K], U8, name="wscale", align_bytes=64)
@@ -68,8 +74,8 @@ def tile_moe_bds_lin_none_kernel(tc, dyT, w_words, w_scales, gate, offs, pos1, p
         def stage_tile(shape, dtype, name, at):
             return stage.tile(shape, dtype, name=name, offset=at, align_bytes=64)
 
-        def work_tile(pieces, name, at):
-            return work.tile([P, pieces * BANK, PACK], BF16, name=name, offset=at * PIECE, align_bytes=64)
+        def work_tile(cols, name, at):
+            return work.tile([P, cols, PACK], BF16, name=name, offset=at, align_bytes=64)
 
         rows = dyT.rearrange("(a p j) t -> a p j t", p=P, j=PACK)
 
@@ -106,6 +112,7 @@ def tile_moe_bds_lin_none_kernel(tc, dyT, w_words, w_scales, gate, offs, pos1, p
         for q in range(4):
             nc.sync.dma_start(wscale[32 * q : 32 * q + 4, :, :].bitcast(I32), scale_rows[4 * q : 4 * q + 4, :, :].bitcast(I32))
         load_gates(1)
+        nc.sync.dma_start(rest_col[:], gate[0, WIDE + MULTIPLIED[LAST] : WIDE + C].rearrange("(p i) -> p i", i=1))
         load_raw(1, 1)
         load_raw(2, 1)
         for tile, src in zip(pos_sb, (pos1, pos2, pos3)):
@@ -156,25 +163,28 @@ def tile_moe_bds_lin_none_kernel(tc, dyT, w_words, w_scales, gate, offs, pos1, p
         sums = {}
         added = {g: 0 for g in bank_of}
 
-        def multiply(g, a, codes, scales):
-            if added[g] == 0:
+        def multiply(g, a, codes, scales, c0):
+            opens = added[g] == 0
+            if opens:
                 sums[g] = bank(bank_of[g])
-            added[g] = added[g] + 1
+            cols = codes.shape[1]
+            added[g] = added[g] + cols
             m = min(g, E) * PASSES + a
             nc.tensor.matmul_mx(
-                out=sums[g][:],
+                out=sums[g][:, c0 : c0 + cols],
                 lhsT=words[:, m, :].bitcast(E2M1X4),
                 lhsT_scale=wscale[:, m, :],
                 rhs=codes.bitcast(E5M2X4),
                 rhs_scale=scales,
-                start=added[g] == 1,
-                stop=added[g] == PASSES,
+                start=opens,
+                stop=added[g] == PASSES * BANK,
             )
 
-        def quantise(pieces, src, codes, scales):
+        def quantise(pieces, src, codes, scales, c0=0):
             nc.vector.quantize_mx(out=codes.bitcast(E5M2X4), scales=scales, in_=src.rearrange("p c j -> p (c j)"))
+            cols = src.shape[1] // len(pieces)
             for n, (g, a) in enumerate(pieces):
-                multiply(g, a, codes[:, n * BANK : (n + 1) * BANK], scales[:, n * BANK : (n + 1) * BANK])
+                multiply(g, a, codes[:, n * cols : (n + 1) * cols], scales[:, n * cols : (n + 1) * cols], c0)
 
         def bring_out(g):
             nc.scalar.copy(dx[:, g * C : (g + 1) * C], sums[g][:])
@@ -198,23 +208,23 @@ def tile_moe_bds_lin_none_kernel(tc, dyT, w_words, w_scales, gate, offs, pos1, p
         for k in range(LAST):
             h, a = CYCLES[k]
             g = MULTIPLIED[k]
+            if k == 0:
+                tile = work_tile(4 * BANK, "rounded", LAP)
+                shared, front, third = tile[:, 0:BANK], tile[:, BANK : 3 * BANK], tile[:, 3 * BANK :]
+            else:
+                front = work_tile(2 * BANK, "front%d" % k, FRONT[k])[:]
+                third = work_tile(BANK, "third%d" % k, THIRD[k])[:]
+            if k in SHARED:
+                shared = work_tile(BANK, "shared%d" % k, SHARED[k])[:]
             if k < PASSES:
-                tile = work_tile(4, "rounded%d" % k, 1)
-                routed, shared = (tile[:, BANK:], tile[:, 0:BANK]) if k == 0 else (tile[:, 0:WIDE], tile[:, WIDE:])
                 gpsimd_round(shared, a, 0)
-            else:
-                tile = work_tile(TRIO, "rounded%d" % k, 4 - k)
-                routed = tile[:]
-            if k == 0 or k >= PASSES:
-                held.append((a, work_tile(1, "held%d" % k, {0: 5, 3: 4, 4: 3}[k])))
+            if k in HELD:
+                held.append((a, work_tile(BANK, "held%d" % k, HELD[k])))
                 gpsimd_round(held[-1][1][:], a, 1)
-            gpsimd_product(routed[:, 0:g], staged[k][:, :, 0:g], gate_sb[h][:, 0:g])
-            if k + 1 < LAST:
-                vector_gathers(k + 1, staged[k + 1])
-            else:
-                vector_gathers(LAST, parts[0])
-            vector_product(routed[:, 2 * C :], staged[k][:, :, 2 * C :], gate_bank[h, 2][:])
-            vector_product(routed[:, g : 2 * C], staged[k][:, :, g : 2 * C], gate_bank[h, 1][:, g - C :])
+            gpsimd_product(front[:, 0:g], staged[k][:, :, 0:g], gate_sb[h][:, 0:g])
+            vector_gathers(k + 1, staged[k + 1])
+            vector_product(third, staged[k][:, :, 2 * C :], gate_bank[h, 2][:])
+            vector_product(front[:, g:], staged[k][:, :, g : 2 * C], gate_bank[h, 1][:, g - C :])
             if k + 2 < LAST:
                 stage_cycle(k + 2)
                 scalar_gathers(k + 2, staged[k + 2], [GATHERED[k + 2], WIDE])
@@ -224,39 +234,48 @@ def tile_moe_bds_lin_none_kernel(tc, dyT, w_words, w_scales, gate, offs, pos1, p
                 quantise([(E, a), experts[0]], tile[:, 0 : 2 * BANK], codes[:, 0 : 2 * BANK], scales[:, 0 : 2 * BANK])
                 quantise(experts[1:], tile[:, 2 * BANK :], codes[:, 2 * BANK :], scales[:, 2 * BANK :])
             else:
-                behind = experts[2:] + ([(E, a)] if k < PASSES else [])
-                end = (2 + len(behind)) * BANK
-                quantise(behind, tile[:, 2 * BANK :], codes[:, 2 * BANK : end], scales[:, 2 * BANK : end])
-                quantise(experts[0:2], tile[:, 0 : 2 * BANK], codes[:, 0 : 2 * BANK], scales[:, 0 : 2 * BANK])
+                if k in SHARED:
+                    quantise([(E, a)], shared, codes[:, 3 * BANK :], scales[:, 3 * BANK :])
+                quantise(experts[2:], third, codes[:, 2 * BANK : 3 * BANK], scales[:, 2 * BANK : 3 * BANK])
+                quantise(experts[0:2], front, codes[:, 0 : 2 * BANK], scales[:, 0 : 2 * BANK])
             if k == PASSES - 1:
                 for n in range(TRIO):
                     bring_out(n)
+                rest_bank = bank(1)
+                nc.tensor.transpose(rest_bank[:, 0:P], rest_col[:].to_broadcast([P, P]), ident[:])
             if k + 2 == LAST:
                 cuts = [0, C, 2 * C, 2 * C + HALF, WIDE]
                 parts = []
                 for c0, c1 in zip(cuts, cuts[1:]):
                     parts.append(stage_tile([P, PACK, c1 - c0], F32, "part%d" % c0, STAGED + 4 * PACK * c0))
-                    if c0 > 0:
-                        scalar_gathers(LAST, parts[-1], [c0, c1], c0)
+                    scalar_gathers(LAST, parts[-1], [max(c0, GATHERED[LAST]), c1], c0)
+                staged[LAST] = parts[0]
 
         h, a = CYCLES[LAST]
-        tile = work_tile(TRIO, "rounded_last", 0)
-        gpsimd_product(tile[:, 0:C], parts[0][:], gate_sb[h][:, 0:C])
-        vector_product(tile[:, C : 2 * C], parts[1][:], gate_bank[h, 1][:])
-        for n in range(2):
-            cols = slice(n * HALF, (n + 1) * HALF)
-            vector_product(tile[:, 2 * C + cols.start : 2 * C + cols.stop], parts[2 + n][:], gate_bank[h, 2][:, cols])
-        ds = stage_tile([P, BANK], F32, "ds", STAGED + PASSES * 4 * BANK)
-        nc.scalar.copy(ds[:], sums[E][:])
+        g = MULTIPLIED[LAST]
+        tile = work_tile(2 * BANK + HALF, "rounded_last", FRONT[LAST])
+        front, back = tile[:, 0 : 2 * BANK], tile[:, 2 * BANK :]
+        gpsimd_product(front[:, 0:g], parts[0][:, :, 0:g], gate_sb[h][:, 0:g])
+        vector_product(front[:, C:], parts[1][:], gate_bank[h, 1][:])
+        vector_product(front[:, g:C], parts[0][:, :, g:C], rest_bank[:, 0 : C - g])
+        vector_product(back, parts[2][:], gate_bank[h, 2][:, 0:HALF])
         codes, scales = code_tiles()
-        for n in (1, 2, 0):
-            cols = slice(n * C, (n + 1) * C)
-            quantise([(TRIO + n, a)], tile[:, cols], codes[:, cols], scales[:, cols])
-            bring_out(TRIO + n)
-        codes = stage_tile([P, PASSES * BANK], U32, "held_codes", STAGED)
-        scales = keep.tile([P, PASSES * BANK], U8, name="held_scales", align_bytes=64)
+        quantise([(4, a)], front[:, C:], codes[:, 0:BANK], scales[:, 0:BANK])
+        bring_out(4)
+        late = stage_tile([P, HALF, PACK], BF16, "late", STAGED)
+        ds = stage_tile([P, BANK], F32, "ds", STAGED + 4 * BANK)
+        codes = stage_tile([P, 5 * BANK], U32, "late_codes", STAGED + 8 * BANK)
+        scales = keep.tile([P, 5 * BANK], U8, name="late_scales", align_bytes=64)
+        nc.scalar.copy(ds[:], sums[E][:])
+        quantise([(3, a)], front[:, 0:C], codes[:, 0:BANK], scales[:, 0:BANK])
+        bring_out(3)
+        vector_product(late[:], parts[3][:], gate_bank[h, 2][:, HALF:])
+        for n, src in enumerate((back, late[:])):
+            cols = slice(BANK + n * HALF, BANK + (n + 1) * HALF)
+            quantise([(5, a)], src, codes[:, cols], scales[:, cols], n * HALF)
+        bring_out(5)
         for n, (a, tile) in enumerate(held):
-            cols = slice(n * BANK, (n + 1) * BANK)
+            cols = slice((2 + n) * BANK, (3 + n) * BANK)
             quantise([(E + 1, a)], tile[:], codes[:, cols], scales[:, cols])
 
         fetched = [stage_tile([P, T], F32, "fetched%d" % n, n * 4 * T) for n in range(2)]

@@ -30,11 +30,14 @@ TRIO = 3
 WIDE = TRIO * C
 CYCLES = [(0, 0), (0, 1), (0, 2), (1, 1), (1, 2), (1, 0)]
 LAST = len(CYCLES) - 1
-GATHERED = [768, 384, 384, 384, 384, 384]
+OWN = 2
 MULTIPLIED = [640, C, C, C, C, 384]
-WINDOW = WIDE - min(GATHERED) + GROUP
+WINDOW = WIDE + GROUP
 HALF = C // 2
+PARTS = [(0, C), (C, 2 * C), (2 * C, 2 * C + HALF), (2 * C + HALF, WIDE)]
 STAGED = 4 * PACK * WIDE
+GATES = STAGED
+SECOND = GATES + 9 * 256
 PIECE = 2 * PACK * BANK
 LAP = 64
 FRONT = {1: PIECE + 2 * LAP, 2: PIECE + LAP, 3: PIECE + 2 * LAP, 4: PIECE, 5: PIECE}
@@ -55,7 +58,7 @@ def tile_moe_bds_lin_none_kernel(tc, dyT, w_words, w_scales, gate, offs, pos1, p
         offs_sb = keep.tile([P, S // GROUP], U16, name="offs_sb")
         pos_sb = [keep.tile([P, T // GROUP], U16, name="pos_sb%d" % r) for r in range(3)]
         gate_cols = [max(MULTIPLIED[k] for k in range(len(CYCLES)) if CYCLES[k][0] == h) for h in range(2)]
-        gate_sb = [keep.tile([P, gate_cols[h]], F32, name="gate_sb%d" % h) for h in range(2)]
+        gate_sb = [keep.tile([P, gate_cols[0]], F32, name="gate_sb0"), stage.tile([P, gate_cols[1]], F32, name="gate_sb1", offset=GATES, align_bytes=64)]
         gate_col = [keep.tile([P, 2, PACK], F32, name="gate_col%d" % h) for h in range(2)]
         rest_col = keep.tile([P, 1], F32, name="rest_col")
         ident = keep.tile([P, P], F32, name="ident")
@@ -79,8 +82,10 @@ def tile_moe_bds_lin_none_kernel(tc, dyT, w_words, w_scales, gate, offs, pos1, p
 
         rows = dyT.rearrange("(a p j) t -> a p j t", p=P, j=PACK)
 
+        others = [j for j in range(PACK) if j != OWN]
+
         def load_windows(a):
-            for j in range(PACK):
+            for j in [OWN] + others:
                 nc.sync.dma_start(window[a, j][:, 0:T], rows[a, :, j, :])
 
         def load_raw(a, h):
@@ -128,7 +133,12 @@ def tile_moe_bds_lin_none_kernel(tc, dyT, w_words, w_scales, gate, offs, pos1, p
 
         def looked_up(k, j, c0, c1):
             h, a = CYCLES[k]
-            table = opening[:, j, :] if a == 0 else window[a, j][:]
+            if a > 0:
+                table = window[a, j][:]
+            elif c1 - c0 < T:
+                table = opening[:, j, :]
+            else:
+                table = opening[:, j : j + 2, :].rearrange("p j t -> p (j t)")
             return table.indirect(offs_sb[:, (h * WIDE + c0) // GROUP : (h * WIDE + c1) // GROUP])
 
         def by_runs(ap):
@@ -141,12 +151,15 @@ def tile_moe_bds_lin_none_kernel(tc, dyT, w_words, w_scales, gate, offs, pos1, p
             runs = gates.rearrange("p (c i) -> p c i", i=RUN)
             return runs.unsqueeze(2).to_broadcast([P, runs.shape[1], PACK, RUN])
 
-        def vector_gathers(k, tile):
-            for j in range(PACK):
-                nc.vector.tensor_copy(tile[:, j, 0 : GATHERED[k]], looked_up(k, j, 0, GATHERED[k]))
+        staged = {}
 
-        def scalar_gathers(k, tile, cuts, first=0):
-            for j in range(PACK):
+        def vector_gather(k, j, c0, c1):
+            tile, first = staged[k, c0]
+            nc.vector.tensor_copy(tile[:, j, c0 - first : c1 - first], looked_up(k, j, c0, c1))
+
+        def scalar_gathers(k, planes, cuts):
+            tile, first = staged[k, cuts[0]]
+            for j in planes:
                 for c0, c1 in zip(cuts, cuts[1:]):
                     nc.scalar.activation(tile[:, j, c0 - first : c1 - first], looked_up(k, j, c0, c1), COPY)
 
@@ -194,20 +207,23 @@ def tile_moe_bds_lin_none_kernel(tc, dyT, w_words, w_scales, gate, offs, pos1, p
             scales = ring.tile([P, 4 * BANK], U8, name="scales", tag="scales", bufs=3, align_bytes=64)
             return codes, scales
 
-        staged = {}
-
-        def stage_cycle(k):
-            staged[k] = stage_tile([P, PACK, WIDE], F32, "staged%d" % k, (k % 2) * STAGED)
+        def stage_cycle(k, c0=0, c1=WIDE):
+            staged[k, c0] = (stage_tile([P, PACK, c1 - c0], F32, "staged%d_%d" % (k, c0), (k % 2) * SECOND + 4 * PACK * c0), c0)
 
         stage_cycle(0)
-        vector_gathers(0, staged[0])
-        scalar_gathers(0, staged[0], [GATHERED[0], 2 * C, WIDE])
+        for j in range(OWN):
+            vector_gather(0, j, 0, WIDE // 2)
+        vector_gather(0, OWN, 0, WIDE)
+        staged[0, WIDE // 2] = staged[0, 0]
+        scalar_gathers(0, range(OWN), [WIDE // 2, 2 * C, WIDE])
+        scalar_gathers(0, [PACK - 1], [0, C, 2 * C, WIDE])
         stage_cycle(1)
-        scalar_gathers(1, staged[1], [GATHERED[1], WIDE])
+        scalar_gathers(1, others, [0, WIDE])
         held = []
         for k in range(LAST):
             h, a = CYCLES[k]
             g = MULTIPLIED[k]
+            values = staged[k, 0][0]
             if k == 0:
                 tile = work_tile(4 * BANK, "rounded", LAP)
                 shared, front, third = tile[:, 0:BANK], tile[:, BANK : 3 * BANK], tile[:, 3 * BANK :]
@@ -221,13 +237,17 @@ def tile_moe_bds_lin_none_kernel(tc, dyT, w_words, w_scales, gate, offs, pos1, p
             if k in HELD:
                 held.append((a, work_tile(BANK, "held%d" % k, HELD[k])))
                 gpsimd_round(held[-1][1][:], a, 1)
-            gpsimd_product(front[:, 0:g], staged[k][:, :, 0:g], gate_sb[h][:, 0:g])
-            vector_gathers(k + 1, staged[k + 1])
-            vector_product(third, staged[k][:, :, 2 * C :], gate_bank[h, 2][:])
-            vector_product(front[:, g:], staged[k][:, :, g : 2 * C], gate_bank[h, 1][:, g - C :])
+            gpsimd_product(front[:, 0:g], values[:, :, 0:g], gate_sb[h][:, 0:g])
+            if k + 1 < LAST:
+                vector_gather(k + 1, OWN, 0, WIDE)
+            else:
+                for j in range(TRIO):
+                    vector_gather(LAST, j, 0, C)
+            vector_product(third, values[:, :, 2 * C :], gate_bank[h, 2][:])
+            vector_product(front[:, g:], values[:, :, g : 2 * C], gate_bank[h, 1][:, g - C :])
             if k + 2 < LAST:
                 stage_cycle(k + 2)
-                scalar_gathers(k + 2, staged[k + 2], [GATHERED[k + 2], WIDE])
+                scalar_gathers(k + 2, others, [0, WIDE])
             codes, scales = code_tiles()
             experts = [(TRIO * h + n, a) for n in range(TRIO)]
             if k == 0:
@@ -244,15 +264,13 @@ def tile_moe_bds_lin_none_kernel(tc, dyT, w_words, w_scales, gate, offs, pos1, p
                 rest_bank = bank(1)
                 nc.tensor.transpose(rest_bank[:, 0:P], rest_col[:].to_broadcast([P, P]), ident[:])
             if k + 2 == LAST:
-                cuts = [0, C, 2 * C, 2 * C + HALF, WIDE]
-                parts = []
-                for c0, c1 in zip(cuts, cuts[1:]):
-                    parts.append(stage_tile([P, PACK, c1 - c0], F32, "part%d" % c0, STAGED + 4 * PACK * c0))
-                    scalar_gathers(LAST, parts[-1], [max(c0, GATHERED[LAST]), c1], c0)
-                staged[LAST] = parts[0]
+                for c0, c1 in PARTS:
+                    stage_cycle(LAST, c0, c1)
+                    scalar_gathers(LAST, range(TRIO if c0 == 0 else 0, PACK), [c0, c1])
 
         h, a = CYCLES[LAST]
         g = MULTIPLIED[LAST]
+        parts = [staged[LAST, c0][0] for c0, c1 in PARTS]
         tile = work_tile(2 * BANK + HALF, "rounded_last", FRONT[LAST])
         front, back = tile[:, 0 : 2 * BANK], tile[:, 2 * BANK :]
         gpsimd_product(front[:, 0:g], parts[0][:, :, 0:g], gate_sb[h][:, 0:g])
@@ -262,9 +280,9 @@ def tile_moe_bds_lin_none_kernel(tc, dyT, w_words, w_scales, gate, offs, pos1, p
         codes, scales = code_tiles()
         quantise([(4, a)], front[:, C:], codes[:, 0:BANK], scales[:, 0:BANK])
         bring_out(4)
-        late = stage_tile([P, HALF, PACK], BF16, "late", STAGED)
-        ds = stage_tile([P, BANK], F32, "ds", STAGED + 4 * BANK)
-        codes = stage_tile([P, 5 * BANK], U32, "late_codes", STAGED + 8 * BANK)
+        late = stage_tile([P, HALF, PACK], BF16, "late", GATES + LAP)
+        ds = stage_tile([P, BANK], F32, "ds", 3 * 4 * T)
+        codes = stage_tile([P, 5 * BANK], U32, "late_codes", GATES + LAP - 5 * 4 * BANK)
         scales = keep.tile([P, 5 * BANK], U8, name="late_scales", align_bytes=64)
         nc.scalar.copy(ds[:], sums[E][:])
         quantise([(3, a)], front[:, 0:C], codes[:, 0:BANK], scales[:, 0:BANK])
@@ -279,8 +297,8 @@ def tile_moe_bds_lin_none_kernel(tc, dyT, w_words, w_scales, gate, offs, pos1, p
             quantise([(E + 1, a)], tile[:], codes[:, cols], scales[:, cols])
 
         fetched = [stage_tile([P, T], F32, "fetched%d" % n, n * 4 * T) for n in range(2)]
-        partial = [stage_tile([P, T], F32, "partial%d" % n, (2 + n) * 4 * T) for n in range(2)]
-        total = stage_tile([P, T], F32, "total", 4 * 4 * T)
+        partial = [stage_tile([P, T], F32, "partial%d" % n, at) for n, at in enumerate((2 * 4 * T, SECOND))]
+        total = stage_tile([P, T], F32, "total", SECOND + 4 * T)
 
         def slots_of(r, cols):
             return dx[:].indirect(pos_sb[r][:, cols.start // GROUP : cols.stop // GROUP])

@@ -170,7 +170,10 @@ def tile_moe_bds_lin_none_kernel(tc, dyT, w_words, w_scales, gate, offs, pos1, p
             nc.gpsimd.tensor_tensor(as_words(dst), by_runs(src), spread(gates), MULT)
 
         def gpsimd_round(dst, a, h):
-            nc.gpsimd.tensor_scalar(dst, raw[a, h].rearrange("p j c -> p c j"), 1.0, 0.0, MULT, ADD)
+            if (a, h) == (0, 0):
+                nc.gpsimd.tensor_scalar(dst, raw[a, h].rearrange("p j c -> p c j"), 1.0, 0.0, MULT, ADD)
+            else:
+                nc.gpsimd.tensor_scalar(as_words(dst), by_runs(raw[a, h]), 1.0, 0.0, MULT, ADD)
 
         bank_of = {0: 4, 1: 5, 2: 6, 3: 4, 4: 5, 5: 6, E: 7, E + 1: 0}
         sums = {}

from contextlib import ExitStack

import concourse.mybir as mybir
from concourse.masks import make_identity

K, T, E, C, N = 128, 1024, 6, 512, 1536
S = E * C
FLOPS = 2 * K * N * (S + T)
BYTES = 4 * N * T + (E + 1) * (N * K // 2 + N * K // 32) + 4 * S + 2 * 128 * (S + 3 * T) // 16 + 4 * K * T

F32 = mybir.dt.float32
BF16 = mybir.dt.bfloat16
I32 = mybir.dt.int32
U32 = mybir.dt.uint32
U16 = mybir.dt.uint16
U8 = mybir.dt.uint8
E5M2X4 = mybir.dt.float8_e5m2_x4
E2M1X4 = mybir.dt.float4_e2m1fn_x4
MULT = mybir.AluOpType.mult
ADD = mybir.AluOpType.add
COPY = mybir.ActivationFunctionType.Copy

P = 128
PACK = 4
PASSES = N // (P * PACK)
BANK = 512
GROUP = 16
RUN = 2
TRIO = 3
WIDE = TRIO * C
CYCLES = [(0, 0), (0, 1), (0, 2), (1, 1), (1, 2), (1, 0)]
LAST = len(CYCLES) - 1
OWN = 2
MULTIPLIED = [640, C, C, C, C, 384]
WINDOW = WIDE + GROUP
HALF = C // 2
PARTS = [(0, C), (C, 2 * C), (2 * C, 2 * C + HALF), (2 * C + HALF, WIDE)]
STAGED = 4 * PACK * WIDE
GATES = STAGED
SECOND = GATES + 9 * 256
PIECE = 2 * PACK * BANK
LAP = 64
FRONT = {1: PIECE + 2 * LAP, 2: PIECE + LAP, 3: PIECE + 2 * LAP, 4: PIECE, 5: PIECE}
THIRD = {1: 2 * LAP, 2: 3 * PIECE + LAP, 3: 2 * LAP, 4: 3 * PIECE}
SHARED = {1: 3 * PIECE + 2 * LAP, 2: LAP}
HELD = {0: 5 * PIECE, 3: 4 * PIECE, 4: 0}


def tile_moe_bds_lin_none_kernel(tc, dyT, w_words, w_scales, gate, offs, pos1, pos2, pos3, out):
    nc = tc.nc
    with ExitStack() as ctx:
        keep = ctx.enter_context(tc.tile_pool(name="keep", bufs=1))
        ring = ctx.enter_context(tc.tile_pool(name="ring", bufs=3))
        work = ctx.enter_context(tc.tile_pool(name="work", bufs=1))
        stage = ctx.enter_context(tc.tile_pool(name="stage", bufs=1))
        psum = ctx.enter_context(tc.psum_pool(name="psum", bufs=1))

        offs_sb = keep.tile([P, S // GROUP], U16, name="offs_sb")
        pos_sb = [keep.tile([P, T // GROUP], U16, name="pos_sb%d" % r) for r in range(3)]
        gate_cols = [max(MULTIPLIED[k] for k in range(len(CYCLES)) if CYCLES[k][0] == h) for h in range(2)]
        gate_sb = [keep.tile([P, gate_cols[0]], F32, name="gate_sb0"), stage.tile([P, gate_cols[1]], F32, name="gate_sb1", offset=GATES, align_bytes=64)]
        gate_col = [keep.tile([P, 2, PACK], F32, name="gate_col%d" % h) for h in range(2)]
        rest_col = keep.tile([P, 1], F32, name="rest_col")
        ident = keep.tile([P, P], F32, name="ident")
        words = keep.tile([P, (E + 1) * PASSES, 2 * K], U8, name="words", align_bytes=64)
        wscale = keep.tile([P, (E + 1) * PASSES, K], U8, name="wscale", align_bytes=64)
        dx = keep.tile([P, S], F32, name="dx")
        opening = keep.tile([P, PACK, T], F32, name="opening")
        window = {(a, j): keep.tile([P, WINDOW], F32, name="window%d_%d" % (a, j)) for a in (1, 2) for j in range(PACK)}
        raw = {(a, h): keep.tile([P, PACK, BANK], F32, name="raw%d_%d" % (a, h))[:] for a in (1, 2) for h in range(2)}
        for h in range(2):
            raw[0, h] = opening[:, :, h * BANK : (h + 1) * BANK]

        def bank(b):
            return psum.tile([P, BANK], F32, name="bank", tag="bank%d" % b, bufs=1)

        def stage_tile(shape, dtype, name, at):
            return stage.tile(shape, dtype, name=name, offset=at, align_bytes=64)

        def work_tile(cols, name, at):
            return work.tile([P, cols, PACK], BF16, name=name, offset=at, align_bytes=64)

        rows = dyT.rearrange("(a p j) t -> a p j t", p=P, j=PACK)

        others = [j for j in range(PACK) if j != OWN]

        def load_windows(a):
            for j in [OWN] + others:
                nc.sync.dma_start(window[a, j][:, 0:T], rows[a, :, j, :])

        def load_raw(a, h):
            nc.sync.dma_start(raw[a, h], rows[a, :, :, h * BANK : (h + 1) * BANK])

        def load_gates(h):
            nc.sync.dma_start(gate_col[h][:], gate[0, h * WIDE + C : (h + 1) * WIDE].rearrange("(e p i) -> p e i", p=P, i=PACK))
            nc.sync.dma_start(gate_sb[h][:], gate[0:P, h * WIDE : h * WIDE + gate_cols[h]])

        nought = keep.tile([P, 1], F32, name="nought")
        nc.vector.memset(nought[:], 0.0)
        nc.scalar.activation(ident[:], nought[:].to_broadcast([P, P]), COPY)
        nc.vector.memset(wscale[:].rearrange("p m k -> p (m k)").bitcast(I32), 0)
        make_identity(nc, ident[:], nomemset=True)

        nc.sync.dma_start(opening[:, 0, :], rows[0, :, 0, :])
        nc.sync.dma_start(offs_sb[:], offs)
        nc.sync.dma_start(opening[:, 1, :], rows[0, :, 1, :])
        nc.sync.dma_start(opening[:, 2:PACK, 0:BANK], rows[0, :, 2:PACK, 0:BANK])
        for j in range(2, PACK):
            nc.sync.dma_start(opening[:, j, BANK:T], rows[0, :, j, BANK:T])
        load_gates(0)
        load_windows(1)
        load_raw(1, 0)
        load_windows(2)
        load_raw(2, 0)
        nc.sync.dma_start(words[:].bitcast(I32), w_words.rearrange("e a p b -> p (e a) b").bitcast(I32))
        scale_rows = w_scales.rearrange("e a f k -> f (e a) k")
        for q in range(4):
            nc.sync.dma_start(wscale[32 * q : 32 * q + 4, :, :].bitcast(I32), scale_rows[4 * q : 4 * q + 4, :, :].bitcast(I32))
        load_gates(1)
        nc.sync.dma_start(rest_col[:], gate[0, WIDE + MULTIPLIED[LAST] : WIDE + C].rearrange("(p i) -> p i", i=1))
        load_raw(1, 1)
        load_raw(2, 1)
        for tile, src in zip(pos_sb, (pos1, pos2, pos3)):
            nc.sync.dma_start(tile[:], src)

        gate_bank = {}
        for h in range(2):
            for n in range(2):
                gate_bank[h, n + 1] = bank(2 * h + n)
                by_place = gate_bank[h, n + 1][:].rearrange("p (c i) -> p i c", i=PACK)
                for i in range(PACK):
                    nc.tensor.transpose(by_place[:, i, :], gate_col[h][:, n, i : i + 1].to_broadcast([P, P]), ident[:])

        def looked_up(k, j, c0, c1):
            h, a = CYCLES[k]
            if a > 0:
                table = window[a, j][:]
            elif c1 - c0 < T:
                table = opening[:, j, :]
            else:
                table = opening[:, j : j + 2, :].rearrange("p j t -> p (j t)")
            return table.indirect(offs_sb[:, (h * WIDE + c0) // GROUP : (h * WIDE + c1) // GROUP])

        def by_runs(ap):
            return ap.rearrange("p j (c i) -> p c j i", i=RUN)

        def as_words(ap):
            return ap.rearrange("p (c i) j -> p c j i", i=RUN)

        def spread(gates):
            runs = gates.rearrange("p (c i) -> p c i", i=RUN)
            return runs.unsqueeze(2).to_broadcast([P, runs.shape[1], PACK, RUN])

        staged = {}

        def vector_gather(k, j, c0, c1):
            tile, first = staged[k, c0]
            nc.vector.tensor_copy(tile[:, j, c0 - first : c1 - first], looked_up(k, j, c0, c1))

        def scalar_gathers(k, planes, cuts):
            tile, first = staged[k, cuts[0]]
            for j in planes:
                for c0, c1 in zip(cuts, cuts[1:]):
                    nc.scalar.activation(tile[:, j, c0 - first : c1 - first], looked_up(k, j, c0, c1), COPY)

        def vector_product(dst, src, gates):
            nc.vector.tensor_tensor(as_words(dst), by_runs(src), spread(gates), MULT)

        def gpsimd_product(dst, src, gates):
            nc.gpsimd.tensor_tensor(as_words(dst), by_runs(src), spread(gates), MULT)

        def gpsimd_round(dst, a, h):
            if (a, h) == (0, 0):
                nc.gpsimd.tensor_scalar(dst, raw[a, h].rearrange("p j c -> p c j"), 1.0, 0.0, MULT, ADD)
            else:
                nc.gpsimd.tensor_scalar(as_words(dst), by_runs(raw[a, h]), 1.0, 0.0, MULT, ADD)

        bank_of = {0: 4, 1: 5, 2: 6, 3: 4, 4: 5, 5: 6, E: 7, E + 1: 0}
        sums = {}
        added = {g: 0 for g in bank_of}

        def multiply(g, a, codes, scales, c0):
            opens = added[g] == 0
            if opens:
                sums[g] = bank(bank_of[g])
            cols = codes.shape[1]
            added[g] = added[g] + cols
            m = min(g, E) * PASSES + a
            nc.tensor.matmul_mx(
                out=sums[g][:, c0 : c0 + cols],
                lhsT=words[:, m, :].bitcast(E2M1X4),
                lhsT_scale=wscale[:, m, :],
                rhs=codes.bitcast(E5M2X4),
                rhs_scale=scales,
                start=opens,
                stop=added[g] == PASSES * BANK,
            )

        def quantise(pieces, src, codes, scales, c0=0):
            nc.vector.quantize_mx(out=codes.bitcast(E5M2X4), scales=scales, in_=src.rearrange("p c j -> p (c j)"))
            cols = src.shape[1] // len(pieces)
            for n, (g, a) in enumerate(pieces):
                multiply(g, a, codes[:, n * cols : (n + 1) * cols], scales[:, n * cols : (n + 1) * cols], c0)

        def bring_out(g):
            nc.scalar.copy(dx[:, g * C : (g + 1) * C], sums[g][:])

        def code_tiles():
            codes = ring.tile([P, 4 * BANK], U32, name="codes", tag="codes", bufs=3, align_bytes=64)
            scales = ring.tile([P, 4 * BANK], U8, name="scales", tag="scales", bufs=3, align_bytes=64)
            return codes, scales

        def stage_cycle(k, c0=0, c1=WIDE):
            staged[k, c0] = (stage_tile([P, PACK, c1 - c0], F32, "staged%d_%d" % (k, c0), (k % 2) * SECOND + 4 * PACK * c0), c0)

        stage_cycle(0)
        for j in range(OWN):
            vector_gather(0, j, 0, WIDE // 2)
        vector_gather(0, OWN, 0, WIDE)
        staged[0, WIDE // 2] = staged[0, 0]
        scalar_gathers(0, range(OWN), [WIDE // 2, 2 * C, WIDE])
        scalar_gathers(0, [PACK - 1], [0, C, 2 * C, WIDE])
        stage_cycle(1)
        scalar_gathers(1, others, [0, WIDE])
        held = []
        for k in range(LAST):
            h, a = CYCLES[k]
            g = MULTIPLIED[k]
            values = staged[k, 0][0]
            if k == 0:
                tile = work_tile(4 * BANK, "rounded", LAP)
                shared, front, third = tile[:, 0:BANK], tile[:, BANK : 3 * BANK], tile[:, 3 * BANK :]
            else:
                front = work_tile(2 * BANK, "front%d" % k, FRONT[k])[:]
                third = work_tile(BANK, "third%d" % k, THIRD[k])[:]
            if k in SHARED:
                shared = work_tile(BANK, "shared%d" % k, SHARED[k])[:]
            if k < PASSES:
                gpsimd_round(shared, a, 0)
            if k in HELD:
                held.append((a, work_tile(BANK, "held%d" % k, HELD[k])))
                gpsimd_round(held[-1][1][:], a, 1)
            gpsimd_product(front[:, 0:g], values[:, :, 0:g], gate_sb[h][:, 0:g])
            if k + 1 < LAST:
                vector_gather(k + 1, OWN, 0, WIDE)
            else:
                for j in range(TRIO):
                    vector_gather(LAST, j, 0, C)
            vector_product(third, values[:, :, 2 * C :], gate_bank[h, 2][:])
            vector_product(front[:, g:], values[:, :, g : 2 * C], gate_bank[h, 1][:, g - C :])
            if k + 2 < LAST:
                stage_cycle(k + 2)
                scalar_gathers(k + 2, others, [0, WIDE])
            codes, scales = code_tiles()
            experts = [(TRIO * h + n, a) for n in range(TRIO)]
            if k == 0:
                quantise([(E, a), experts[0]], tile[:, 0 : 2 * BANK], codes[:, 0 : 2 * BANK], scales[:, 0 : 2 * BANK])
                quantise(experts[1:], tile[:, 2 * BANK :], codes[:, 2 * BANK :], scales[:, 2 * BANK :])
            else:
                if k in SHARED:
                    quantise([(E, a)], shared, codes[:, 3 * BANK :], scales[:, 3 * BANK :])
                quantise(experts[2:], third, codes[:, 2 * BANK : 3 * BANK], scales[:, 2 * BANK : 3 * BANK])
                quantise(experts[0:2], front, codes[:, 0 : 2 * BANK], scales[:, 0 : 2 * BANK])
            if k == PASSES - 1:
                for n in range(TRIO):
                    bring_out(n)
                rest_bank = bank(1)
                nc.tensor.transpose(rest_bank[:, 0:P], rest_col[:].to_broadcast([P, P]), ident[:])
            if k + 2 == LAST:
                for c0, c1 in PARTS:
                    stage_cycle(LAST, c0, c1)
                    scalar_gathers(LAST, range(TRIO if c0 == 0 else 0, PACK), [c0, c1])

        h, a = CYCLES[LAST]
        g = MULTIPLIED[LAST]
        parts = [staged[LAST, c0][0] for c0, c1 in PARTS]
        tile = work_tile(2 * BANK + HALF, "rounded_last", FRONT[LAST])
        front, back = tile[:, 0 : 2 * BANK], tile[:, 2 * BANK :]
        gpsimd_product(front[:, 0:g], parts[0][:, :, 0:g], gate_sb[h][:, 0:g])
        vector_product(front[:, C:], parts[1][:], gate_bank[h, 1][:])
        vector_product(front[:, g:C], parts[0][:, :, g:C], rest_bank[:, 0 : C - g])
        vector_product(back, parts[2][:], gate_bank[h, 2][:, 0:HALF])
        codes, scales = code_tiles()
        quantise([(4, a)], front[:, C:], codes[:, 0:BANK], scales[:, 0:BANK])
        bring_out(4)
        late = stage_tile([P, HALF, PACK], BF16, "late", GATES + LAP)
        ds = stage_tile([P, BANK], F32, "ds", 3 * 4 * T)
        codes = stage_tile([P, 5 * BANK], U32, "late_codes", GATES + LAP - 5 * 4 * BANK)
        scales = keep.tile([P, 5 * BANK], U8, name="late_scales", align_bytes=64)
        nc.scalar.copy(ds[:], sums[E][:])
        quantise([(3, a)], front[:, 0:C], codes[:, 0:BANK], scales[:, 0:BANK])
        bring_out(3)
        vector_product(late[:], parts[3][:], gate_bank[h, 2][:, HALF:])
        for n, src in enumerate((back, late[:])):
            cols = slice(BANK + n * HALF, BANK + (n + 1) * HALF)
            quantise([(5, a)], src, codes[:, cols], scales[:, cols], n * HALF)
        bring_out(5)
        for n, (a, tile) in enumerate(held):
            cols = slice((2 + n) * BANK, (3 + n) * BANK)
            quantise([(E + 1, a)], tile[:], codes[:, cols], scales[:, cols])

        fetched = [stage_tile([P, T], F32, "fetched%d" % n, n * 4 * T) for n in range(2)]
        partial = [stage_tile([P, T], F32, "partial%d" % n, at) for n, at in enumerate((2 * 4 * T, SECOND))]
        total = stage_tile([P, T], F32, "total", SECOND + 4 * T)

        def slots_of(r, cols):
            return dx[:].indirect(pos_sb[r][:, cols.start // GROUP : cols.stop // GROUP])

        def add(dst, in0, in1):
            nc.vector.tensor_tensor(dst, in0, in1, ADD)

        halves = [slice(0, BANK), slice(BANK, T)]
        ends = [slice(0, BANK), slice(BANK, 3 * T // 4), slice(3 * T // 4, T)]
        for cols in reversed(halves):
            nc.scalar.activation(fetched[0][:, cols], slots_of(1, cols), COPY)
        for cols in ends:
            nc.scalar.activation(fetched[1][:, cols], slots_of(2, cols), COPY)
        low, high = halves
        add(partial[0][:, low], slots_of(0, low), ds[:])
        add(partial[0][:, high], slots_of(0, high), fetched[0][:, high])
        add(partial[1][:, low], partial[0][:, low], fetched[0][:, low])
        add(partial[1][:, high], partial[0][:, high], sums[E + 1][:])
        for cols in ends:
            add(total[:, cols], partial[1][:, cols], fetched[1][:, cols])
            nc.sync.dma_start(out[:, cols], total[:, cols])
